import numpy as np
import ml_dtypes


def mxq(x, axis, fmt="e4m3"):
    dtype, down = {"e4m3": (ml_dtypes.float8_e4m3fn, 7), "e5m2": (ml_dtypes.float8_e5m2, 14)}[fmt]
    v = np.moveaxis(np.asarray(x, np.float32).astype(ml_dtypes.bfloat16).astype(np.float64), axis, -1)
    blocks = v.reshape(v.shape[:-1] + (-1, 32))
    amax = np.abs(blocks).max(-1, keepdims=True)
    byte = np.maximum(np.where(amax > 0, np.frexp(amax)[1] - 1 + 127, 0) - down, 1)
    scale = np.exp2(byte - 127.0)
    codes = (blocks / scale).astype(np.float32).astype(dtype).astype(np.float64)
    return np.moveaxis((codes * scale).reshape(v.shape), -1, axis)


WIDE = False


def mx_kscale(k):
    if not WIDE:
        return np.ones(k)
    levels = np.array([10, -10, 5, -5, 0])
    if k % 512:
        return np.exp2(np.random.permutation(np.resize(levels, k // 32))).repeat(32)
    a = np.empty((k // 512, 16))
    for p in range(k // 512):
        a[p, :8] = np.random.permutation(np.resize(levels, 8))
        for g in range(8):
            far = levels[np.abs(levels - a[p, g]) >= 10]
            a[p, g + 8] = far[np.random.randint(len(far))]
    return np.exp2(a.ravel()).repeat(32)


def f64(x):
    return np.asarray(x).astype(np.float64)


def striped(idx):
    return np.tile(idx.reshape(-1, 16).T, (8, 1)).astype(np.uint16)


def unstriped(offs):
    return offs[:16].T.reshape(-1).astype(np.int64)


E2M1 = np.array([0.0, 0.5, 1.0, 1.5, 2.0, 3.0, 4.0, 6.0, -0.0, -0.5, -1.0, -1.5, -2.0, -3.0, -4.0, -6.0])


def pack_weight(w, fmt):
    k, n = w.shape
    w = f64(np.asarray(w, np.float32).astype(ml_dtypes.bfloat16)).reshape(k // 32, 32, n)
    amax = np.abs(w).max(1)
    if fmt == "e4m3":
        byte = np.frexp(amax)[1] - 1 + 127 - 7
    else:
        mant, ex = np.frexp(amax / 6.0)
        byte = np.where(mant > 0.5, ex, ex - 1) + 127
    byte = np.clip(np.where(amax > 0, byte, 1), 1, 254)
    scaled = (w * np.exp2(127.0 - byte)[:, None, :]).reshape(k, n).astype(np.float32)
    by_word = np.ascontiguousarray(scaled.reshape(k // 512, 128, 4, n).transpose(0, 1, 3, 2))
    if fmt == "e4m3":
        words = by_word.astype(ml_dtypes.float8_e4m3fn).view(np.uint8)
    else:
        c = by_word.astype(ml_dtypes.float4_e2m1fn).view(np.uint8) & 0xF
        words = (c[..., 0::2] | (c[..., 1::2] << 4)).reshape(k // 512, 128, 2 * n)
    return np.ascontiguousarray(words), np.ascontiguousarray(byte.astype(np.uint8).reshape(k // 512, 16, n))


def unpack_weight(words, scales, fmt):
    g, _, n = scales.shape
    words = np.ascontiguousarray(words).reshape(g, 128, n, -1)
    if fmt == "e4m3":
        vals = words.view(ml_dtypes.float8_e4m3fn).astype(np.float64)
    else:
        nib = np.empty((g, 128, n, 4), np.uint8)
        nib[..., 0::2] = words & 0xF
        nib[..., 1::2] = words >> 4
        vals = E2M1[nib]
    vals = vals * np.repeat(np.exp2(scales.astype(np.float64) - 127.0), 8, axis=1)[..., None]
    return vals.transpose(0, 1, 3, 2).reshape(g * 512, n)


def gelu(v):
    return 0.5 * v * (1.0 + np.tanh(np.sqrt(2.0 / np.pi) * (v + 0.044715 * v**3)))


K, M, H, N, T, T2, T3, S = 1024, 512, 1024, 768, 2048, 1024, 2048, 512

def setup_inputs():
    n = np.random.standard_normal
    s, s2, u = mx_kscale(K)[:, None], mx_kscale(M)[:, None], mx_kscale(H)[:, None]
    tab_words, tab_scales = pack_weight(n((K, T)) * s, "e4m3")
    tab2_words, tab2_scales = pack_weight(n((M, T2)) * s2, "e4m3")
    tab3_words, tab3_scales = pack_weight(n((M, T3)) * s2, "e2m1")
    wg_words, wg_scales = pack_weight(n((K, H)) / np.sqrt(K) / s * u.T, "e2m1")
    wa_words, wa_scales = pack_weight(n((M, H)) / np.sqrt(M) / s2, "e4m3")
    return {
        "tab_words": tab_words, "tab_scales": tab_scales,
        "tab2_words": tab2_words, "tab2_scales": tab2_scales,
        "tab3_words": tab3_words, "tab3_scales": tab3_scales,
        "offs": striped(np.random.permutation(T)[:S]),
        "offs2": striped(np.random.permutation(T2)[:S]),
        "offs3": striped(np.random.permutation(T3)[:S]),
        "wg_words": wg_words, "wg_scales": wg_scales,
        "wr": (n((M, H)) / np.sqrt(M) / s2).astype(np.float32),
        "br": (0.5 * n(H)).astype(np.float32),
        "wa_words": wa_words, "wa_scales": wa_scales,
        "ba": (0.5 * n(H)).astype(np.float32),
        "w1": (n((H, N)) / np.sqrt(H) / u).astype(np.float32),
        "w2": (n((H, N)) / np.sqrt(H) / u).astype(np.float32),
        "bo": (0.5 * n(N)).astype(np.float32),
    }

def reference(tab_words, tab_scales, tab2_words, tab2_scales, tab3_words, tab3_scales, offs, offs2, offs3,
              wg_words, wg_scales, wr, br, wa_words, wa_scales, ba, w1, w2, bo):
    v = unpack_weight(tab_words, tab_scales, "e4m3")[:, unstriped(offs)]
    v2 = unpack_weight(tab2_words, tab2_scales, "e4m3")[:, unstriped(offs2)]
    v3 = unpack_weight(tab3_words, tab3_scales, "e2m1")[:, unstriped(offs3)]
    guest = unpack_weight(wg_words, wg_scales, "e2m1").T @ v
    room = (mxq(f64(wr), 0, "e4m3").T @ v2) + f64(br)[:, None]
    arrival = (unpack_weight(wa_words, wa_scales, "e4m3").T @ v3) + f64(ba)[:, None]
    h1 = mxq(guest * room, 0, "e4m3")
    h2 = mxq(guest * arrival, 0, "e4m3")
    y = mxq(f64(w1), 0, "e4m3").T @ h1 + mxq(f64(w2), 0, "e4m3").T @ h2
    return y + f64(bo)[:, None]

@@ -1,0 +1,312 @@
+from contextlib import ExitStack
+
+import concourse.mybir as mybir
+from concourse.masks import make_identity
+
+K, M, H, N, T, T2, T3, S = 1024, 512, 1024, 768, 2048, 1024, 2048, 512
+FLOPS = 2 * S * (K * H + 2 * M * H + 2 * H * N)
+
+F32 = mybir.dt.float32
+BF16 = mybir.dt.bfloat16
+I32 = mybir.dt.int32
+U32 = mybir.dt.uint32
+U16 = mybir.dt.uint16
+U8 = mybir.dt.uint8
+FP8X4 = mybir.dt.float8_e4m3fn_x4
+FP4X4 = mybir.dt.float4_e2m1fn_x4
+MULT = mybir.AluOpType.mult
+ADD = mybir.AluOpType.add
+IDENTITY = mybir.ActivationFunctionType.Identity
+
+P = 128
+PASS = 512
+CHUNK = 128
+ROW0 = 112
+
+
+def tile_list_upgrade_offer_scores_kernel(
+    tc, tab_words, tab_scales, tab2_words, tab2_scales, tab3_words, tab3_scales, offs, offs2, offs3,
+    wg_words, wg_scales, wr, br, wa_words, wa_scales, ba, w1, w2, bo, out,
+):
+    nc = tc.nc
+    with ExitStack() as ctx:
+        lists = ctx.enter_context(tc.tile_pool(name="lists", bufs=1))
+        sb = ctx.enter_context(tc.tile_pool(name="sb", bufs=1))
+        ps = ctx.enter_context(tc.psum_pool(name="ps", bufs=1))
+
+        def tile(name, shape, dtype, tag=None):
+            return sb.tile(shape, dtype, name=name, tag=tag or name, align_bytes=64)
+
+        def bank(name, b):
+            return ps.tile([P, PASS], F32, name=name, tag="bank%d" % b)
+
+        idx = lists.tile([P, S // 16], U16, name="idx")
+        idx2 = lists.tile([P, S // 16], U16, name="idx2")
+        idx3 = lists.tile([P, S // 16], U16, name="idx3")
+        nc.sync.dma_start(idx[:], offs)
+        nc.sync.dma_start(idx2[:], offs2)
+        nc.sync.dma_start(idx3[:], offs3)
+
+        v_sc = tile("v_sc", [P, 2 * T], U8)
+        v2_sc = tile("v2_sc", [P, T2], U8)
+        v3_sc = tile("v3_sc", [P, T3], U8)
+        wg_sc_raw = tile("wg_sc_raw", [P, 2 * H], U8)
+        wa_sc_raw = tile("wa_sc_raw", [P, H], U8)
+        nc.scalar.dma_start(
+            v_sc[ROW0:P, :].rearrange("q (a t) -> q a t", a=2).bitcast(I32),
+            tab_scales.rearrange("a q t -> q a t").bitcast(I32),
+        )
+        nc.scalar.dma_start(v2_sc[ROW0:P, :].bitcast(I32), tab2_scales[0].bitcast(I32))
+        nc.scalar.dma_start(v3_sc[ROW0:P, :].bitcast(I32), tab3_scales[0].bitcast(I32))
+        nc.scalar.dma_start(
+            wg_sc_raw[ROW0:P, :].rearrange("q (a c) -> q a c", a=2).bitcast(I32),
+            wg_scales.rearrange("a q c -> q a c").bitcast(I32),
+        )
+        nc.scalar.dma_start(wa_sc_raw[ROW0:P, :].bitcast(I32), wa_scales[0].bitcast(I32))
+        planes = tile("planes", [P, 3 * H + 4 * S], U8)
+        nc.vector.memset(v_sc[0:ROW0, :].bitcast(I32), 0)
+        nc.vector.memset(v2_sc[0:ROW0, :].bitcast(I32), 0)
+        nc.vector.memset(v3_sc[0:ROW0, :].bitcast(I32), 0)
+        nc.gpsimd.memset(wg_sc_raw[96:ROW0, :].bitcast(I32), 0)
+        nc.gpsimd.memset(wa_sc_raw[96:ROW0, :].bitcast(I32), 0)
+        nc.gpsimd.memset(planes[:].bitcast(I32), 0)
+
+        bias_raw = tile("bias_raw", [4, PASS], F32)
+        bias_rows = tile("bias_rows", [P, PASS], F32)
+        ident = tile("ident", [P, P], F32)
+        nc.scalar.dma_start(bias_raw[0:2, :], br.rearrange("(a r) -> a r", a=2))
+        nc.scalar.dma_start(bias_raw[2:4, :], ba.rearrange("(a r) -> a r", a=2))
+        nc.scalar.dma_start(bias_rows[P - 6 : P, 0:P], bo.rearrange("(c p) -> c p", p=P))
+        nc.gpsimd.memset(bias_rows[0 : P - 6, 0:P], 0.0)
+        nc.gpsimd.memset(bias_rows[:, P:PASS], 0.0)
+        make_identity(nc, ident[:])
+
+        wr_raw = [tile("wr_raw%d" % a, [P, 4, PASS], F32) for a in range(2)]
+        v_words = [tile("v_words%d" % a, [P, T], U32) for a in range(2)]
+        v2_words = tile("v2_words", [P, T2], U32)
+        wr_rows = wr.rearrange("(p j) r -> p j r", j=4)
+        for a in range(2):
+            nc.sync.dma_start(wr_raw[a][:], wr_rows[:, :, a * PASS : (a + 1) * PASS])
+        nc.sync.dma_start(v2_words[:].bitcast(I32), tab2_words[0].rearrange("p t i -> p (t i)").bitcast(I32))
+        for a in range(2):
+            nc.sync.dma_start(v_words[a][:].bitcast(I32), tab_words[a].rearrange("p t i -> p (t i)").bitcast(I32))
+
+        wr_bf = [tile("wr_bf%d" % a, [P, 4 * PASS], BF16) for a in range(2)]
+        wr_q = [tile("wr_q%d" % a, [P, PASS], U32) for a in range(2)]
+        wr_s = [tile("wr_s%d" % a, [P, PASS], U8) for a in range(2)]
+
+        def cast_wr(copy, a):
+            copy(
+                wr_bf[a][:].rearrange("p (t q e j) -> p t q j e", t=4, e=4, j=4),
+                wr_raw[a][:].rearrange("p j (q t e) -> p t q j e", t=4, e=4),
+            )
+
+        def quantize(codes, scales, values):
+            nc.vector.quantize_mx(out=codes.bitcast(FP8X4), scales=scales, in_=values)
+
+        nc.scalar.copy(
+            bias_rows[0:4, :].rearrange("a (t q e) -> a t q e", t=4, e=4),
+            bias_raw[:].rearrange("a (q t e) -> a t q e", t=4, e=4),
+        )
+        bias_ps = bank("bias_ps", 7)
+        for t in range(4):
+            nc.tensor.transpose(bias_ps[:, t * P : (t + 1) * P], bias_rows[:, t * P : (t + 1) * P], ident[:])
+        bias = tile("bias", [P, 4, 4], F32)
+        bias_o = tile("bias_o", [P, 6], F32)
+        nc.scalar.activation(bias[:], bias_ps[:].rearrange("p (t c) -> p t c", t=4)[:, :, 0:4], IDENTITY)
+        nc.scalar.activation(bias_o[:], bias_ps[:, P - 6 : P], IDENTITY)
+
+        cast_wr(nc.scalar.copy, 0)
+        cast_wr(nc.scalar.copy, 1)
+
+        got_sc = tile("got_sc", [P, 4 * S], U8)
+        for a in range(2):
+            nc.vector.tensor_copy(got_sc[:, a * S : (a + 1) * S], v_sc[:, a * T : (a + 1) * T].indirect(idx[:]))
+        nc.vector.tensor_copy(got_sc[:, 2 * S : 3 * S], v2_sc[:].indirect(idx2[:]))
+        nc.vector.tensor_copy(got_sc[:, 3 * S : 4 * S], v3_sc[:].indirect(idx3[:]))
+        staged = tile("staged", [P, 3 * H + 4 * S], U8)
+        nc.vector.tensor_copy(staged[96:P, 3 * H :].bitcast(I32), got_sc[96:P, :].bitcast(I32))
+        for raw, c0, c1 in ((wg_sc_raw, 0, 2 * H), (wa_sc_raw, 2 * H, 3 * H)):
+            nc.vector.tensor_copy(
+                staged[96:P, c0:c1].bitcast(I32).rearrange("p (h t u w) -> p h u t w", t=4, u=8, w=4),
+                raw[96:P, :].bitcast(I32).rearrange("p (h u w t) -> p h u t w", t=4, u=8, w=4),
+            )
+        for q in range(4):
+            nc.sync.dma_start(
+                planes[32 * q : 32 * q + 4, :].bitcast(I32), staged[ROW0 + 4 * q : ROW0 + 4 * q + 4, :].bitcast(I32)
+            )
+        wg_sc = [planes[:, a * H : (a + 1) * H] for a in range(2)]
+        wa_sc = planes[:, 2 * H : 3 * H]
+        g_sc = [planes[:, 3 * H + a * S : 3 * H + (a + 1) * S] for a in range(2)]
+        g2_sc = planes[:, 3 * H + 2 * S : 3 * H + 3 * S]
+        g3_sc = planes[:, 3 * H + 3 * S :]
+
+        wg_raw = tile("wg_raw", [P, 4 * H], U8, tag="wg_sc_raw")
+        v3_words = tile("v3_words", [P, T3], U16, tag="wa_sc_raw")
+        nc.sync.dma_start(
+            wg_raw[:].rearrange("p (a c) -> p a c", a=2).bitcast(I32), wg_words.rearrange("a p c -> p a c").bitcast(I32)
+        )
+        nc.sync.dma_start(v3_words[:].bitcast(I32), tab3_words[0].bitcast(I32))
+
+        g = [tile("g%d" % a, [P, S], U32) for a in range(2)]
+        g2 = tile("g2", [P, S], U32)
+        g3 = tile("g3", [P, S], U16)
+        wg_p = tile("wg_p", [P, 4 * H], U8)
+        wa_p = tile("wa_p", [P, 4 * H], U8)
+        quantize(wr_q[0][:], wr_s[0][:], wr_bf[0][:])
+        nc.vector.tensor_copy(g2[:], v2_words[:].indirect(idx2[:]))
+        wa_raw = tile("wa_raw", [P, 4 * H], U8, tag="v2_words")
+        nc.sync.dma_start(wa_raw[:].bitcast(I32), wa_words[0].rearrange("p c i -> p (c i)").bitcast(I32))
+        nc.vector.tensor_copy(g[0][:], v_words[0][:].indirect(idx[:]))
+        quantize(wr_q[1][:], wr_s[1][:], wr_bf[1][:])
+        nc.vector.tensor_copy(g[1][:], v_words[1][:].indirect(idx[:]))
+        nc.vector.tensor_copy(
+            wg_p[:].bitcast(I32).rearrange("p (h t q w) -> p h t q w", t=4, q=32, w=2),
+            wg_raw[:].bitcast(I32).rearrange("p (h q t w) -> p h t q w", t=4, q=32, w=2),
+        )
+        nc.vector.tensor_copy(g3[:], v3_words[:].indirect(idx3[:]))
+        nc.vector.tensor_copy(
+            wa_p[:].bitcast(I32).rearrange("p (h t q w) -> p h t q w", t=4, q=32, w=4),
+            wa_raw[:].bitcast(I32).rearrange("p (h q t w) -> p h t q w", t=4, q=32, w=4),
+        )
+
+        def load_w(raw, w, a, cols):
+            rows = w[a * PASS : (a + 1) * PASS, cols].rearrange("(q t e) n -> t q e n", t=4, e=4)
+            for t in range(4):
+                nc.sync.dma_start(raw[:, t, :], rows[t])
+
+        stage2 = [(w1, 0, "v_words0"), (w2, 0, "staged"), (w1, 1, "v_words1")]
+        w_raw = []
+        for w, a, tag in stage2:
+            w_raw.append(tile("w_raw%d" % len(w_raw), [P, 4, N], F32, tag=tag))
+            load_w(w_raw[-1], w, a, slice(0, N))
+        third = N // 3
+        w_last = []
+
+        def load_last(tag):
+            i = len(w_last)
+            w_last.append(tile("w_last%d" % i, [P, 4, third], F32, tag=tag))
+            load_w(w_last[i], w2, 1, slice(i * third, (i + 1) * third))
+
+        for tag in ("wg_sc_raw", "wa_sc_raw", "v2_words"):
+            load_last(tag)
+
+        room = [tile("room%d" % a, [P, 4, S], F32) for a in range(2)]
+        arrival = [tile("arrival%d" % a, [P, 4, S], F32) for a in range(2)]
+
+        def make_room(a, slots, banks):
+            for t, b in zip(slots, banks):
+                acc = bank("room_ps%d%d" % (a, t), b)
+                cols = slice(t * P, (t + 1) * P)
+                nc.tensor.matmul_mx(acc[:], wr_q[a][:, cols].bitcast(FP8X4), wr_s[a][:, cols], g2[:].bitcast(FP8X4), g2_sc,
+                                    start=True, stop=True)
+                nc.scalar.activation(room[a][:, t, :], acc[:], IDENTITY, bias=bias[:, t, a : a + 1])
+
+        def make_arrival(a, banks):
+            for t, b in enumerate(banks):
+                acc = bank("arrival_ps%d%d" % (a, t), b)
+                c0 = a * PASS + t * P
+                nc.tensor.matmul_mx(acc[:], wa_p[:, 4 * c0 : 4 * (c0 + P)].bitcast(FP8X4), wa_sc[:, c0 : c0 + P],
+                                    g3[:].bitcast(FP4X4), g3_sc, start=True, stop=True)
+                nc.scalar.activation(arrival[a][:, t, :], acc[:], IDENTITY, bias=bias[:, t, 2 + a : 3 + a])
+
+        def make_guest(a):
+            banks = []
+            for n in range(S // CHUNK):
+                acc = bank("guest_ps%d%d" % (a, n), n)
+                tok = slice(n * CHUNK, (n + 1) * CHUNK)
+                for t in range(4):
+                    c0 = a * PASS + t * P
+                    for k in range(2):
+                        nc.tensor.matmul_mx(
+                            acc[:, t * CHUNK : (t + 1) * CHUNK],
+                            wg_p[:, 2 * (k * H + c0) : 2 * (k * H + c0 + P)].bitcast(FP4X4), wg_sc[k][:, c0 : c0 + P],
+                            g[k][:, tok].bitcast(FP8X4), g_sc[k][:, tok], start=(k == 0), stop=(k == 1),
+                        )
+                banks.append(acc)
+            return banks
+
+        h_bf = [[tile("h_bf%d0" % i, [P, 4 * S], BF16, tag="h_bf%d" % i)] for i in range(2)]
+        h_q = [[tile("h_q%d%d" % (i, a), [P, S], U32) for a in range(2)] for i in range(2)]
+        h_s = [[tile("h_s%d%d" % (i, a), [P, S], U8) for a in range(2)] for i in range(2)]
+
+        def product(i, a, n, guest):
+            other = (room, arrival)[i][a]
+            nc.vector.tensor_tensor(
+                h_bf[i][a][:, 4 * n * CHUNK : 4 * (n + 1) * CHUNK].rearrange("p (c i t) -> p c t i", t=4, i=4),
+                guest[:].rearrange("p (t c i) -> p c t i", t=4, i=4),
+                other[:, :, n * CHUNK : (n + 1) * CHUNK].rearrange("p t (c i) -> p c t i", i=4),
+                MULT,
+            )
+
+        def cast_w(copy, values, raw):
+            copy(values.rearrange("p (c i t) -> p c t i", t=4, i=4), raw.rearrange("p t (c i) -> p c t i", i=4))
+
+        w_bf = [tile("w_bf%d" % i, [P, 4 * N], BF16) for i in range(4)]
+        w_q = [tile("w_q%d" % i, [P, N], U32) for i in range(4)]
+        w_s = [tile("w_s%d" % i, [P, N], U8) for i in range(4)]
+
+        def quantize_w(i, c0, c1):
+            quantize(w_q[i][:, c0:c1], w_s[i][:, c0:c1], w_bf[i][:, 4 * c0 : 4 * c1])
+
+        make_room(0, (0, 1, 2, 3), (0, 1, 2, 3))
+        make_room(1, (0, 1), (4, 5))
+        guest = make_guest(0)
+        make_arrival(0, (6, 7, 4, 5))
+        make_room(1, (2, 3), (6, 7))
+        make_arrival(1, (4, 5, 6, 7))
+        for n in range(4):
+            product(0, 0, n, guest[n])
+        product(1, 0, 0, guest[0])
+        quantize(h_q[0][0][:], h_s[0][0][:], h_bf[0][0][:])
+        for n in range(1, 4):
+            product(1, 0, n, guest[n])
+        guest = make_guest(1)
+        for i in range(3):
+            cast_w(nc.scalar.copy, w_bf[i][:, 0 : 4 * PASS], w_raw[i][:, :, 0:PASS])
+            cast_w(nc.scalar.copy, w_bf[i][:, 4 * PASS : 4 * N], w_raw[i][:, :, PASS:N])
+        h_bf[0].append(tile("h_bf01", [P, 4 * S], BF16, tag="h_bf0"))
+        product(0, 1, 0, guest[0])
+        quantize(h_q[1][0][:], h_s[1][0][:], h_bf[1][0][:])
+        h_bf[1].append(tile("h_bf11", [P, 4 * S], BF16, tag="h_bf1"))
+        product(1, 1, 0, guest[0])
+        product(0, 1, 1, guest[1])
+        product(1, 1, 1, guest[1])
+        quantize_w(0, 0, PASS)
+        quantize_w(0, PASS, N)
+        product(0, 1, 2, guest[2])
+        product(1, 1, 2, guest[2])
+        product(0, 1, 3, guest[3])
+        product(1, 1, 3, guest[3])
+        quantize_w(1, 0, PASS)
+        quantize(h_q[0][1][:], h_s[0][1][:], h_bf[0][1][:])
+        quantize_w(1, PASS, N)
+        quantize(h_q[1][1][:], h_s[1][1][:], h_bf[1][1][:])
+        cast_w(nc.vector.tensor_copy, w_bf[3][:, 0 : 4 * third], w_last[0][:])
+        quantize_w(2, 0, PASS)
+        cast_w(nc.vector.tensor_copy, w_bf[3][:, 4 * third : 8 * third], w_last[1][:])
+        cast_w(nc.scalar.copy, w_bf[3][:, 8 * third : 12 * third], w_last[2][:])
+        quantize_w(3, 0, third)
+        quantize_w(2, PASS, N)
+        quantize_w(3, third, 2 * third)
+        quantize_w(3, 2 * third, N)
+
+        acc = [bank("out_ps%d" % c, (4 + c) % 8) for c in range(N // P)]
+
+        def score(c, i):
+            cols = slice(c * P, (c + 1) * P)
+            nc.tensor.matmul_mx(acc[c][:], w_q[i][:, cols].bitcast(FP8X4), w_s[i][:, cols],
+                                h_q[i % 2][i // 2][:].bitcast(FP8X4), h_s[i % 2][i // 2][:], start=(i == 0), stop=(i == 3))
+
+        for i in range(3):
+            for c in range(N // P):
+                score(c, i)
+        res = [tile("res%d" % u, [P, 3, S], F32) for u in range(2)]
+        for c in range(N // P):
+            score(c, 3)
+            dst = res[c % 2][:, c // 2, :]
+            if c % 2 == 0:
+                nc.scalar.activation(dst, acc[c][:], IDENTITY, bias=bias_o[:, c : c + 1])
+            else:
+                nc.vector.tensor_scalar(dst, acc[c][:], bias_o[:, c : c + 1], None, ADD)
+            nc.sync.dma_start(out[c * P : (c + 1) * P, :], dst)

@@ -43,53 +43,55 @@ def tile_list_upgrade_offer_scores_kernel(
         idx = lists.tile([P, S // 16], U16, name="idx")
         idx2 = lists.tile([P, S // 16], U16, name="idx2")
         idx3 = lists.tile([P, S // 16], U16, name="idx3")
-        nc.sync.dma_start(idx[:], offs)
-        nc.sync.dma_start(idx2[:], offs2)
-        nc.sync.dma_start(idx3[:], offs3)
-
         v_sc = tile("v_sc", [P, 2 * T], U8)
         v2_sc = tile("v2_sc", [P, T2], U8)
         v3_sc = tile("v3_sc", [P, T3], U8)
         wg_sc_raw = tile("wg_sc_raw", [P, 2 * H], U8)
         wa_sc_raw = tile("wa_sc_raw", [P, H], U8)
-        nc.scalar.dma_start(
-            v_sc[ROW0:P, :].rearrange("q (a t) -> q a t", a=2).bitcast(I32),
-            tab_scales.rearrange("a q t -> q a t").bitcast(I32),
-        )
-        nc.scalar.dma_start(v2_sc[ROW0:P, :].bitcast(I32), tab2_scales[0].bitcast(I32))
-        nc.scalar.dma_start(v3_sc[ROW0:P, :].bitcast(I32), tab3_scales[0].bitcast(I32))
-        nc.scalar.dma_start(
-            wg_sc_raw[ROW0:P, :].rearrange("q (a c) -> q a c", a=2).bitcast(I32),
-            wg_scales.rearrange("a q c -> q a c").bitcast(I32),
-        )
-        nc.scalar.dma_start(wa_sc_raw[ROW0:P, :].bitcast(I32), wa_scales[0].bitcast(I32))
         planes = tile("planes", [P, 3 * H + 4 * S], U8)
+        bias_raw = tile("bias_raw", [4, PASS], F32)
+        bias_rows = tile("bias_rows", [P, PASS], F32)
+        bo_rows = tile("bo_rows", [P, P], F32)
+        ident = tile("ident", [P, P], F32)
+        wr_raw = [tile("wr_raw0", [P, 4, PASS], F32)]
+        v_words = [tile("v_words0", [P, T], U32)]
+        v2_words = tile("v2_words", [P, T2], U32)
+        v3_words = tile("v3_words", [P, T3], U16)
+        wa_raw = tile("wa_raw", [P, 4 * H], U8)
+        wr_rows = wr.rearrange("(p j) r -> p j r", j=4)
+
         nc.vector.memset(v_sc[0:ROW0, :].bitcast(I32), 0)
         nc.vector.memset(v2_sc[0:ROW0, :].bitcast(I32), 0)
         nc.vector.memset(v3_sc[0:ROW0, :].bitcast(I32), 0)
+        nc.gpsimd.memset(bo_rows[:], 0.0)
+        nc.gpsimd.memset(bias_rows[:], 0.0)
+        make_identity(nc, ident[:])
         nc.gpsimd.memset(wg_sc_raw[96:ROW0, :].bitcast(I32), 0)
         nc.gpsimd.memset(wa_sc_raw[96:ROW0, :].bitcast(I32), 0)
         nc.gpsimd.memset(planes[:].bitcast(I32), 0)
 
-        bias_raw = tile("bias_raw", [4, PASS], F32)
-        bias_rows = tile("bias_rows", [P, PASS], F32)
-        ident = tile("ident", [P, P], F32)
-        nc.scalar.dma_start(bias_raw[0:2, :], br.rearrange("(a r) -> a r", a=2))
-        nc.scalar.dma_start(bias_raw[2:4, :], ba.rearrange("(a r) -> a r", a=2))
-        nc.scalar.dma_start(bias_rows[P - 6 : P, 0:P], bo.rearrange("(c p) -> c p", p=P))
-        nc.gpsimd.memset(bias_rows[0 : P - 6, 0:P], 0.0)
-        nc.gpsimd.memset(bias_rows[:, P:PASS], 0.0)
-        make_identity(nc, ident[:])
-
-        wr_raw = [tile("wr_raw%d" % a, [P, 4, PASS], F32) for a in range(2)]
-        v_words = [tile("v_words%d" % a, [P, T], U32) for a in range(2)]
-        v2_words = tile("v2_words", [P, T2], U32)
-        wr_rows = wr.rearrange("(p j) r -> p j r", j=4)
-        for a in range(2):
-            nc.sync.dma_start(wr_raw[a][:], wr_rows[:, :, a * PASS : (a + 1) * PASS])
+        nc.sync.dma_start(idx[:], offs)
+        nc.sync.dma_start(
+            v_sc[ROW0:P, :].rearrange("q (a t) -> q a t", a=2).bitcast(I32),
+            tab_scales.rearrange("a q t -> q a t").bitcast(I32),
+        )
+        nc.sync.dma_start(idx2[:], offs2)
+        nc.sync.dma_start(v2_sc[ROW0:P, :].bitcast(I32), tab2_scales[0].bitcast(I32))
+        nc.sync.dma_start(idx3[:], offs3)
+        nc.sync.dma_start(v3_sc[ROW0:P, :].bitcast(I32), tab3_scales[0].bitcast(I32))
+        nc.sync.dma_start(bias_raw[0:2, :], br.rearrange("(a r) -> a r", a=2))
+        nc.sync.dma_start(wr_raw[0][:], wr_rows[:, :, 0:PASS])
+        nc.sync.dma_start(bias_raw[2:4, :], ba.rearrange("(a r) -> a r", a=2))
+        nc.sync.dma_start(
+            wg_sc_raw[ROW0:P, :].rearrange("q (a c) -> q a c", a=2).bitcast(I32),
+            wg_scales.rearrange("a q c -> q a c").bitcast(I32),
+        )
+        nc.sync.dma_start(wa_sc_raw[ROW0:P, :].bitcast(I32), wa_scales[0].bitcast(I32))
         nc.sync.dma_start(v2_words[:].bitcast(I32), tab2_words[0].rearrange("p t i -> p (t i)").bitcast(I32))
-        for a in range(2):
-            nc.sync.dma_start(v_words[a][:].bitcast(I32), tab_words[a].rearrange("p t i -> p (t i)").bitcast(I32))
+        nc.sync.dma_start(v3_words[:].bitcast(I32), tab3_words[0].bitcast(I32))
+        nc.sync.dma_start(wa_raw[:].bitcast(I32), wa_words[0].rearrange("p c i -> p (c i)").bitcast(I32))
+        nc.sync.dma_start(v_words[0][:].bitcast(I32), tab_words[0].rearrange("p t i -> p (t i)").bitcast(I32))
+        nc.sync.dma_start(bo_rows[0:6, :], bo.rearrange("(c p) -> c p", p=P))
 
         wr_bf = [tile("wr_bf%d" % a, [P, 4 * PASS], BF16) for a in range(2)]
         wr_q = [tile("wr_q%d" % a, [P, PASS], U32) for a in range(2)]
@@ -112,12 +114,9 @@ def tile_list_upgrade_offer_scores_kernel(
         for t in range(4):
             nc.tensor.transpose(bias_ps[:, t * P : (t + 1) * P], bias_rows[:, t * P : (t + 1) * P], ident[:])
         bias = tile("bias", [P, 4, 4], F32)
-        bias_o = tile("bias_o", [P, 6], F32)
         nc.scalar.activation(bias[:], bias_ps[:].rearrange("p (t c) -> p t c", t=4)[:, :, 0:4], IDENTITY)
-        nc.scalar.activation(bias_o[:], bias_ps[:, P - 6 : P], IDENTITY)
 
         cast_wr(nc.scalar.copy, 0)
-        cast_wr(nc.scalar.copy, 1)
 
         got_sc = tile("got_sc", [P, 4 * S], U8)
         for a in range(2):
@@ -131,22 +130,15 @@ def tile_list_upgrade_offer_scores_kernel(
                 staged[96:P, c0:c1].bitcast(I32).rearrange("p (h t u w) -> p h u t w", t=4, u=8, w=4),
                 raw[96:P, :].bitcast(I32).rearrange("p (h u w t) -> p h u t w", t=4, u=8, w=4),
             )
-        for q in range(4):
-            nc.sync.dma_start(
-                planes[32 * q : 32 * q + 4, :].bitcast(I32), staged[ROW0 + 4 * q : ROW0 + 4 * q + 4, :].bitcast(I32)
-            )
+        for r in range(4):
+            nc.sync.dma_start(planes[r:P:32, :].bitcast(I32), staged[ROW0 + r : P : 4, :].bitcast(I32))
+        v_words.append(tile("v_words1", [P, T], U32, tag="wa_sc_raw"))
+        nc.sync.dma_start(v_words[1][:].bitcast(I32), tab_words[1].rearrange("p t i -> p (t i)").bitcast(I32))
         wg_sc = [planes[:, a * H : (a + 1) * H] for a in range(2)]
         wa_sc = planes[:, 2 * H : 3 * H]
         g_sc = [planes[:, 3 * H + a * S : 3 * H + (a + 1) * S] for a in range(2)]
         g2_sc = planes[:, 3 * H + 2 * S : 3 * H + 3 * S]
         g3_sc = planes[:, 3 * H + 3 * S :]
-
-        wg_raw = tile("wg_raw", [P, 4 * H], U8, tag="wg_sc_raw")
-        v3_words = tile("v3_words", [P, T3], U16, tag="wa_sc_raw")
-        nc.sync.dma_start(
-            wg_raw[:].rearrange("p (a c) -> p a c", a=2).bitcast(I32), wg_words.rearrange("a p c -> p a c").bitcast(I32)
-        )
-        nc.sync.dma_start(v3_words[:].bitcast(I32), tab3_words[0].bitcast(I32))
 
         g = [tile("g%d" % a, [P, S], U32) for a in range(2)]
         g2 = tile("g2", [P, S], U32)
@@ -155,19 +147,22 @@ def tile_list_upgrade_offer_scores_kernel(
         wa_p = tile("wa_p", [P, 4 * H], U8)
         quantize(wr_q[0][:], wr_s[0][:], wr_bf[0][:])
         nc.vector.tensor_copy(g2[:], v2_words[:].indirect(idx2[:]))
-        wa_raw = tile("wa_raw", [P, 4 * H], U8, tag="v2_words")
-        nc.sync.dma_start(wa_raw[:].bitcast(I32), wa_words[0].rearrange("p c i -> p (c i)").bitcast(I32))
-        nc.vector.tensor_copy(g[0][:], v_words[0][:].indirect(idx[:]))
-        quantize(wr_q[1][:], wr_s[1][:], wr_bf[1][:])
-        nc.vector.tensor_copy(g[1][:], v_words[1][:].indirect(idx[:]))
-        nc.vector.tensor_copy(
-            wg_p[:].bitcast(I32).rearrange("p (h t q w) -> p h t q w", t=4, q=32, w=2),
-            wg_raw[:].bitcast(I32).rearrange("p (h q t w) -> p h t q w", t=4, q=32, w=2),
+        wg_raw = tile("wg_raw", [P, 4 * H], U8, tag="v2_words")
+        nc.sync.dma_start(
+            wg_raw[:].rearrange("p (a c) -> p a c", a=2).bitcast(I32), wg_words.rearrange("a p c -> p a c").bitcast(I32)
         )
         nc.vector.tensor_copy(g3[:], v3_words[:].indirect(idx3[:]))
+        wr_raw.append(tile("wr_raw1", [P, 4, PASS], F32, tag="v3_words"))
+        nc.sync.dma_start(wr_raw[1][:], wr_rows[:, :, PASS:H])
         nc.vector.tensor_copy(
             wa_p[:].bitcast(I32).rearrange("p (h t q w) -> p h t q w", t=4, q=32, w=4),
             wa_raw[:].bitcast(I32).rearrange("p (h q t w) -> p h t q w", t=4, q=32, w=4),
+        )
+        for a in range(2):
+            nc.vector.tensor_copy(g[a][:], v_words[a][:].indirect(idx[:]))
+        nc.vector.tensor_copy(
+            wg_p[:].bitcast(I32).rearrange("p (h t q w) -> p h t q w", t=4, q=32, w=2),
+            wg_raw[:].bitcast(I32).rearrange("p (h q t w) -> p h t q w", t=4, q=32, w=2),
         )
 
         def load_w(raw, w, a, cols):
@@ -175,21 +170,19 @@ def tile_list_upgrade_offer_scores_kernel(
             for t in range(4):
                 nc.sync.dma_start(raw[:, t, :], rows[t])
 
-        stage2 = [(w1, 0, "v_words0"), (w2, 0, "staged"), (w1, 1, "v_words1")]
-        w_raw = []
-        for w, a, tag in stage2:
-            w_raw.append(tile("w_raw%d" % len(w_raw), [P, 4, N], F32, tag=tag))
-            load_w(w_raw[-1], w, a, slice(0, N))
-        third = N // 3
-        w_last = []
+        w_raw = [tile("w_raw%d" % i, [P, 4, N], F32, tag=tag) for i, tag in enumerate(("v_words0", "staged"))]
+        for i, w in enumerate((w1, w2)):
+            load_w(w_raw[i], w, 0, slice(0, N))
+        late_cols = (slice(0, PASS), slice(PASS, N))
+        late_width = (PASS, N - PASS)
+        w_late = []
 
-        def load_last(tag):
-            i = len(w_last)
-            w_last.append(tile("w_last%d" % i, [P, 4, third], F32, tag=tag))
-            load_w(w_last[i], w2, 1, slice(i * third, (i + 1) * third))
+        def load_late(tags):
+            u = len(w_late)
+            w_late.append([tile("w_late%d%d" % (u, i), [P, 4, late_width[u]], F32, tag=tag) for i, tag in enumerate(tags)])
+            for i, w in enumerate((w1, w2)):
+                load_w(w_late[u][i], w, 1, late_cols[u])
 
-        for tag in ("wg_sc_raw", "wa_sc_raw", "v2_words"):
-            load_last(tag)
 
         room = [tile("room%d" % a, [P, 4, S], F32) for a in range(2)]
         arrival = [tile("arrival%d" % a, [P, 4, S], F32) for a in range(2)]
@@ -233,80 +226,98 @@ def tile_list_upgrade_offer_scores_kernel(
         def product(i, a, n, guest):
             other = (room, arrival)[i][a]
             nc.vector.tensor_tensor(
-                h_bf[i][a][:, 4 * n * CHUNK : 4 * (n + 1) * CHUNK].rearrange("p (c i t) -> p c t i", t=4, i=4),
-                guest[:].rearrange("p (t c i) -> p c t i", t=4, i=4),
-                other[:, :, n * CHUNK : (n + 1) * CHUNK].rearrange("p t (c i) -> p c t i", i=4),
+                h_bf[i][a][:, 4 * n * CHUNK : 4 * (n + 1) * CHUNK].rearrange("p (c i t) -> p c t i", t=4, i=2),
+                guest[:].rearrange("p (t c i) -> p c t i", t=4, i=2),
+                other[:, :, n * CHUNK : (n + 1) * CHUNK].rearrange("p t (c i) -> p c t i", i=2),
                 MULT,
             )
 
         def cast_w(copy, values, raw):
             copy(values.rearrange("p (c i t) -> p c t i", t=4, i=4), raw.rearrange("p t (c i) -> p c t i", i=4))
 
-        w_bf = [tile("w_bf%d" % i, [P, 4 * N], BF16) for i in range(4)]
-        w_q = [tile("w_q%d" % i, [P, N], U32) for i in range(4)]
-        w_s = [tile("w_s%d" % i, [P, N], U8) for i in range(4)]
+        w_bf = [tile("w_bf%d" % i, [P, 4 * N], BF16) for i in range(2)]
+        w_q = [tile("w_q%d" % i, [P, N], U32) for i in range(2)]
+        w_s = [tile("w_s%d" % i, [P, N], U8) for i in range(2)]
+        late_bf = [tile("late_bf%d" % u, [P, 8 * late_width[u]], BF16) for u in range(2)]
+        late_q = [tile("late_q%d" % u, [P, 2 * late_width[u]], U32) for u in range(2)]
+        late_s = [tile("late_s%d" % u, [P, 2 * late_width[u]], U8) for u in range(2)]
 
         def quantize_w(i, c0, c1):
             quantize(w_q[i][:, c0:c1], w_s[i][:, c0:c1], w_bf[i][:, 4 * c0 : 4 * c1])
 
+        def quantize_h(i, a):
+            quantize(h_q[i][a][:], h_s[i][a][:], h_bf[i][a][:])
+
+        def cast_late(copy, u, i):
+            cast_w(copy, late_bf[u][:, 4 * i * late_width[u] : 4 * (i + 1) * late_width[u]], w_late[u][i][:])
+
         make_room(0, (0, 1, 2, 3), (0, 1, 2, 3))
-        make_room(1, (0, 1), (4, 5))
+        bo_ps = bank("bo_ps", 6)
+        nc.tensor.transpose(bo_ps[:, 0:P], bo_rows[:], ident[:])
+        bias_o = tile("bias_o", [P, 6], F32)
+        nc.scalar.activation(bias_o[:], bo_ps[:, 0:6], IDENTITY)
+        make_arrival(0, (4, 5, 6, 7))
         guest = make_guest(0)
-        make_arrival(0, (6, 7, 4, 5))
-        make_room(1, (2, 3), (6, 7))
         make_arrival(1, (4, 5, 6, 7))
-        for n in range(4):
-            product(0, 0, n, guest[n])
-        product(1, 0, 0, guest[0])
-        quantize(h_q[0][0][:], h_s[0][0][:], h_bf[0][0][:])
-        for n in range(1, 4):
-            product(1, 0, n, guest[n])
+        cast_wr(nc.scalar.copy, 1)
+        load_late(("wa_sc_raw", "v2_words"))
+        load_late(("wa_p", "g3"))
+        for i, n in ((0, 0), (0, 1), (1, 0), (1, 1), (0, 2), (1, 2), (0, 3)):
+            product(i, 0, n, guest[n])
+        quantize(wr_q[1][:], wr_s[1][:], wr_bf[1][:])
+        product(1, 0, 3, guest[3])
+        quantize_h(0, 0)
+        make_room(1, (0, 1, 2, 3), (4, 5, 6, 7))
         guest = make_guest(1)
-        for i in range(3):
+        for i in range(2):
             cast_w(nc.scalar.copy, w_bf[i][:, 0 : 4 * PASS], w_raw[i][:, :, 0:PASS])
             cast_w(nc.scalar.copy, w_bf[i][:, 4 * PASS : 4 * N], w_raw[i][:, :, PASS:N])
-        h_bf[0].append(tile("h_bf01", [P, 4 * S], BF16, tag="h_bf0"))
+        cast_late(nc.scalar.copy, 0, 0)
+        cast_late(nc.scalar.copy, 1, 0)
+        quantize_h(1, 0)
+        for i in range(2):
+            h_bf[i].append(tile("h_bf%d1" % i, [P, 4 * S], BF16, tag="h_bf%d" % i))
+        for n in range(4):
+            product(1, 1, n, guest[n])
         product(0, 1, 0, guest[0])
-        quantize(h_q[1][0][:], h_s[1][0][:], h_bf[1][0][:])
-        h_bf[1].append(tile("h_bf11", [P, 4 * S], BF16, tag="h_bf1"))
-        product(1, 1, 0, guest[0])
+        quantize_h(1, 1)
         product(0, 1, 1, guest[1])
-        product(1, 1, 1, guest[1])
         quantize_w(0, 0, PASS)
         quantize_w(0, PASS, N)
         product(0, 1, 2, guest[2])
-        product(1, 1, 2, guest[2])
         product(0, 1, 3, guest[3])
-        product(1, 1, 3, guest[3])
         quantize_w(1, 0, PASS)
-        quantize(h_q[0][1][:], h_s[0][1][:], h_bf[0][1][:])
+        quantize_h(0, 1)
         quantize_w(1, PASS, N)
-        quantize(h_q[1][1][:], h_s[1][1][:], h_bf[1][1][:])
-        cast_w(nc.vector.tensor_copy, w_bf[3][:, 0 : 4 * third], w_last[0][:])
-        quantize_w(2, 0, PASS)
-        cast_w(nc.vector.tensor_copy, w_bf[3][:, 4 * third : 8 * third], w_last[1][:])
-        cast_w(nc.scalar.copy, w_bf[3][:, 8 * third : 12 * third], w_last[2][:])
-        quantize_w(3, 0, third)
-        quantize_w(2, PASS, N)
-        quantize_w(3, third, 2 * third)
-        quantize_w(3, 2 * third, N)
+        cast_late(nc.vector.tensor_copy, 0, 1)
+        cast_late(nc.vector.tensor_copy, 1, 1)
+        for i in (1, 0):
+            for u in range(2):
+                width = late_width[u]
+                quantize(late_q[u][:, i * width : (i + 1) * width], late_s[u][:, i * width : (i + 1) * width],
+                         late_bf[u][:, 4 * i * width : 4 * (i + 1) * width])
 
         acc = [bank("out_ps%d" % c, (4 + c) % 8) for c in range(N // P)]
 
-        def score(c, i):
-            cols = slice(c * P, (c + 1) * P)
-            nc.tensor.matmul_mx(acc[c][:], w_q[i][:, cols].bitcast(FP8X4), w_s[i][:, cols],
-                                h_q[i % 2][i // 2][:].bitcast(FP8X4), h_s[i % 2][i // 2][:], start=(i == 0), stop=(i == 3))
+        def score(c, codes, scales, i, a):
+            nc.tensor.matmul_mx(acc[c][:], codes.bitcast(FP8X4), scales, h_q[i][a][:].bitcast(FP8X4), h_s[i][a][:],
+                                start=((i, a) == (0, 0)), stop=((i, a) == (0, 1)))
 
-        for i in range(3):
+        for i in range(2):
             for c in range(N // P):
-                score(c, i)
-        res = [tile("res%d" % u, [P, 3, S], F32) for u in range(2)]
+                cols = slice(c * P, (c + 1) * P)
+                score(c, w_q[i][:, cols], w_s[i][:, cols], i, 0)
+        res = [tile("res%d" % c, [P, S], F32) for c in range(N // P)]
+        def score_late(c, i):
+            c0 = i * late_width[c // 4] + c % 4 * P
+            score(c, late_q[c // 4][:, c0 : c0 + P], late_s[c // 4][:, c0 : c0 + P], i, 1)
+
         for c in range(N // P):
-            score(c, 3)
-            dst = res[c % 2][:, c // 2, :]
+            score_late(c, 1)
+        for c in range(N // P):
+            score_late(c, 0)
             if c % 2 == 0:
-                nc.scalar.activation(dst, acc[c][:], IDENTITY, bias=bias_o[:, c : c + 1])
+                nc.scalar.activation(res[c][:], acc[c][:], IDENTITY, bias=bias_o[:, c : c + 1])
             else:
-                nc.vector.tensor_scalar(dst, acc[c][:], bias_o[:, c : c + 1], None, ADD)
-            nc.sync.dma_start(out[c * P : (c + 1) * P, :], dst)
+                nc.vector.tensor_scalar(res[c][:], acc[c][:], bias_o[:, c : c + 1], None, ADD)
+            nc.sync.dma_start(out[c * P : (c + 1) * P, :], res[c][:])

@@ -170,9 +170,9 @@ def tile_list_upgrade_offer_scores_kernel(
             for t in range(4):
                 nc.sync.dma_start(raw[:, t, :], rows[t])
 
-        w_raw = [tile("w_raw%d" % i, [P, 4, N], F32, tag=tag) for i, tag in enumerate(("v_words0", "staged"))]
-        for i, w in enumerate((w1, w2)):
-            load_w(w_raw[i], w, 0, slice(0, N))
+        w_raw = [tile("w_raw%d" % i, [P, 4, N], F32, tag=tag) for i, tag in enumerate(("staged", "v_words0"))]
+        for i in (1, 0):
+            load_w(w_raw[i], (w1, w2)[i], 0, slice(0, N))
         late_cols = (slice(0, PASS), slice(PASS, N))
         late_width = (PASS, N - PASS)
         w_late = []
@@ -180,8 +180,8 @@ def tile_list_upgrade_offer_scores_kernel(
         def load_late(tags):
             u = len(w_late)
             w_late.append([tile("w_late%d%d" % (u, i), [P, 4, late_width[u]], F32, tag=tag) for i, tag in enumerate(tags)])
-            for i, w in enumerate((w1, w2)):
-                load_w(w_late[u][i], w, 1, late_cols[u])
+            for i in (1, 0):
+                load_w(w_late[u][i], (w1, w2)[i], 1, late_cols[u])
 
 
         room = [tile("room%d" % a, [P, 4, S], F32) for a in range(2)]
@@ -219,7 +219,7 @@ def tile_list_upgrade_offer_scores_kernel(
                 banks.append(acc)
             return banks
 
-        h_bf = [[tile("h_bf%d0" % i, [P, 4 * S], BF16, tag="h_bf%d" % i)] for i in range(2)]
+        h_bf = [[tile("h_bf%d%d" % (i, a), [P, 4 * S], BF16) for a in range(2)] for i in range(2)]
         h_q = [[tile("h_q%d%d" % (i, a), [P, S], U32) for a in range(2)] for i in range(2)]
         h_s = [[tile("h_s%d%d" % (i, a), [P, S], U8) for a in range(2)] for i in range(2)]
 
@@ -248,6 +248,9 @@ def tile_list_upgrade_offer_scores_kernel(
         def quantize_h(i, a):
             quantize(h_q[i][a][:], h_s[i][a][:], h_bf[i][a][:])
 
+        def quantize_late(u, c0, c1):
+            quantize(late_q[u][:, c0:c1], late_s[u][:, c0:c1], late_bf[u][:, 4 * c0 : 4 * c1])
+
         def cast_late(copy, u, i):
             cast_w(copy, late_bf[u][:, 4 * i * late_width[u] : 4 * (i + 1) * late_width[u]], w_late[u][i][:])
 
@@ -258,52 +261,51 @@ def tile_list_upgrade_offer_scores_kernel(
         nc.scalar.activation(bias_o[:], bo_ps[:, 0:6], IDENTITY)
         make_arrival(0, (4, 5, 6, 7))
         guest = make_guest(0)
-        make_arrival(1, (4, 5, 6, 7))
         cast_wr(nc.scalar.copy, 1)
-        load_late(("wa_sc_raw", "v2_words"))
-        load_late(("wa_p", "g3"))
-        for i, n in ((0, 0), (0, 1), (1, 0), (1, 1), (0, 2), (1, 2), (0, 3)):
+        make_arrival(1, (4, 5, 6, 7))
+        load_late(("v2_words", "wa_sc_raw"))
+        load_late(("g3", "wa_p"))
+        for i, n in ((0, 0), (0, 1), (1, 0), (1, 1), (0, 2), (1, 2)):
             product(i, 0, n, guest[n])
         quantize(wr_q[1][:], wr_s[1][:], wr_bf[1][:])
+        product(0, 0, 3, guest[3])
         product(1, 0, 3, guest[3])
         quantize_h(0, 0)
         make_room(1, (0, 1, 2, 3), (4, 5, 6, 7))
         guest = make_guest(1)
-        for i in range(2):
-            cast_w(nc.scalar.copy, w_bf[i][:, 0 : 4 * PASS], w_raw[i][:, :, 0:PASS])
-            cast_w(nc.scalar.copy, w_bf[i][:, 4 * PASS : 4 * N], w_raw[i][:, :, PASS:N])
+        cast_w(nc.scalar.copy, w_bf[0][:, 0 : 4 * PASS], w_raw[0][:, :, 0:PASS])
+        cast_w(nc.scalar.copy, w_bf[0][:, 4 * PASS : 4 * N], w_raw[0][:, :, PASS:N])
+        cast_late(nc.scalar.copy, 0, 1)
         cast_late(nc.scalar.copy, 0, 0)
-        cast_late(nc.scalar.copy, 1, 0)
         quantize_h(1, 0)
-        for i in range(2):
-            h_bf[i].append(tile("h_bf%d1" % i, [P, 4 * S], BF16, tag="h_bf%d" % i))
-        for n in range(4):
-            product(1, 1, n, guest[n])
+        cast_w(nc.vector.tensor_copy, w_bf[1][:], w_raw[1][:])
+        product(1, 1, 0, guest[0])
+        quantize_w(1, 0, PASS)
+        quantize_w(1, PASS, N)
         product(0, 1, 0, guest[0])
-        quantize_h(1, 1)
+        product(1, 1, 1, guest[1])
         product(0, 1, 1, guest[1])
+        product(1, 1, 2, guest[2])
+        product(1, 1, 3, guest[3])
         quantize_w(0, 0, PASS)
         quantize_w(0, PASS, N)
+        quantize_h(1, 1)
         product(0, 1, 2, guest[2])
+        quantize_late(0, PASS, 2 * PASS)
         product(0, 1, 3, guest[3])
-        quantize_w(1, 0, PASS)
-        quantize_h(0, 1)
-        quantize_w(1, PASS, N)
-        cast_late(nc.vector.tensor_copy, 0, 1)
         cast_late(nc.vector.tensor_copy, 1, 1)
-        for i in (1, 0):
-            for u in range(2):
-                width = late_width[u]
-                quantize(late_q[u][:, i * width : (i + 1) * width], late_s[u][:, i * width : (i + 1) * width],
-                         late_bf[u][:, 4 * i * width : 4 * (i + 1) * width])
+        cast_late(nc.vector.tensor_copy, 1, 0)
+        quantize_h(0, 1)
+        quantize_late(1, 0, PASS)
+        quantize_late(0, 0, PASS)
 
         acc = [bank("out_ps%d" % c, (4 + c) % 8) for c in range(N // P)]
 
         def score(c, codes, scales, i, a):
             nc.tensor.matmul_mx(acc[c][:], codes.bitcast(FP8X4), scales, h_q[i][a][:].bitcast(FP8X4), h_s[i][a][:],
-                                start=((i, a) == (0, 0)), stop=((i, a) == (0, 1)))
+                                start=((i, a) == (1, 0)), stop=((i, a) == (0, 1)))
 
-        for i in range(2):
+        for i in (1, 0):
             for c in range(N // P):
                 cols = slice(c * P, (c + 1) * P)
                 score(c, w_q[i][:, cols], w_s[i][:, cols], i, 0)
@@ -312,9 +314,11 @@ def tile_list_upgrade_offer_scores_kernel(
             c0 = i * late_width[c // 4] + c % 4 * P
             score(c, late_q[c // 4][:, c0 : c0 + P], late_s[c // 4][:, c0 : c0 + P], i, 1)
 
-        for c in range(N // P):
+        for c in range(4):
             score_late(c, 1)
-        for c in range(N // P):
+        for c in (4, 5, 0, 1, 2, 3):
+            if c >= 4:
+                score_late(c, 1)
             score_late(c, 0)
             if c % 2 == 0:
                 nc.scalar.activation(res[c][:], acc[c][:], IDENTITY, bias=bias_o[:, c : c + 1])

@@ -132,8 +132,10 @@ def tile_list_upgrade_offer_scores_kernel(
             )
         for r in range(4):
             nc.sync.dma_start(planes[r:P:32, :].bitcast(I32), staged[ROW0 + r : P : 4, :].bitcast(I32))
-        v_words.append(tile("v_words1", [P, T], U32, tag="wa_sc_raw"))
-        nc.sync.dma_start(v_words[1][:].bitcast(I32), tab_words[1].rearrange("p t i -> p (t i)").bitcast(I32))
+        wg_raw = tile("wg_raw", [P, 4 * H], U8, tag="wa_sc_raw")
+        nc.sync.dma_start(
+            wg_raw[:].rearrange("p (a c) -> p a c", a=2).bitcast(I32), wg_words.rearrange("a p c -> p a c").bitcast(I32)
+        )
         wg_sc = [planes[:, a * H : (a + 1) * H] for a in range(2)]
         wa_sc = planes[:, 2 * H : 3 * H]
         g_sc = [planes[:, 3 * H + a * S : 3 * H + (a + 1) * S] for a in range(2)]
@@ -147,10 +149,8 @@ def tile_list_upgrade_offer_scores_kernel(
         wa_p = tile("wa_p", [P, 4 * H], U8)
         quantize(wr_q[0][:], wr_s[0][:], wr_bf[0][:])
         nc.vector.tensor_copy(g2[:], v2_words[:].indirect(idx2[:]))
-        wg_raw = tile("wg_raw", [P, 4 * H], U8, tag="v2_words")
-        nc.sync.dma_start(
-            wg_raw[:].rearrange("p (a c) -> p a c", a=2).bitcast(I32), wg_words.rearrange("a p c -> p a c").bitcast(I32)
-        )
+        v_words.append(tile("v_words1", [P, T], U32, tag="v2_words"))
+        nc.sync.dma_start(v_words[1][:].bitcast(I32), tab_words[1].rearrange("p t i -> p (t i)").bitcast(I32))
         nc.vector.tensor_copy(g3[:], v3_words[:].indirect(idx3[:]))
         wr_raw.append(tile("wr_raw1", [P, 4, PASS], F32, tag="v3_words"))
         nc.sync.dma_start(wr_raw[1][:], wr_rows[:, :, PASS:H])
@@ -158,20 +158,21 @@ def tile_list_upgrade_offer_scores_kernel(
             wa_p[:].bitcast(I32).rearrange("p (h t q w) -> p h t q w", t=4, q=32, w=4),
             wa_raw[:].bitcast(I32).rearrange("p (h q t w) -> p h t q w", t=4, q=32, w=4),
         )
-        for a in range(2):
-            nc.vector.tensor_copy(g[a][:], v_words[a][:].indirect(idx[:]))
+        nc.vector.tensor_copy(g[0][:], v_words[0][:].indirect(idx[:]))
         nc.vector.tensor_copy(
             wg_p[:].bitcast(I32).rearrange("p (h t q w) -> p h t q w", t=4, q=32, w=2),
             wg_raw[:].bitcast(I32).rearrange("p (h q t w) -> p h t q w", t=4, q=32, w=2),
         )
+        for u in range(2):
+            nc.vector.tensor_copy(g[1][:, u * S // 2 : (u + 1) * S // 2], v_words[1][:].indirect(idx[:, u * 16 : (u + 1) * 16]))
 
         def load_w(raw, w, a, cols):
             rows = w[a * PASS : (a + 1) * PASS, cols].rearrange("(q t e) n -> t q e n", t=4, e=4)
             for t in range(4):
                 nc.sync.dma_start(raw[:, t, :], rows[t])
 
-        w_raw = [tile("w_raw%d" % i, [P, 4, N], F32, tag=tag) for i, tag in enumerate(("staged", "v_words0"))]
-        for i in (1, 0):
+        w_raw = [tile("w_raw%d" % i, [P, 4, N], F32, tag=tag) for i, tag in enumerate(("v_words0", "staged"))]
+        for i in range(2):
             load_w(w_raw[i], (w1, w2)[i], 0, slice(0, N))
         late_cols = (slice(0, PASS), slice(PASS, N))
         late_width = (PASS, N - PASS)
@@ -273,39 +274,35 @@ def tile_list_upgrade_offer_scores_kernel(
         quantize_h(0, 0)
         make_room(1, (0, 1, 2, 3), (4, 5, 6, 7))
         guest = make_guest(1)
-        cast_w(nc.scalar.copy, w_bf[0][:, 0 : 4 * PASS], w_raw[0][:, :, 0:PASS])
-        cast_w(nc.scalar.copy, w_bf[0][:, 4 * PASS : 4 * N], w_raw[0][:, :, PASS:N])
-        cast_late(nc.scalar.copy, 0, 1)
+        for i in range(2):
+            cast_w(nc.scalar.copy, w_bf[i][:, 0 : 4 * PASS], w_raw[i][:, :, 0:PASS])
+            cast_w(nc.scalar.copy, w_bf[i][:, 4 * PASS : 4 * N], w_raw[i][:, :, PASS:N])
         cast_late(nc.scalar.copy, 0, 0)
         quantize_h(1, 0)
-        cast_w(nc.vector.tensor_copy, w_bf[1][:], w_raw[1][:])
-        product(1, 1, 0, guest[0])
-        quantize_w(1, 0, PASS)
-        quantize_w(1, PASS, N)
-        product(0, 1, 0, guest[0])
-        product(1, 1, 1, guest[1])
-        product(0, 1, 1, guest[1])
-        product(1, 1, 2, guest[2])
-        product(1, 1, 3, guest[3])
+        for i, n in ((1, 0), (0, 0), (1, 1), (0, 1), (1, 2), (1, 3)):
+            product(i, 1, n, guest[n])
         quantize_w(0, 0, PASS)
         quantize_w(0, PASS, N)
-        quantize_h(1, 1)
         product(0, 1, 2, guest[2])
-        quantize_late(0, PASS, 2 * PASS)
+        quantize_h(1, 1)
         product(0, 1, 3, guest[3])
+        cast_late(nc.vector.tensor_copy, 0, 1)
+        quantize_h(0, 1)
+        quantize_w(1, 0, PASS)
+        quantize_w(1, PASS, N)
+        quantize_late(0, PASS, 2 * PASS)
         cast_late(nc.vector.tensor_copy, 1, 1)
         cast_late(nc.vector.tensor_copy, 1, 0)
-        quantize_h(0, 1)
-        quantize_late(1, 0, PASS)
         quantize_late(0, 0, PASS)
+        quantize_late(1, 0, PASS)
 
         acc = [bank("out_ps%d" % c, (4 + c) % 8) for c in range(N // P)]
 
         def score(c, codes, scales, i, a):
             nc.tensor.matmul_mx(acc[c][:], codes.bitcast(FP8X4), scales, h_q[i][a][:].bitcast(FP8X4), h_s[i][a][:],
-                                start=((i, a) == (1, 0)), stop=((i, a) == (0, 1)))
+                                start=((i, a) == (0, 0)), stop=((i, a) == (0, 1)))
 
-        for i in (1, 0):
+        for i in range(2):
             for c in range(N // P):
                 cols = slice(c * P, (c + 1) * P)
                 score(c, w_q[i][:, cols], w_s[i][:, cols], i, 0)
@@ -316,11 +313,11 @@ def tile_list_upgrade_offer_scores_kernel(
 
         for c in range(4):
             score_late(c, 1)
-        for c in (4, 5, 0, 1, 2, 3):
+        for c in range(N // P):
             if c >= 4:
                 score_late(c, 1)
             score_late(c, 0)
-            if c % 2 == 0:
+            if c != 4:
                 nc.scalar.activation(res[c][:], acc[c][:], IDENTITY, bias=bias_o[:, c : c + 1])
             else:
                 nc.vector.tensor_scalar(res[c][:], acc[c][:], bias_o[:, c : c + 1], None, ADD)

@@ -22,6 +22,7 @@ P = 128
 PASS = 512
 CHUNK = 128
 ROW0 = 112
+PAIR = 256
 
 
 def tile_list_upgrade_offer_scores_kernel(
@@ -40,35 +41,34 @@ def tile_list_upgrade_offer_scores_kernel(
         def bank(name, b):
             return ps.tile([P, PASS], F32, name=name, tag="bank%d" % b)
 
+        def quantize(codes, scales, values):
+            nc.vector.quantize_mx(out=codes.bitcast(FP8X4), scales=scales, in_=values)
+
         idx = lists.tile([P, S // 16], U16, name="idx")
         idx2 = lists.tile([P, S // 16], U16, name="idx2")
         idx3 = lists.tile([P, S // 16], U16, name="idx3")
         v_sc = tile("v_sc", [P, 2 * T], U8)
         v2_sc = tile("v2_sc", [P, T2], U8)
         v3_sc = tile("v3_sc", [P, T3], U8)
-        wg_sc_raw = tile("wg_sc_raw", [P, 2 * H], U8)
-        wa_sc_raw = tile("wa_sc_raw", [P, H], U8)
+        w_sc_raw = tile("w_sc_raw", [P, 3 * H], U8)
         planes = tile("planes", [P, 3 * H + 4 * S], U8)
         bias_raw = tile("bias_raw", [4, PASS], F32)
-        bias_rows = tile("bias_rows", [P, PASS], F32)
-        bo_rows = tile("bo_rows", [P, P], F32)
+        bo_raw = tile("bo_raw", [2, 3 * P], F32)
+        bias_rows = tile("bias_rows", [P, 7 * P], F32)
         ident = tile("ident", [P, P], F32)
         wr_raw = [tile("wr_raw0", [P, 4, PASS], F32)]
         v_words = [tile("v_words0", [P, T], U32)]
         v2_words = tile("v2_words", [P, T2], U32)
+        wg_raw = tile("wg_raw", [P, 4 * H], U8)
         v3_words = tile("v3_words", [P, T3], U16)
-        wa_raw = tile("wa_raw", [P, 4 * H], U8)
         wr_rows = wr.rearrange("(p j) r -> p j r", j=4)
 
         nc.vector.memset(v_sc[0:ROW0, :].bitcast(I32), 0)
         nc.vector.memset(v2_sc[0:ROW0, :].bitcast(I32), 0)
         nc.vector.memset(v3_sc[0:ROW0, :].bitcast(I32), 0)
-        nc.gpsimd.memset(bo_rows[:], 0.0)
         nc.gpsimd.memset(bias_rows[:], 0.0)
         make_identity(nc, ident[:])
-        nc.gpsimd.memset(wg_sc_raw[96:ROW0, :].bitcast(I32), 0)
-        nc.gpsimd.memset(wa_sc_raw[96:ROW0, :].bitcast(I32), 0)
-        nc.gpsimd.memset(planes[:].bitcast(I32), 0)
+        nc.gpsimd.memset(w_sc_raw[0:ROW0, :].bitcast(I32), 0)
 
         nc.sync.dma_start(idx[:], offs)
         nc.sync.dma_start(
@@ -77,25 +77,25 @@ def tile_list_upgrade_offer_scores_kernel(
         )
         nc.sync.dma_start(idx2[:], offs2)
         nc.sync.dma_start(v2_sc[ROW0:P, :].bitcast(I32), tab2_scales[0].bitcast(I32))
+        nc.sync.dma_start(wr_raw[0][:], wr_rows[:, :, 0:PASS])
         nc.sync.dma_start(idx3[:], offs3)
         nc.sync.dma_start(v3_sc[ROW0:P, :].bitcast(I32), tab3_scales[0].bitcast(I32))
-        nc.sync.dma_start(bias_raw[0:2, :], br.rearrange("(a r) -> a r", a=2))
-        nc.sync.dma_start(wr_raw[0][:], wr_rows[:, :, 0:PASS])
-        nc.sync.dma_start(bias_raw[2:4, :], ba.rearrange("(a r) -> a r", a=2))
         nc.sync.dma_start(
-            wg_sc_raw[ROW0:P, :].rearrange("q (a c) -> q a c", a=2).bitcast(I32),
+            w_sc_raw[ROW0:P, 0 : 2 * H].rearrange("q (a c) -> q a c", a=2).bitcast(I32),
             wg_scales.rearrange("a q c -> q a c").bitcast(I32),
         )
-        nc.sync.dma_start(wa_sc_raw[ROW0:P, :].bitcast(I32), wa_scales[0].bitcast(I32))
+        nc.sync.dma_start(w_sc_raw[ROW0:P, 2 * H :].bitcast(I32), wa_scales[0].bitcast(I32))
+        nc.sync.dma_start(bias_raw[0:2, :], br.rearrange("(a r) -> a r", a=2))
         nc.sync.dma_start(v2_words[:].bitcast(I32), tab2_words[0].rearrange("p t i -> p (t i)").bitcast(I32))
-        nc.sync.dma_start(v3_words[:].bitcast(I32), tab3_words[0].bitcast(I32))
-        nc.sync.dma_start(wa_raw[:].bitcast(I32), wa_words[0].rearrange("p c i -> p (c i)").bitcast(I32))
+        nc.sync.dma_start(
+            wg_raw[:].rearrange("p (a c) -> p a c", a=2).bitcast(I32), wg_words.rearrange("a p c -> p a c").bitcast(I32)
+        )
+        nc.sync.dma_start(bias_raw[2:4, :], ba.rearrange("(a r) -> a r", a=2))
+        nc.sync.dma_start(bo_raw[:], bo.rearrange("(h n) -> h n", h=2))
         nc.sync.dma_start(v_words[0][:].bitcast(I32), tab_words[0].rearrange("p t i -> p (t i)").bitcast(I32))
-        nc.sync.dma_start(bo_rows[0:6, :], bo.rearrange("(c p) -> c p", p=P))
+        nc.sync.dma_start(v3_words[:].bitcast(I32), tab3_words[0].bitcast(I32))
 
         wr_bf = [tile("wr_bf%d" % a, [P, 4 * PASS], BF16) for a in range(2)]
-        wr_q = [tile("wr_q%d" % a, [P, PASS], U32) for a in range(2)]
-        wr_s = [tile("wr_s%d" % a, [P, PASS], U8) for a in range(2)]
 
         def cast_wr(copy, a):
             copy(
@@ -103,39 +103,38 @@ def tile_list_upgrade_offer_scores_kernel(
                 wr_raw[a][:].rearrange("p j (q t e) -> p t q j e", t=4, e=4),
             )
 
-        def quantize(codes, scales, values):
-            nc.vector.quantize_mx(out=codes.bitcast(FP8X4), scales=scales, in_=values)
+        cast_wr(nc.scalar.copy, 0)
 
         nc.scalar.copy(
-            bias_rows[0:4, :].rearrange("a (t q e) -> a t q e", t=4, e=4),
+            bias_rows[0:4, 0:PASS].rearrange("a (t q e) -> a t q e", t=4, e=4),
             bias_raw[:].rearrange("a (q t e) -> a t q e", t=4, e=4),
         )
-        bias_ps = bank("bias_ps", 7)
+        bias_ps = bank("bias_ps", 2)
         for t in range(4):
             nc.tensor.transpose(bias_ps[:, t * P : (t + 1) * P], bias_rows[:, t * P : (t + 1) * P], ident[:])
         bias = tile("bias", [P, 4, 4], F32)
         nc.scalar.activation(bias[:], bias_ps[:].rearrange("p (t c) -> p t c", t=4)[:, :, 0:4], IDENTITY)
-
-        cast_wr(nc.scalar.copy, 0)
+        nc.scalar.copy(bias_rows[0:2, PASS:], bo_raw[:])
+        bo_ps = bank("bo_ps", 3)
+        for c in range(3):
+            nc.tensor.transpose(bo_ps[:, c * P : (c + 1) * P], bias_rows[:, PASS + c * P : PASS + (c + 1) * P], ident[:])
+        bias_o = tile("bias_o", [P, 3, 2], F32)
+        nc.scalar.activation(bias_o[:], bo_ps[:, 0 : 3 * P].rearrange("p (c h) -> p c h", c=3)[:, :, 0:2], IDENTITY)
 
         got_sc = tile("got_sc", [P, 4 * S], U8)
         for a in range(2):
             nc.vector.tensor_copy(got_sc[:, a * S : (a + 1) * S], v_sc[:, a * T : (a + 1) * T].indirect(idx[:]))
         nc.vector.tensor_copy(got_sc[:, 2 * S : 3 * S], v2_sc[:].indirect(idx2[:]))
         nc.vector.tensor_copy(got_sc[:, 3 * S : 4 * S], v3_sc[:].indirect(idx3[:]))
-        staged = tile("staged", [P, 3 * H + 4 * S], U8)
-        nc.vector.tensor_copy(staged[96:P, 3 * H :].bitcast(I32), got_sc[96:P, :].bitcast(I32))
-        for raw, c0, c1 in ((wg_sc_raw, 0, 2 * H), (wa_sc_raw, 2 * H, 3 * H)):
-            nc.vector.tensor_copy(
-                staged[96:P, c0:c1].bitcast(I32).rearrange("p (h t u w) -> p h u t w", t=4, u=8, w=4),
-                raw[96:P, :].bitcast(I32).rearrange("p (h u w t) -> p h u t w", t=4, u=8, w=4),
-            )
-        for r in range(4):
-            nc.sync.dma_start(planes[r:P:32, :].bitcast(I32), staged[ROW0 + r : P : 4, :].bitcast(I32))
-        wg_raw = tile("wg_raw", [P, 4 * H], U8, tag="wa_sc_raw")
-        nc.sync.dma_start(
-            wg_raw[:].rearrange("p (a c) -> p a c", a=2).bitcast(I32), wg_words.rearrange("a p c -> p a c").bitcast(I32)
+        nc.vector.tensor_copy(planes[:, 3 * H :].bitcast(I32), got_sc[:].bitcast(I32))
+        nc.vector.tensor_copy(
+            planes[:, 0 : 3 * H].bitcast(I32).rearrange("p (h t u w) -> p h u t w", t=4, u=8, w=4),
+            w_sc_raw[:].bitcast(I32).rearrange("p (h u w t) -> p h u t w", t=4, u=8, w=4),
         )
+        for r in range(4):
+            nc.sync.dma_start(planes[r:P:32, :].bitcast(I32), planes[ROW0 + r : P : 4, :].bitcast(I32))
+        v_words.append(tile("v_words1", [P, T], U32, tag="w_sc_raw"))
+        nc.sync.dma_start(v_words[1][:].bitcast(I32), tab_words[1].rearrange("p t i -> p (t i)").bitcast(I32))
         wg_sc = [planes[:, a * H : (a + 1) * H] for a in range(2)]
         wa_sc = planes[:, 2 * H : 3 * H]
         g_sc = [planes[:, 3 * H + a * S : 3 * H + (a + 1) * S] for a in range(2)]
@@ -147,58 +146,48 @@ def tile_list_upgrade_offer_scores_kernel(
         g3 = tile("g3", [P, S], U16)
         wg_p = tile("wg_p", [P, 4 * H], U8)
         wa_p = tile("wa_p", [P, 4 * H], U8)
-        quantize(wr_q[0][:], wr_s[0][:], wr_bf[0][:])
+        wr_q = [tile("wr_q%d" % a, [P, PASS], U32, tag=tag) for a, tag in enumerate(("got_sc", "wr_q1"))]
+        wr_s = [tile("wr_s%d" % a, [P, PASS], U8) for a in range(2)]
         nc.vector.tensor_copy(g2[:], v2_words[:].indirect(idx2[:]))
-        v_words.append(tile("v_words1", [P, T], U32, tag="v2_words"))
-        nc.sync.dma_start(v_words[1][:].bitcast(I32), tab_words[1].rearrange("p t i -> p (t i)").bitcast(I32))
-        nc.vector.tensor_copy(g3[:], v3_words[:].indirect(idx3[:]))
-        wr_raw.append(tile("wr_raw1", [P, 4, PASS], F32, tag="v3_words"))
+        wa_raw = tile("wa_raw", [P, 4 * H], U8, tag="v2_words")
+        nc.sync.dma_start(wa_raw[:].bitcast(I32), wa_words[0].rearrange("p c i -> p (c i)").bitcast(I32))
+        quantize(wr_q[0][:], wr_s[0][:], wr_bf[0][:])
+        wr_raw.append(tile("wr_raw1", [P, 4, PASS], F32, tag="wr_bf0"))
         nc.sync.dma_start(wr_raw[1][:], wr_rows[:, :, PASS:H])
-        nc.vector.tensor_copy(
-            wa_p[:].bitcast(I32).rearrange("p (h t q w) -> p h t q w", t=4, q=32, w=4),
-            wa_raw[:].bitcast(I32).rearrange("p (h q t w) -> p h t q w", t=4, q=32, w=4),
-        )
-        nc.vector.tensor_copy(g[0][:], v_words[0][:].indirect(idx[:]))
         nc.vector.tensor_copy(
             wg_p[:].bitcast(I32).rearrange("p (h t q w) -> p h t q w", t=4, q=32, w=2),
             wg_raw[:].bitcast(I32).rearrange("p (h q t w) -> p h t q w", t=4, q=32, w=2),
         )
+        nc.vector.tensor_copy(g[0][:], v_words[0][:].indirect(idx[:]))
+        w_raw = tile("w_raw", [P, 4, 4, N], F32, tag="v_words0")
+        for a in range(2):
+            for i in range(2):
+                rows = (w1, w2)[i][a * PASS : (a + 1) * PASS, :].rearrange("(q t e) n -> t q e n", t=4, e=4)
+                for t in range(4):
+                    nc.sync.dma_start(w_raw[:, 2 * a + i, t, :], rows[t])
+
+        nc.vector.tensor_copy(g3[:], v3_words[:].indirect(idx3[:]))
         for u in range(2):
             nc.vector.tensor_copy(g[1][:, u * S // 2 : (u + 1) * S // 2], v_words[1][:].indirect(idx[:, u * 16 : (u + 1) * 16]))
-
-        def load_w(raw, w, a, cols):
-            rows = w[a * PASS : (a + 1) * PASS, cols].rearrange("(q t e) n -> t q e n", t=4, e=4)
-            for t in range(4):
-                nc.sync.dma_start(raw[:, t, :], rows[t])
-
-        w_raw = [tile("w_raw%d" % i, [P, 4, N], F32, tag=tag) for i, tag in enumerate(("v_words0", "staged"))]
-        for i in range(2):
-            load_w(w_raw[i], (w1, w2)[i], 0, slice(0, N))
-        late_cols = (slice(0, PASS), slice(PASS, N))
-        late_width = (PASS, N - PASS)
-        w_late = []
-
-        def load_late(tags):
-            u = len(w_late)
-            w_late.append([tile("w_late%d%d" % (u, i), [P, 4, late_width[u]], F32, tag=tag) for i, tag in enumerate(tags)])
-            for i in (1, 0):
-                load_w(w_late[u][i], (w1, w2)[i], 1, late_cols[u])
-
+        nc.vector.tensor_copy(
+            wa_p[:].bitcast(I32).rearrange("p (h t q w) -> p h t q w", t=4, q=32, w=4),
+            wa_raw[:].bitcast(I32).rearrange("p (h q t w) -> p h t q w", t=4, q=32, w=4),
+        )
 
         room = [tile("room%d" % a, [P, 4, S], F32) for a in range(2)]
         arrival = [tile("arrival%d" % a, [P, 4, S], F32) for a in range(2)]
 
-        def make_room(a, slots, banks):
-            for t, b in zip(slots, banks):
-                acc = bank("room_ps%d%d" % (a, t), b)
+        def make_room(a):
+            for t in range(4):
+                acc = bank("room_ps%d%d" % (a, t), 4 + t)
                 cols = slice(t * P, (t + 1) * P)
                 nc.tensor.matmul_mx(acc[:], wr_q[a][:, cols].bitcast(FP8X4), wr_s[a][:, cols], g2[:].bitcast(FP8X4), g2_sc,
                                     start=True, stop=True)
                 nc.scalar.activation(room[a][:, t, :], acc[:], IDENTITY, bias=bias[:, t, a : a + 1])
 
-        def make_arrival(a, banks):
-            for t, b in enumerate(banks):
-                acc = bank("arrival_ps%d%d" % (a, t), b)
+        def make_arrival(a):
+            for t in range(4):
+                acc = bank("arrival_ps%d%d" % (a, t), 4 + t)
                 c0 = a * PASS + t * P
                 nc.tensor.matmul_mx(acc[:], wa_p[:, 4 * c0 : 4 * (c0 + P)].bitcast(FP8X4), wa_sc[:, c0 : c0 + P],
                                     g3[:].bitcast(FP4X4), g3_sc, start=True, stop=True)
@@ -236,89 +225,72 @@ def tile_list_upgrade_offer_scores_kernel(
         def cast_w(copy, values, raw):
             copy(values.rearrange("p (c i t) -> p c t i", t=4, i=4), raw.rearrange("p t (c i) -> p c t i", i=4))
 
-        w_bf = [tile("w_bf%d" % i, [P, 4 * N], BF16) for i in range(2)]
+        w_bf = [tile("w_bf%d" % i, [P, 4 * N], BF16, tag=tag) for i, tag in enumerate(("wr_raw0", "w_sc_raw"))]
         w_q = [tile("w_q%d" % i, [P, N], U32) for i in range(2)]
         w_s = [tile("w_s%d" % i, [P, N], U8) for i in range(2)]
-        late_bf = [tile("late_bf%d" % u, [P, 8 * late_width[u]], BF16) for u in range(2)]
-        late_q = [tile("late_q%d" % u, [P, 2 * late_width[u]], U32) for u in range(2)]
-        late_s = [tile("late_s%d" % u, [P, 2 * late_width[u]], U8) for u in range(2)]
+        late_bf = [tile("late_bf%d" % u, [P, 8 * PAIR], BF16, tag=tag) for u, tag in enumerate(("v2_words", "v3_words", "wg_raw"))]
+        late_q = [tile("late_q%d" % u, [P, 2 * PAIR], U32) for u in range(3)]
+        late_s = [tile("late_s%d" % u, [P, 2 * PAIR], U8) for u in range(3)]
 
-        def quantize_w(i, c0, c1):
-            quantize(w_q[i][:, c0:c1], w_s[i][:, c0:c1], w_bf[i][:, 4 * c0 : 4 * c1])
+        def quantize_w(i):
+            for c0, c1 in ((0, PASS), (PASS, N)):
+                quantize(w_q[i][:, c0:c1], w_s[i][:, c0:c1], w_bf[i][:, 4 * c0 : 4 * c1])
 
         def quantize_h(i, a):
             quantize(h_q[i][a][:], h_s[i][a][:], h_bf[i][a][:])
 
-        def quantize_late(u, c0, c1):
-            quantize(late_q[u][:, c0:c1], late_s[u][:, c0:c1], late_bf[u][:, 4 * c0 : 4 * c1])
-
         def cast_late(copy, u, i):
-            cast_w(copy, late_bf[u][:, 4 * i * late_width[u] : 4 * (i + 1) * late_width[u]], w_late[u][i][:])
+            cast_w(copy, late_bf[u][:, 4 * i * PAIR : 4 * (i + 1) * PAIR], w_raw[:, 2 + i, :, u * PAIR : (u + 1) * PAIR])
 
-        make_room(0, (0, 1, 2, 3), (0, 1, 2, 3))
-        bo_ps = bank("bo_ps", 6)
-        nc.tensor.transpose(bo_ps[:, 0:P], bo_rows[:], ident[:])
-        bias_o = tile("bias_o", [P, 6], F32)
-        nc.scalar.activation(bias_o[:], bo_ps[:, 0:6], IDENTITY)
-        make_arrival(0, (4, 5, 6, 7))
+        make_room(0)
         guest = make_guest(0)
-        cast_wr(nc.scalar.copy, 1)
-        make_arrival(1, (4, 5, 6, 7))
-        load_late(("v2_words", "wa_sc_raw"))
-        load_late(("g3", "wa_p"))
-        for i, n in ((0, 0), (0, 1), (1, 0), (1, 1), (0, 2), (1, 2)):
-            product(i, 0, n, guest[n])
-        quantize(wr_q[1][:], wr_s[1][:], wr_bf[1][:])
-        product(0, 0, 3, guest[3])
-        product(1, 0, 3, guest[3])
+        make_arrival(0)
+        make_arrival(1)
+        for n in range(4):
+            product(0, 0, n, guest[n])
+        cast_wr(nc.vector.tensor_copy, 1)
         quantize_h(0, 0)
-        make_room(1, (0, 1, 2, 3), (4, 5, 6, 7))
+        quantize(wr_q[1][:], wr_s[1][:], wr_bf[1][:])
+        make_room(1)
+        for n in range(4):
+            product(1, 0, n, guest[n])
         guest = make_guest(1)
-        for i in range(2):
-            cast_w(nc.scalar.copy, w_bf[i][:, 0 : 4 * PASS], w_raw[i][:, :, 0:PASS])
-            cast_w(nc.scalar.copy, w_bf[i][:, 4 * PASS : 4 * N], w_raw[i][:, :, PASS:N])
-        cast_late(nc.scalar.copy, 0, 0)
         quantize_h(1, 0)
-        for i, n in ((1, 0), (0, 0), (1, 1), (0, 1), (1, 2), (1, 3)):
-            product(i, 1, n, guest[n])
-        quantize_w(0, 0, PASS)
-        quantize_w(0, PASS, N)
-        product(0, 1, 2, guest[2])
+        for i in range(2):
+            cast_w(nc.scalar.copy, w_bf[i][:], w_raw[:, i])
+        for n in range(4):
+            product(1, 1, n, guest[n])
         quantize_h(1, 1)
-        product(0, 1, 3, guest[3])
-        cast_late(nc.vector.tensor_copy, 0, 1)
+        for n in range(4):
+            product(0, 1, n, guest[n])
+        quantize_w(0)
         quantize_h(0, 1)
-        quantize_w(1, 0, PASS)
-        quantize_w(1, PASS, N)
-        quantize_late(0, PASS, 2 * PASS)
-        cast_late(nc.vector.tensor_copy, 1, 1)
-        cast_late(nc.vector.tensor_copy, 1, 0)
-        quantize_late(0, 0, PASS)
-        quantize_late(1, 0, PASS)
+        quantize_w(1)
 
         acc = [bank("out_ps%d" % c, (4 + c) % 8) for c in range(N // P)]
 
         def score(c, codes, scales, i, a):
             nc.tensor.matmul_mx(acc[c][:], codes.bitcast(FP8X4), scales, h_q[i][a][:].bitcast(FP8X4), h_s[i][a][:],
-                                start=((i, a) == (0, 0)), stop=((i, a) == (0, 1)))
+                                start=((i, a) == (0, 0)), stop=((i, a) == (1, 1)))
 
         for i in range(2):
             for c in range(N // P):
                 cols = slice(c * P, (c + 1) * P)
                 score(c, w_q[i][:, cols], w_s[i][:, cols], i, 0)
-        res = [tile("res%d" % c, [P, S], F32) for c in range(N // P)]
-        def score_late(c, i):
-            c0 = i * late_width[c // 4] + c % 4 * P
-            score(c, late_q[c // 4][:, c0 : c0 + P], late_s[c // 4][:, c0 : c0 + P], i, 1)
-
-        for c in range(4):
-            score_late(c, 1)
-        for c in range(N // P):
-            if c >= 4:
-                score_late(c, 1)
-            score_late(c, 0)
-            if c != 4:
-                nc.scalar.activation(res[c][:], acc[c][:], IDENTITY, bias=bias_o[:, c : c + 1])
-            else:
-                nc.vector.tensor_scalar(res[c][:], acc[c][:], bias_o[:, c : c + 1], None, ADD)
-            nc.sync.dma_start(out[c * P : (c + 1) * P, :], res[c][:])
+        res = [tile("res%d" % c, [P, S], F32, tag=tag) for c, tag in enumerate(("g0", "g1", "g2", "wr_q1", "wr_bf0", "got_sc"))]
+        casts = ((nc.scalar.copy, nc.vector.tensor_copy), (nc.scalar.copy, nc.vector.tensor_copy), (nc.scalar.copy, nc.scalar.copy))
+        for u in range(3):
+            for i in range(2):
+                cast_late(casts[u][i], u, i)
+        for u in range(3):
+            quantize(late_q[u][:], late_s[u][:], late_bf[u][:])
+            for c in (2 * u, 2 * u + 1):
+                for i in range(2):
+                    c0 = i * PAIR + c % 2 * P
+                    score(c, late_q[u][:, c0 : c0 + P], late_s[u][:, c0 : c0 + P], i, 1)
+                bo_c = bias_o[:, c % 3, c // 3 : c // 3 + 1]
+                if c != 5:
+                    nc.scalar.activation(res[c][:], acc[c][:], IDENTITY, bias=bo_c)
+                else:
+                    nc.vector.tensor_scalar(res[c][:], acc[c][:], bo_c, None, ADD)
+                nc.sync.dma_start(out[c * P : (c + 1) * P, :], res[c][:])

@@ -159,12 +159,17 @@ def tile_list_upgrade_offer_scores_kernel(
             wg_raw[:].bitcast(I32).rearrange("p (h q t w) -> p h t q w", t=4, q=32, w=2),
         )
         nc.vector.tensor_copy(g[0][:], v_words[0][:].indirect(idx[:]))
-        w_raw = tile("w_raw", [P, 4, 4, N], F32, tag="v_words0")
-        for a in range(2):
-            for i in range(2):
-                rows = (w1, w2)[i][a * PASS : (a + 1) * PASS, :].rearrange("(q t e) n -> t q e n", t=4, e=4)
-                for t in range(4):
-                    nc.sync.dma_start(w_raw[:, 2 * a + i, t, :], rows[t])
+        w_raw = tile("w_raw", [P, 16 * N], F32, tag="v_words0")
+        raw = {}
+        at = 0
+        for k, c0, c1 in ((0, 0, N), (1, 0, N), (2, 0, N), (3, 0, PASS), (3, PASS, N)):
+            piece = w_raw[:, at : at + 4 * (c1 - c0)].rearrange("p (t n) -> p t n", t=4)
+            at = at + 4 * (c1 - c0)
+            rows = (w1, w2)[k % 2][k // 2 * PASS : (k // 2 + 1) * PASS, c0:c1].rearrange("(q t e) n -> t q e n", t=4, e=4)
+            for t in range(4):
+                nc.sync.dma_start(piece[:, t, :], rows[t])
+            for c in range(c0 // P, c1 // P):
+                raw[k, c] = (piece, c * P - c0)
 
         nc.vector.tensor_copy(g3[:], v3_words[:].indirect(idx3[:]))
         for u in range(2):
@@ -222,75 +227,120 @@ def tile_list_upgrade_offer_scores_kernel(
                 MULT,
             )
 
-        def cast_w(copy, values, raw):
-            copy(values.rearrange("p (c i t) -> p c t i", t=4, i=4), raw.rearrange("p t (c i) -> p c t i", i=4))
+        groups = {}
+        place = {}
 
-        w_bf = [tile("w_bf%d" % i, [P, 4 * N], BF16, tag=tag) for i, tag in enumerate(("wr_raw0", "w_sc_raw"))]
-        w_q = [tile("w_q%d" % i, [P, N], U32) for i in range(2)]
-        w_s = [tile("w_s%d" % i, [P, N], U8) for i in range(2)]
-        late_bf = [tile("late_bf%d" % u, [P, 8 * PAIR], BF16, tag=tag) for u, tag in enumerate(("v2_words", "v3_words", "wg_raw"))]
-        late_q = [tile("late_q%d" % u, [P, 2 * PAIR], U32) for u in range(3)]
-        late_s = [tile("late_s%d" % u, [P, 2 * PAIR], U8) for u in range(3)]
+        def new_group(name, tiles, tag):
+            width = P * len(tiles)
+            groups[name] = (
+                tile(name + "_bf", [P, 4 * width], BF16, tag=tag),
+                tile(name + "_q", [P, width], U32),
+                tile(name + "_s", [P, width], U8),
+            )
+            for j, kc in enumerate(tiles):
+                place[kc] = (name, j * P)
 
-        def quantize_w(i):
-            for c0, c1 in ((0, PASS), (PASS, N)):
-                quantize(w_q[i][:, c0:c1], w_s[i][:, c0:c1], w_bf[i][:, 4 * c0 : 4 * c1])
+        def cast_w(engine, k, c0, c1):
+            piece, r0 = raw[k, c0]
+            name, b0 = place[k, c0]
+            width = P * (c1 - c0)
+            src = piece[:, :, r0 : r0 + width]
+            dst = groups[name][0][:, 4 * b0 : 4 * (b0 + width)]
+            if engine == "pool":
+                nc.gpsimd.tensor_scalar(dst.rearrange("p (n t) -> p n t", t=4), src.rearrange("p t n -> p n t"), 1.0, 0.0, MULT, ADD)
+            else:
+                copy = nc.scalar.copy if engine == "scalar" else nc.vector.tensor_copy
+                copy(dst.rearrange("p (c i t) -> p c t i", t=4, i=4), src.rearrange("p t (c i) -> p c t i", i=4))
+
+        def quantize_w(name):
+            values, codes, scales = groups[name]
+            quantize(codes[:], scales[:], values[:])
 
         def quantize_h(i, a):
             quantize(h_q[i][a][:], h_s[i][a][:], h_bf[i][a][:])
 
-        def cast_late(copy, u, i):
-            cast_w(copy, late_bf[u][:, 4 * i * PAIR : 4 * (i + 1) * PAIR], w_raw[:, 2 + i, :, u * PAIR : (u + 1) * PAIR])
+        acc = {}
+        done = {}
 
+        def score(k, tiles):
+            for c in tiles:
+                if c not in acc:
+                    acc[c] = bank("out_ps%d" % c, (4 + c) % 8)
+                done[c] = done.get(c, 0) + 1
+                name, b0 = place[k, c]
+                cols = slice(b0, b0 + P)
+                nc.tensor.matmul_mx(acc[c][:], groups[name][1][:, cols].bitcast(FP8X4), groups[name][2][:, cols],
+                                    h_q[k % 2][k // 2][:].bitcast(FP8X4), h_s[k % 2][k // 2][:],
+                                    start=(done[c] == 1), stop=(done[c] == 4))
+
+        def finish(c, engine):
+            res = tile("res%d" % c, [P, S], F32, tag=("g0", "g1", "g2", "wr_q1", "wr_bf0", "got_sc")[c])
+            bo_c = bias_o[:, c % 3, c // 3 : c // 3 + 1]
+            if engine == "vector":
+                nc.vector.tensor_scalar(res[:], acc[c][:], bo_c, None, ADD)
+            else:
+                nc.scalar.activation(res[:], acc[c][:], IDENTITY, bias=bo_c)
+            nc.sync.dma_start(out[c * P : (c + 1) * P, :], res[:])
+
+        new_group("w0a", [(0, 0), (0, 1)], "v_sc")
+        new_group("w1a", [(1, c) for c in range(4)], "wr_raw0")
+        new_group("w2a", [(2, c) for c in range(4)], "w_sc_raw")
+        new_group("w3a", [(3, c) for c in range(4)], "v2_words")
+        new_group("last", [(2, 4), (2, 5), (3, 4), (3, 5)], "wg_raw")
         make_room(0)
         guest = make_guest(0)
         make_arrival(0)
         make_arrival(1)
-        for n in range(4):
-            product(0, 0, n, guest[n])
-        cast_wr(nc.vector.tensor_copy, 1)
-        quantize_h(0, 0)
-        quantize(wr_q[1][:], wr_s[1][:], wr_bf[1][:])
-        make_room(1)
-        for n in range(4):
-            product(1, 0, n, guest[n])
-        guest = make_guest(1)
-        quantize_h(1, 0)
+        for t in range(4):
+            nc.gpsimd.tensor_scalar(
+                wr_bf[1][:].rearrange("p (t q e j) -> p t q e j", t=4, e=4, j=4)[:, t],
+                wr_raw[1][:].rearrange("p j (q t e) -> p t q e j", t=4, e=4)[:, t],
+                1.0, 0.0, MULT, ADD,
+            )
         for i in range(2):
-            cast_w(nc.scalar.copy, w_bf[i][:], w_raw[:, i])
+            for n in range(4):
+                product(i, 0, n, guest[n])
+        quantize(wr_q[1][:], wr_s[1][:], wr_bf[1][:])
+        cast_w("scalar", 0, 0, 2)
+        make_room(1)
+        guest = make_guest(1)
+        quantize_h(0, 0)
+        quantize_w("w0a")
+        quantize_h(1, 0)
+        score(0, (0, 1))
+        new_group("w0b", [(0, c) for c in range(2, 6)], "h_bf10")
+        for c in range(2, 6):
+            cast_w("pool", 0, c, c + 1)
+        new_group("w1b", [(1, 4), (1, 5)], "v3_words")
+        for c in range(4, 6):
+            cast_w("pool", 1, c, c + 1)
+        cast_w("scalar", 1, 0, 4)
+        cast_w("scalar", 2, 0, 4)
+        cast_w("scalar", 3, 0, 4)
         for n in range(4):
             product(1, 1, n, guest[n])
-        quantize_h(1, 1)
-        for n in range(4):
+        for n in range(2):
             product(0, 1, n, guest[n])
-        quantize_w(0)
+        quantize_w("w0b")
+        score(0, range(2, 6))
+        for n in range(2, 4):
+            product(0, 1, n, guest[n])
+        quantize_w("w1a")
+        score(1, range(4))
         quantize_h(0, 1)
-        quantize_w(1)
-
-        acc = [bank("out_ps%d" % c, (4 + c) % 8) for c in range(N // P)]
-
-        def score(c, codes, scales, i, a):
-            nc.tensor.matmul_mx(acc[c][:], codes.bitcast(FP8X4), scales, h_q[i][a][:].bitcast(FP8X4), h_s[i][a][:],
-                                start=((i, a) == (0, 0)), stop=((i, a) == (1, 1)))
-
-        for i in range(2):
-            for c in range(N // P):
-                cols = slice(c * P, (c + 1) * P)
-                score(c, w_q[i][:, cols], w_s[i][:, cols], i, 0)
-        res = [tile("res%d" % c, [P, S], F32, tag=tag) for c, tag in enumerate(("g0", "g1", "g2", "wr_q1", "wr_bf0", "got_sc"))]
-        casts = ((nc.scalar.copy, nc.vector.tensor_copy), (nc.scalar.copy, nc.vector.tensor_copy), (nc.scalar.copy, nc.scalar.copy))
-        for u in range(3):
-            for i in range(2):
-                cast_late(casts[u][i], u, i)
-        for u in range(3):
-            quantize(late_q[u][:], late_s[u][:], late_bf[u][:])
-            for c in (2 * u, 2 * u + 1):
-                for i in range(2):
-                    c0 = i * PAIR + c % 2 * P
-                    score(c, late_q[u][:, c0 : c0 + P], late_s[u][:, c0 : c0 + P], i, 1)
-                bo_c = bias_o[:, c % 3, c // 3 : c // 3 + 1]
-                if c != 5:
-                    nc.scalar.activation(res[c][:], acc[c][:], IDENTITY, bias=bo_c)
-                else:
-                    nc.vector.tensor_scalar(res[c][:], acc[c][:], bo_c, None, ADD)
-                nc.sync.dma_start(out[c * P : (c + 1) * P, :], res[c][:])
+        quantize_w("w1b")
+        score(1, (4, 5))
+        quantize_w("w2a")
+        score(2, range(4))
+        quantize_h(1, 1)
+        cast_w("vector", 2, 4, 6)
+        cast_w("vector", 3, 4, 6)
+        quantize_w("w3a")
+        quantize_w("last")
+        for c in range(4):
+            score(3, (c,))
+            finish(c, "scalar")
+        for c in (4, 5):
+            score(2, (c,))
+            score(3, (c,))
+            finish(c, ("vector", "scalar")[c % 2])

@@ -50,7 +50,6 @@ def tile_list_upgrade_offer_scores_kernel(
         v_sc = tile("v_sc", [P, 2 * T], U8)
         v2_sc = tile("v2_sc", [P, T2], U8)
         v3_sc = tile("v3_sc", [P, T3], U8)
-        w_sc_raw = tile("w_sc_raw", [P, 3 * H], U8)
         planes = tile("planes", [P, 3 * H + 4 * S], U8)
         bias_raw = tile("bias_raw", [4, PASS], F32)
         bo_raw = tile("bo_raw", [2, 3 * P], F32)
@@ -68,7 +67,7 @@ def tile_list_upgrade_offer_scores_kernel(
         nc.vector.memset(v3_sc[0:ROW0, :].bitcast(I32), 0)
         nc.gpsimd.memset(bias_rows[:], 0.0)
         make_identity(nc, ident[:])
-        nc.gpsimd.memset(w_sc_raw[0:ROW0, :].bitcast(I32), 0)
+        nc.gpsimd.memset(planes[0:ROW0, 0 : 3 * H].bitcast(I32), 0)
 
         nc.sync.dma_start(idx[:], offs)
         nc.sync.dma_start(
@@ -81,10 +80,10 @@ def tile_list_upgrade_offer_scores_kernel(
         nc.sync.dma_start(idx3[:], offs3)
         nc.sync.dma_start(v3_sc[ROW0:P, :].bitcast(I32), tab3_scales[0].bitcast(I32))
         nc.sync.dma_start(
-            w_sc_raw[ROW0:P, 0 : 2 * H].rearrange("q (a c) -> q a c", a=2).bitcast(I32),
+            planes[ROW0:P, 0 : 2 * H].rearrange("q (a c) -> q a c", a=2).bitcast(I32),
             wg_scales.rearrange("a q c -> q a c").bitcast(I32),
         )
-        nc.sync.dma_start(w_sc_raw[ROW0:P, 2 * H :].bitcast(I32), wa_scales[0].bitcast(I32))
+        nc.sync.dma_start(planes[ROW0:P, 2 * H : 3 * H].bitcast(I32), wa_scales[0].bitcast(I32))
         nc.sync.dma_start(bias_raw[0:2, :], br.rearrange("(a r) -> a r", a=2))
         nc.sync.dma_start(v2_words[:].bitcast(I32), tab2_words[0].rearrange("p t i -> p (t i)").bitcast(I32))
         nc.sync.dma_start(
@@ -127,16 +126,10 @@ def tile_list_upgrade_offer_scores_kernel(
         nc.vector.tensor_copy(got_sc[:, 2 * S : 3 * S], v2_sc[:].indirect(idx2[:]))
         nc.vector.tensor_copy(got_sc[:, 3 * S : 4 * S], v3_sc[:].indirect(idx3[:]))
         nc.vector.tensor_copy(planes[:, 3 * H :].bitcast(I32), got_sc[:].bitcast(I32))
-        nc.vector.tensor_copy(
-            planes[:, 0 : 3 * H].bitcast(I32).rearrange("p (h t u w) -> p h u t w", t=4, u=8, w=4),
-            w_sc_raw[:].bitcast(I32).rearrange("p (h u w t) -> p h u t w", t=4, u=8, w=4),
-        )
         for r in range(4):
             nc.sync.dma_start(planes[r:P:32, :].bitcast(I32), planes[ROW0 + r : P : 4, :].bitcast(I32))
-        v_words.append(tile("v_words1", [P, T], U32, tag="w_sc_raw"))
-        nc.sync.dma_start(v_words[1][:].bitcast(I32), tab_words[1].rearrange("p t i -> p (t i)").bitcast(I32))
-        wg_sc = [planes[:, a * H : (a + 1) * H] for a in range(2)]
-        wa_sc = planes[:, 2 * H : 3 * H]
+        wa_raw = tile("wa_raw", [P, 4 * H], U8, tag="got_sc")
+        nc.sync.dma_start(wa_raw[:].bitcast(I32), wa_words[0].rearrange("p c i -> p (c i)").bitcast(I32))
         g_sc = [planes[:, 3 * H + a * S : 3 * H + (a + 1) * S] for a in range(2)]
         g2_sc = planes[:, 3 * H + 2 * S : 3 * H + 3 * S]
         g3_sc = planes[:, 3 * H + 3 * S :]
@@ -145,12 +138,11 @@ def tile_list_upgrade_offer_scores_kernel(
         g2 = tile("g2", [P, S], U32)
         g3 = tile("g3", [P, S], U16)
         wg_p = tile("wg_p", [P, 4 * H], U8)
-        wa_p = tile("wa_p", [P, 4 * H], U8)
-        wr_q = [tile("wr_q%d" % a, [P, PASS], U32, tag=tag) for a, tag in enumerate(("got_sc", "wr_q1"))]
+        wr_q = [tile("wr_q%d" % a, [P, PASS], U32, tag=tag) for a, tag in enumerate(("wr_q0", "wr_q1"))]
         wr_s = [tile("wr_s%d" % a, [P, PASS], U8) for a in range(2)]
         nc.vector.tensor_copy(g2[:], v2_words[:].indirect(idx2[:]))
-        wa_raw = tile("wa_raw", [P, 4 * H], U8, tag="v2_words")
-        nc.sync.dma_start(wa_raw[:].bitcast(I32), wa_words[0].rearrange("p c i -> p (c i)").bitcast(I32))
+        v_words.append(tile("v_words1", [P, T], U32, tag="v2_words"))
+        nc.sync.dma_start(v_words[1][:].bitcast(I32), tab_words[1].rearrange("p t i -> p (t i)").bitcast(I32))
         quantize(wr_q[0][:], wr_s[0][:], wr_bf[0][:])
         wr_raw.append(tile("wr_raw1", [P, 4, PASS], F32, tag="wr_bf0"))
         nc.sync.dma_start(wr_raw[1][:], wr_rows[:, :, PASS:H])
@@ -172,12 +164,26 @@ def tile_list_upgrade_offer_scores_kernel(
                 raw[k, c] = (piece, c * P - c0)
 
         nc.vector.tensor_copy(g3[:], v3_words[:].indirect(idx3[:]))
+        w_sc = tile("w_sc", [P, 3 * H], U8, tag="v3_words")
+        nc.vector.tensor_copy(
+            w_sc[:].bitcast(I32).rearrange("p (h t u w) -> p h u t w", t=4, u=8, w=4),
+            planes[:, 0 : 3 * H].bitcast(I32).rearrange("p (h u w t) -> p h u t w", t=4, u=8, w=4),
+        )
+        wg_sc = [w_sc[:, a * H : (a + 1) * H] for a in range(2)]
+        wa_sc = w_sc[:, 2 * H : 3 * H]
+        wa_p = [tile("wa_p0", [P, 4 * PASS], U8)]
+
+        def deal_wa(a):
+            nc.vector.tensor_copy(
+                wa_p[a][:].bitcast(I32).rearrange("p (t q w) -> p t q w", t=4, w=4),
+                wa_raw[:, 4 * a * PASS : 4 * (a + 1) * PASS].bitcast(I32).rearrange("p (q t w) -> p t q w", t=4, w=4),
+            )
+
+        deal_wa(0)
         for u in range(2):
             nc.vector.tensor_copy(g[1][:, u * S // 2 : (u + 1) * S // 2], v_words[1][:].indirect(idx[:, u * 16 : (u + 1) * 16]))
-        nc.vector.tensor_copy(
-            wa_p[:].bitcast(I32).rearrange("p (h t q w) -> p h t q w", t=4, q=32, w=4),
-            wa_raw[:].bitcast(I32).rearrange("p (h q t w) -> p h t q w", t=4, q=32, w=4),
-        )
+        wa_p.append(tile("wa_p1", [P, 4 * PASS], U8, tag="v2_words"))
+        deal_wa(1)
 
         room = [tile("room%d" % a, [P, 4, S], F32) for a in range(2)]
         arrival = [tile("arrival%d" % a, [P, 4, S], F32) for a in range(2)]
@@ -194,13 +200,13 @@ def tile_list_upgrade_offer_scores_kernel(
             for t in range(4):
                 acc = bank("arrival_ps%d%d" % (a, t), 4 + t)
                 c0 = a * PASS + t * P
-                nc.tensor.matmul_mx(acc[:], wa_p[:, 4 * c0 : 4 * (c0 + P)].bitcast(FP8X4), wa_sc[:, c0 : c0 + P],
+                nc.tensor.matmul_mx(acc[:], wa_p[a][:, 4 * t * P : 4 * (t + 1) * P].bitcast(FP8X4), wa_sc[:, c0 : c0 + P],
                                     g3[:].bitcast(FP4X4), g3_sc, start=True, stop=True)
                 nc.scalar.activation(arrival[a][:, t, :], acc[:], IDENTITY, bias=bias[:, t, 2 + a : 3 + a])
 
-        def make_guest(a):
+        def make_guest(a, chunks):
             banks = []
-            for n in range(S // CHUNK):
+            for n in chunks:
                 acc = bank("guest_ps%d%d" % (a, n), n)
                 tok = slice(n * CHUNK, (n + 1) * CHUNK)
                 for t in range(4):
@@ -274,7 +280,7 @@ def tile_list_upgrade_offer_scores_kernel(
                                     start=(done[c] == 1), stop=(done[c] == 4))
 
         def finish(c, engine):
-            res = tile("res%d" % c, [P, S], F32, tag=("g0", "g1", "g2", "wr_q1", "wr_bf0", "got_sc")[c])
+            res = tile("res%d" % c, [P, S], F32, tag=("g0", "g1", "g2", "wr_q1", "wr_bf0", "wr_q0")[c])
             bo_c = bias_o[:, c % 3, c // 3 : c // 3 + 1]
             if engine == "vector":
                 nc.vector.tensor_scalar(res[:], acc[c][:], bo_c, None, ADD)
@@ -282,58 +288,58 @@ def tile_list_upgrade_offer_scores_kernel(
                 nc.scalar.activation(res[:], acc[c][:], IDENTITY, bias=bo_c)
             nc.sync.dma_start(out[c * P : (c + 1) * P, :], res[:])
 
-        new_group("w0a", [(0, 0), (0, 1)], "v_sc")
-        new_group("w1a", [(1, c) for c in range(4)], "wr_raw0")
-        new_group("w2a", [(2, c) for c in range(4)], "w_sc_raw")
+        new_group("w1a", [(1, c) for c in range(3)], "wr_raw0")
+        new_group("w0a", [(0, c) for c in range(3)], "v_sc")
+        new_group("w2a", [(2, c) for c in range(4)], "got_sc")
         new_group("w3a", [(3, c) for c in range(4)], "v2_words")
         new_group("last", [(2, 4), (2, 5), (3, 4), (3, 5)], "wg_raw")
         make_room(0)
-        guest = make_guest(0)
         make_arrival(0)
+        guest = make_guest(0, (0, 1))
         make_arrival(1)
+        guest = guest + make_guest(0, (2, 3))
         for t in range(4):
             nc.gpsimd.tensor_scalar(
                 wr_bf[1][:].rearrange("p (t q e j) -> p t q e j", t=4, e=4, j=4)[:, t],
                 wr_raw[1][:].rearrange("p j (q t e) -> p t q e j", t=4, e=4)[:, t],
                 1.0, 0.0, MULT, ADD,
             )
-        for i in range(2):
-            for n in range(4):
+        for n in range(4):
+            for i in range(2):
                 product(i, 0, n, guest[n])
         quantize(wr_q[1][:], wr_s[1][:], wr_bf[1][:])
-        cast_w("scalar", 0, 0, 2)
+        cast_w("scalar", 0, 0, 3)
         make_room(1)
-        guest = make_guest(1)
+        guest = make_guest(1, range(4))
         quantize_h(0, 0)
-        quantize_w("w0a")
         quantize_h(1, 0)
-        score(0, (0, 1))
-        new_group("w0b", [(0, c) for c in range(2, 6)], "h_bf10")
-        for c in range(2, 6):
+        new_group("w0b", [(0, c) for c in range(3, 6)], "h_bf10")
+        for c in range(3, 6):
             cast_w("pool", 0, c, c + 1)
-        new_group("w1b", [(1, 4), (1, 5)], "v3_words")
-        for c in range(4, 6):
-            cast_w("pool", 1, c, c + 1)
-        cast_w("scalar", 1, 0, 4)
-        cast_w("scalar", 2, 0, 4)
-        cast_w("scalar", 3, 0, 4)
+        cast_w("scalar", 1, 0, 3)
         for n in range(4):
             product(1, 1, n, guest[n])
-        for n in range(2):
-            product(0, 1, n, guest[n])
+        quantize_w("w0a")
+        score(0, range(3))
         quantize_w("w0b")
-        score(0, range(2, 6))
-        for n in range(2, 4):
+        score(0, range(3, 6))
+        new_group("w1b", [(1, c) for c in range(3, 6)], "h_bf10")
+        for c in range(3, 6):
+            cast_w("pool", 1, c, c + 1)
+        cast_w("scalar", 2, 0, 4)
+        cast_w("scalar", 3, 0, 2)
+        cast_w("scalar", 2, 4, 6)
+        for n in range(4):
             product(0, 1, n, guest[n])
         quantize_w("w1a")
-        score(1, range(4))
+        score(1, range(3))
         quantize_h(0, 1)
         quantize_w("w1b")
-        score(1, (4, 5))
+        score(1, range(3, 6))
         quantize_w("w2a")
         score(2, range(4))
         quantize_h(1, 1)
-        cast_w("vector", 2, 4, 6)
+        cast_w("vector", 3, 2, 4)
         cast_w("vector", 3, 4, 6)
         quantize_w("w3a")
         quantize_w("last")

@@ -288,8 +288,8 @@ def tile_list_upgrade_offer_scores_kernel(
                 nc.scalar.activation(res[:], acc[c][:], IDENTITY, bias=bo_c)
             nc.sync.dma_start(out[c * P : (c + 1) * P, :], res[:])
 
-        new_group("w1a", [(1, c) for c in range(3)], "wr_raw0")
-        new_group("w0a", [(0, c) for c in range(3)], "v_sc")
+        new_group("w1a", [(1, c) for c in range(4)], "wr_raw0")
+        new_group("w0a", [(0, c) for c in range(4)], "v_sc")
         new_group("w2a", [(2, c) for c in range(4)], "got_sc")
         new_group("w3a", [(3, c) for c in range(4)], "v2_words")
         new_group("last", [(2, 4), (2, 5), (3, 4), (3, 5)], "wg_raw")
@@ -307,24 +307,22 @@ def tile_list_upgrade_offer_scores_kernel(
         for n in range(4):
             for i in range(2):
                 product(i, 0, n, guest[n])
+        quantize_h(0, 0)
         quantize(wr_q[1][:], wr_s[1][:], wr_bf[1][:])
-        cast_w("scalar", 0, 0, 3)
+        cast_w("scalar", 0, 0, 4)
         make_room(1)
         guest = make_guest(1, range(4))
-        quantize_h(0, 0)
         quantize_h(1, 0)
-        new_group("w0b", [(0, c) for c in range(3, 6)], "h_bf10")
-        for c in range(3, 6):
+        new_group("w0b", [(0, 4), (0, 5)], "h_bf10")
+        for c in range(4, 6):
             cast_w("pool", 0, c, c + 1)
-        cast_w("scalar", 1, 0, 3)
+        cast_w("scalar", 1, 0, 4)
         for n in range(4):
             product(1, 1, n, guest[n])
         quantize_w("w0a")
-        score(0, range(3))
-        quantize_w("w0b")
-        score(0, range(3, 6))
-        new_group("w1b", [(1, c) for c in range(3, 6)], "h_bf10")
-        for c in range(3, 6):
+        score(0, range(4))
+        new_group("w1b", [(1, 4), (1, 5)], "v_sc")
+        for c in range(4, 6):
             cast_w("pool", 1, c, c + 1)
         cast_w("scalar", 2, 0, 4)
         cast_w("scalar", 3, 0, 2)
@@ -332,13 +330,15 @@ def tile_list_upgrade_offer_scores_kernel(
         for n in range(4):
             product(0, 1, n, guest[n])
         quantize_w("w1a")
-        score(1, range(3))
+        score(1, range(4))
         quantize_h(0, 1)
-        quantize_w("w1b")
-        score(1, range(3, 6))
+        quantize_w("w0b")
+        score(0, (4, 5))
         quantize_w("w2a")
         score(2, range(4))
         quantize_h(1, 1)
+        quantize_w("w1b")
+        score(1, (4, 5))
         cast_w("vector", 3, 2, 4)
         cast_w("vector", 3, 4, 6)
         quantize_w("w3a")

@@ -62,20 +62,20 @@ def tile_list_upgrade_offer_scores_kernel(
         v3_words = tile("v3_words", [P, T3], U16)
         wr_rows = wr.rearrange("(p j) r -> p j r", j=4)
 
-        nc.vector.memset(v_sc[0:ROW0, :].bitcast(I32), 0)
         nc.vector.memset(v2_sc[0:ROW0, :].bitcast(I32), 0)
+        nc.vector.memset(v_sc[0:ROW0, :].bitcast(I32), 0)
         nc.vector.memset(v3_sc[0:ROW0, :].bitcast(I32), 0)
         nc.gpsimd.memset(bias_rows[:], 0.0)
         make_identity(nc, ident[:])
         nc.gpsimd.memset(planes[0:ROW0, 0 : 3 * H].bitcast(I32), 0)
 
+        nc.sync.dma_start(idx2[:], offs2)
+        nc.sync.dma_start(v2_sc[ROW0:P, :].bitcast(I32), tab2_scales[0].bitcast(I32))
         nc.sync.dma_start(idx[:], offs)
         nc.sync.dma_start(
             v_sc[ROW0:P, :].rearrange("q (a t) -> q a t", a=2).bitcast(I32),
             tab_scales.rearrange("a q t -> q a t").bitcast(I32),
         )
-        nc.sync.dma_start(idx2[:], offs2)
-        nc.sync.dma_start(v2_sc[ROW0:P, :].bitcast(I32), tab2_scales[0].bitcast(I32))
         nc.sync.dma_start(wr_raw[0][:], wr_rows[:, :, 0:PASS])
         nc.sync.dma_start(idx3[:], offs3)
         nc.sync.dma_start(v3_sc[ROW0:P, :].bitcast(I32), tab3_scales[0].bitcast(I32))
@@ -121,15 +121,16 @@ def tile_list_upgrade_offer_scores_kernel(
         nc.scalar.activation(bias_o[:], bo_ps[:, 0 : 3 * P].rearrange("p (c h) -> p c h", c=3)[:, :, 0:2], IDENTITY)
 
         got_sc = tile("got_sc", [P, 4 * S], U8)
+        nc.vector.tensor_copy(got_sc[:, 2 * S : 3 * S], v2_sc[:].indirect(idx2[:]))
         for a in range(2):
             nc.vector.tensor_copy(got_sc[:, a * S : (a + 1) * S], v_sc[:, a * T : (a + 1) * T].indirect(idx[:]))
-        nc.vector.tensor_copy(got_sc[:, 2 * S : 3 * S], v2_sc[:].indirect(idx2[:]))
         nc.vector.tensor_copy(got_sc[:, 3 * S : 4 * S], v3_sc[:].indirect(idx3[:]))
         nc.vector.tensor_copy(planes[:, 3 * H :].bitcast(I32), got_sc[:].bitcast(I32))
         for r in range(4):
             nc.sync.dma_start(planes[r:P:32, :].bitcast(I32), planes[ROW0 + r : P : 4, :].bitcast(I32))
-        wa_raw = tile("wa_raw", [P, 4 * H], U8, tag="got_sc")
-        nc.sync.dma_start(wa_raw[:].bitcast(I32), wa_words[0].rearrange("p c i -> p (c i)").bitcast(I32))
+        wa_rows = wa_words[0].rearrange("p c i -> p (c i)")
+        wa_raw = [tile("wa_raw0", [P, 4 * PASS], U8, tag="got_sc")]
+        nc.sync.dma_start(wa_raw[0][:].bitcast(I32), wa_rows[:, 0 : 4 * PASS].bitcast(I32))
         g_sc = [planes[:, 3 * H + a * S : 3 * H + (a + 1) * S] for a in range(2)]
         g2_sc = planes[:, 3 * H + 2 * S : 3 * H + 3 * S]
         g3_sc = planes[:, 3 * H + 3 * S :]
@@ -144,12 +145,14 @@ def tile_list_upgrade_offer_scores_kernel(
         v_words.append(tile("v_words1", [P, T], U32, tag="v2_words"))
         nc.sync.dma_start(v_words[1][:].bitcast(I32), tab_words[1].rearrange("p t i -> p (t i)").bitcast(I32))
         quantize(wr_q[0][:], wr_s[0][:], wr_bf[0][:])
-        wr_raw.append(tile("wr_raw1", [P, 4, PASS], F32, tag="wr_bf0"))
-        nc.sync.dma_start(wr_raw[1][:], wr_rows[:, :, PASS:H])
+        wa_raw.append(tile("wa_raw1", [P, 4 * PASS], U8, tag="wr_bf0"))
+        nc.sync.dma_start(wa_raw[1][:].bitcast(I32), wa_rows[:, 4 * PASS :].bitcast(I32))
         nc.vector.tensor_copy(
             wg_p[:].bitcast(I32).rearrange("p (h t q w) -> p h t q w", t=4, q=32, w=2),
             wg_raw[:].bitcast(I32).rearrange("p (h q t w) -> p h t q w", t=4, q=32, w=2),
         )
+        wr_raw.append(tile("wr_raw1", [P, 4, PASS], F32, tag="wg_raw"))
+        nc.sync.dma_start(wr_raw[1][:], wr_rows[:, :, PASS:H])
         nc.vector.tensor_copy(g[0][:], v_words[0][:].indirect(idx[:]))
         w_raw = tile("w_raw", [P, 16 * N], F32, tag="v_words0")
         raw = {}
@@ -176,7 +179,7 @@ def tile_list_upgrade_offer_scores_kernel(
         def deal_wa(a):
             nc.vector.tensor_copy(
                 wa_p[a][:].bitcast(I32).rearrange("p (t q w) -> p t q w", t=4, w=4),
-                wa_raw[:, 4 * a * PASS : 4 * (a + 1) * PASS].bitcast(I32).rearrange("p (q t w) -> p t q w", t=4, w=4),
+                wa_raw[a][:].bitcast(I32).rearrange("p (q t w) -> p t q w", t=4, w=4),
             )
 
         deal_wa(0)
@@ -291,22 +294,31 @@ def tile_list_upgrade_offer_scores_kernel(
         new_group("w1a", [(1, c) for c in range(4)], "wr_raw0")
         new_group("w0a", [(0, c) for c in range(4)], "v_sc")
         new_group("w2a", [(2, c) for c in range(4)], "got_sc")
-        new_group("w3a", [(3, c) for c in range(4)], "v2_words")
-        new_group("last", [(2, 4), (2, 5), (3, 4), (3, 5)], "wg_raw")
+        new_group("w3a", [(3, 0), (3, 1)], "v2_words")
+        new_group("w3b", [(3, 2), (3, 3)], "v2_sc")
+        new_group("w2b", [(2, 4), (2, 5)], "wg_raw")
+        new_group("w3c", [(3, 4), (3, 5)], "v3_sc")
         make_room(0)
         make_arrival(0)
         guest = make_guest(0, (0, 1))
         make_arrival(1)
         guest = guest + make_guest(0, (2, 3))
-        for t in range(4):
+        for t in range(3):
             nc.gpsimd.tensor_scalar(
                 wr_bf[1][:].rearrange("p (t q e j) -> p t q e j", t=4, e=4, j=4)[:, t],
                 wr_raw[1][:].rearrange("p j (q t e) -> p t q e j", t=4, e=4)[:, t],
                 1.0, 0.0, MULT, ADD,
             )
-        for n in range(4):
+        for i in range(2):
+            for n in range(2):
+                product(i, 0, n, guest[n])
+        for n in range(2, 4):
             for i in range(2):
                 product(i, 0, n, guest[n])
+        nc.scalar.copy(
+            wr_bf[1][:].rearrange("p (t q e j) -> p t q j e", t=4, e=4, j=4)[:, 3],
+            wr_raw[1][:].rearrange("p j (q t e) -> p t q j e", t=4, e=4)[:, 3],
+        )
         quantize_h(0, 0)
         quantize(wr_q[1][:], wr_s[1][:], wr_bf[1][:])
         cast_w("scalar", 0, 0, 4)
@@ -332,21 +344,26 @@ def tile_list_upgrade_offer_scores_kernel(
         quantize_w("w1a")
         score(1, range(4))
         quantize_h(0, 1)
-        quantize_w("w0b")
-        score(0, (4, 5))
         quantize_w("w2a")
         score(2, range(4))
         quantize_h(1, 1)
-        quantize_w("w1b")
-        score(1, (4, 5))
         cast_w("vector", 3, 2, 4)
-        cast_w("vector", 3, 4, 6)
         quantize_w("w3a")
-        quantize_w("last")
-        for c in range(4):
+        for c in range(2):
             score(3, (c,))
             finish(c, "scalar")
+        quantize_w("w3b")
+        for c in range(2, 4):
+            score(3, (c,))
+            finish(c, "scalar")
+        quantize_w("w0b")
+        score(0, (4, 5))
+        cast_w("vector", 3, 4, 6)
+        quantize_w("w1b")
+        score(1, (4, 5))
+        quantize_w("w2b")
+        score(2, (4, 5))
+        quantize_w("w3c")
         for c in (4, 5):
-            score(2, (c,))
             score(3, (c,))
             finish(c, ("vector", "scalar")[c % 2])

@@ -62,28 +62,28 @@ def tile_list_upgrade_offer_scores_kernel(
         v3_words = tile("v3_words", [P, T3], U16)
         wr_rows = wr.rearrange("(p j) r -> p j r", j=4)
 
-        nc.vector.memset(v2_sc[0:ROW0, :].bitcast(I32), 0)
-        nc.vector.memset(v_sc[0:ROW0, :].bitcast(I32), 0)
-        nc.vector.memset(v3_sc[0:ROW0, :].bitcast(I32), 0)
+        nc.gpsimd.memset(v2_sc[:].bitcast(I32), 0)
+        nc.gpsimd.memset(v3_sc[:].bitcast(I32), 0)
+        nc.vector.memset(v_sc[:].bitcast(I32), 0)
+        nc.vector.memset(planes[:, 0 : 3 * H].bitcast(I32), 0)
         nc.gpsimd.memset(bias_rows[:], 0.0)
         make_identity(nc, ident[:])
-        nc.gpsimd.memset(planes[0:ROW0, 0 : 3 * H].bitcast(I32), 0)
 
         nc.sync.dma_start(idx2[:], offs2)
-        nc.sync.dma_start(v2_sc[ROW0:P, :].bitcast(I32), tab2_scales[0].bitcast(I32))
+        nc.sync.dma_start(idx3[:], offs3)
+        nc.sync.dma_start(v2_sc[0:P:8, :].bitcast(I32), tab2_scales[0].bitcast(I32))
         nc.sync.dma_start(idx[:], offs)
+        nc.sync.dma_start(v3_sc[0:P:8, :].bitcast(I32), tab3_scales[0].bitcast(I32))
+        nc.sync.dma_start(wr_raw[0][:], wr_rows[:, :, 0:PASS])
         nc.sync.dma_start(
-            v_sc[ROW0:P, :].rearrange("q (a t) -> q a t", a=2).bitcast(I32),
+            v_sc[0:P:8, :].rearrange("q (a t) -> q a t", a=2).bitcast(I32),
             tab_scales.rearrange("a q t -> q a t").bitcast(I32),
         )
-        nc.sync.dma_start(wr_raw[0][:], wr_rows[:, :, 0:PASS])
-        nc.sync.dma_start(idx3[:], offs3)
-        nc.sync.dma_start(v3_sc[ROW0:P, :].bitcast(I32), tab3_scales[0].bitcast(I32))
         nc.sync.dma_start(
-            planes[ROW0:P, 0 : 2 * H].rearrange("q (a c) -> q a c", a=2).bitcast(I32),
+            planes[0:P:8, 0 : 2 * H].rearrange("q (a c) -> q a c", a=2).bitcast(I32),
             wg_scales.rearrange("a q c -> q a c").bitcast(I32),
         )
-        nc.sync.dma_start(planes[ROW0:P, 2 * H : 3 * H].bitcast(I32), wa_scales[0].bitcast(I32))
+        nc.sync.dma_start(planes[0:P:8, 2 * H : 3 * H].bitcast(I32), wa_scales[0].bitcast(I32))
         nc.sync.dma_start(bias_raw[0:2, :], br.rearrange("(a r) -> a r", a=2))
         nc.sync.dma_start(v2_words[:].bitcast(I32), tab2_words[0].rearrange("p t i -> p (t i)").bitcast(I32))
         nc.sync.dma_start(
@@ -122,12 +122,12 @@ def tile_list_upgrade_offer_scores_kernel(
 
         got_sc = tile("got_sc", [P, 4 * S], U8)
         nc.vector.tensor_copy(got_sc[:, 2 * S : 3 * S], v2_sc[:].indirect(idx2[:]))
+        nc.vector.tensor_copy(got_sc[:, 3 * S : 4 * S], v3_sc[:].indirect(idx3[:]))
         for a in range(2):
             nc.vector.tensor_copy(got_sc[:, a * S : (a + 1) * S], v_sc[:, a * T : (a + 1) * T].indirect(idx[:]))
-        nc.vector.tensor_copy(got_sc[:, 3 * S : 4 * S], v3_sc[:].indirect(idx3[:]))
         nc.vector.tensor_copy(planes[:, 3 * H :].bitcast(I32), got_sc[:].bitcast(I32))
-        for r in range(4):
-            nc.sync.dma_start(planes[r:P:32, :].bitcast(I32), planes[ROW0 + r : P : 4, :].bitcast(I32))
+        for r in range(1, 4):
+            nc.sync.dma_start(planes[r:P:32, :].bitcast(I32), planes[8 * r : P : 32, :].bitcast(I32))
         wa_rows = wa_words[0].rearrange("p c i -> p (c i)")
         wa_raw = [tile("wa_raw0", [P, 4 * PASS], U8, tag="got_sc")]
         nc.sync.dma_start(wa_raw[0][:].bitcast(I32), wa_rows[:, 0 : 4 * PASS].bitcast(I32))

@@ -33,6 +33,8 @@ def tile_list_upgrade_offer_scores_kernel(
     with ExitStack() as ctx:
         lists = ctx.enter_context(tc.tile_pool(name="lists", bufs=1))
         sb = ctx.enter_context(tc.tile_pool(name="sb", bufs=1))
+        shared = ctx.enter_context(tc.tile_pool(name="shared", bufs=1))
+        late = ctx.enter_context(tc.tile_pool(name="late", bufs=1))
         ps = ctx.enter_context(tc.psum_pool(name="ps", bufs=1))
 
         def tile(name, shape, dtype, tag=None):
@@ -62,7 +64,6 @@ def tile_list_upgrade_offer_scores_kernel(
         v3_words = tile("v3_words", [P, T3], U16)
         wr_rows = wr.rearrange("(p j) r -> p j r", j=4)
 
-        nc.gpsimd.memset(v2_sc[:].bitcast(I32), 0)
         nc.gpsimd.memset(v3_sc[:].bitcast(I32), 0)
         nc.vector.memset(v_sc[:].bitcast(I32), 0)
         nc.vector.memset(planes[:, 0 : 3 * H].bitcast(I32), 0)
@@ -70,8 +71,8 @@ def tile_list_upgrade_offer_scores_kernel(
         make_identity(nc, ident[:])
 
         nc.sync.dma_start(idx2[:], offs2)
+        nc.sync.dma_start(v2_sc[:].bitcast(I32), tab2_scales[0].bitcast(I32).unsqueeze(1).to_broadcast([16, 8, T2 // 4]))
         nc.sync.dma_start(idx3[:], offs3)
-        nc.sync.dma_start(v2_sc[0:P:8, :].bitcast(I32), tab2_scales[0].bitcast(I32))
         nc.sync.dma_start(idx[:], offs)
         nc.sync.dma_start(v3_sc[0:P:8, :].bitcast(I32), tab3_scales[0].bitcast(I32))
         nc.sync.dma_start(wr_raw[0][:], wr_rows[:, :, 0:PASS])
@@ -120,7 +121,7 @@ def tile_list_upgrade_offer_scores_kernel(
         bias_o = tile("bias_o", [P, 3, 2], F32)
         nc.scalar.activation(bias_o[:], bo_ps[:, 0 : 3 * P].rearrange("p (c h) -> p c h", c=3)[:, :, 0:2], IDENTITY)
 
-        got_sc = tile("got_sc", [P, 4 * S], U8)
+        got_sc = shared.tile([P, 4 * S], U8, name="got_sc", align_bytes=64, offset=2 * S)
         nc.vector.tensor_copy(got_sc[:, 2 * S : 3 * S], v2_sc[:].indirect(idx2[:]))
         nc.vector.tensor_copy(got_sc[:, 3 * S : 4 * S], v3_sc[:].indirect(idx3[:]))
         for a in range(2):
@@ -129,8 +130,10 @@ def tile_list_upgrade_offer_scores_kernel(
         for r in range(1, 4):
             nc.sync.dma_start(planes[r:P:32, :].bitcast(I32), planes[8 * r : P : 32, :].bitcast(I32))
         wa_rows = wa_words[0].rearrange("p c i -> p (c i)")
-        wa_raw = [tile("wa_raw0", [P, 4 * PASS], U8, tag="got_sc")]
+        wa_raw = [shared.tile([P, 4 * PASS], U8, name="wa_raw0", align_bytes=64, offset=0)]
         nc.sync.dma_start(wa_raw[0][:].bitcast(I32), wa_rows[:, 0 : 4 * PASS].bitcast(I32))
+        v_words.append(shared.tile([P, T], U32, name="v_words1", align_bytes=64, offset=4 * PASS))
+        nc.sync.dma_start(v_words[1][:].bitcast(I32), tab_words[1].rearrange("p t i -> p (t i)").bitcast(I32))
         g_sc = [planes[:, 3 * H + a * S : 3 * H + (a + 1) * S] for a in range(2)]
         g2_sc = planes[:, 3 * H + 2 * S : 3 * H + 3 * S]
         g3_sc = planes[:, 3 * H + 3 * S :]
@@ -142,10 +145,8 @@ def tile_list_upgrade_offer_scores_kernel(
         wr_q = [tile("wr_q%d" % a, [P, PASS], U32, tag=tag) for a, tag in enumerate(("wr_q0", "wr_q1"))]
         wr_s = [tile("wr_s%d" % a, [P, PASS], U8) for a in range(2)]
         nc.vector.tensor_copy(g2[:], v2_words[:].indirect(idx2[:]))
-        v_words.append(tile("v_words1", [P, T], U32, tag="v2_words"))
-        nc.sync.dma_start(v_words[1][:].bitcast(I32), tab_words[1].rearrange("p t i -> p (t i)").bitcast(I32))
         quantize(wr_q[0][:], wr_s[0][:], wr_bf[0][:])
-        wa_raw.append(tile("wa_raw1", [P, 4 * PASS], U8, tag="wr_bf0"))
+        wa_raw.append(tile("wa_raw1", [P, 4 * PASS], U8, tag="v2_words"))
         nc.sync.dma_start(wa_raw[1][:].bitcast(I32), wa_rows[:, 4 * PASS :].bitcast(I32))
         nc.vector.tensor_copy(
             wg_p[:].bitcast(I32).rearrange("p (h t q w) -> p h t q w", t=4, q=32, w=2),
@@ -185,7 +186,7 @@ def tile_list_upgrade_offer_scores_kernel(
         deal_wa(0)
         for u in range(2):
             nc.vector.tensor_copy(g[1][:, u * S // 2 : (u + 1) * S // 2], v_words[1][:].indirect(idx[:, u * 16 : (u + 1) * 16]))
-        wa_p.append(tile("wa_p1", [P, 4 * PASS], U8, tag="v2_words"))
+        wa_p.append(shared.tile([P, 4 * PASS], U8, name="wa_p1", align_bytes=64, offset=4 * PASS))
         deal_wa(1)
 
         room = [tile("room%d" % a, [P, 4, S], F32) for a in range(2)]
@@ -239,13 +240,17 @@ def tile_list_upgrade_offer_scores_kernel(
         groups = {}
         place = {}
 
-        def new_group(name, tiles, tag):
+        def new_group(name, tiles, tag=None, values_at=None, scales_at=None):
             width = P * len(tiles)
-            groups[name] = (
-                tile(name + "_bf", [P, 4 * width], BF16, tag=tag),
-                tile(name + "_q", [P, width], U32),
-                tile(name + "_s", [P, width], U8),
-            )
+            if values_at is None:
+                values = tile(name + "_bf", [P, 4 * width], BF16, tag=tag)
+            else:
+                values = late.tile([P, 4 * width], BF16, name=name + "_bf", align_bytes=64, offset=values_at)
+            if scales_at is None:
+                scales = tile(name + "_s", [P, width], U8)
+            else:
+                scales = late.tile([P, width], U8, name=name + "_s", align_bytes=64, offset=scales_at)
+            groups[name] = (values, tile(name + "_q", [P, width], U32), scales)
             for j, kc in enumerate(tiles):
                 place[kc] = (name, j * P)
 
@@ -261,9 +266,10 @@ def tile_list_upgrade_offer_scores_kernel(
                 copy = nc.scalar.copy if engine == "scalar" else nc.vector.tensor_copy
                 copy(dst.rearrange("p (c i t) -> p c t i", t=4, i=4), src.rearrange("p t (c i) -> p c t i", i=4))
 
-        def quantize_w(name):
+        def quantize_w(name, j0=0, j1=None):
             values, codes, scales = groups[name]
-            quantize(codes[:], scales[:], values[:])
+            c0, c1 = j0 * P, codes.shape[1] if j1 is None else j1 * P
+            quantize(codes[:, c0:c1], scales[:, c0:c1], values[:, 4 * c0 : 4 * c1])
 
         def quantize_h(i, a):
             quantize(h_q[i][a][:], h_s[i][a][:], h_bf[i][a][:])
@@ -293,11 +299,9 @@ def tile_list_upgrade_offer_scores_kernel(
 
         new_group("w1a", [(1, c) for c in range(4)], "wr_raw0")
         new_group("w0a", [(0, c) for c in range(4)], "v_sc")
-        new_group("w2a", [(2, c) for c in range(4)], "got_sc")
-        new_group("w3a", [(3, 0), (3, 1)], "v2_words")
-        new_group("w3b", [(3, 2), (3, 3)], "v2_sc")
-        new_group("w2b", [(2, 4), (2, 5)], "wg_raw")
-        new_group("w3c", [(3, 4), (3, 5)], "v3_sc")
+        new_group("w2a", [(2, c) for c in range(4)])
+        new_group("w3a", [(3, 0), (3, 1)], values_at=4096)
+        new_group("w3b", [(3, 2), (3, 3)], "v2_words")
         make_room(0)
         make_arrival(0)
         guest = make_guest(0, (0, 1))
@@ -338,32 +342,33 @@ def tile_list_upgrade_offer_scores_kernel(
             cast_w("pool", 1, c, c + 1)
         cast_w("scalar", 2, 0, 4)
         cast_w("scalar", 3, 0, 2)
-        cast_w("scalar", 2, 4, 6)
+        cast_w("scalar", 3, 2, 4)
         for n in range(4):
             product(0, 1, n, guest[n])
         quantize_w("w1a")
         score(1, range(4))
         quantize_h(0, 1)
+        quantize_w("w0b")
         quantize_w("w2a")
         score(2, range(4))
         quantize_h(1, 1)
-        cast_w("vector", 3, 2, 4)
-        quantize_w("w3a")
-        for c in range(2):
-            score(3, (c,))
-            finish(c, "scalar")
-        quantize_w("w3b")
-        for c in range(2, 4):
-            score(3, (c,))
-            finish(c, "scalar")
-        quantize_w("w0b")
-        score(0, (4, 5))
-        cast_w("vector", 3, 4, 6)
         quantize_w("w1b")
+        quantize_w("w3a")
+        for c in (0, 1):
+            score(3, (c,))
+            finish(c, "scalar")
+        score(0, (4, 5))
         score(1, (4, 5))
-        quantize_w("w2b")
+        new_group("last", [(2, 4), (2, 5), (3, 4), (3, 5)], values_at=64)
+        cast_w("vector", 2, 4, 6)
+        quantize_w("w3b")
+        for c in (2, 3):
+            score(3, (c,))
+            finish(c, "scalar")
+        cast_w("vector", 3, 4, 6)
+        quantize_w("last", 0, 2)
         score(2, (4, 5))
-        quantize_w("w3c")
+        quantize_w("last", 2, 4)
         for c in (4, 5):
             score(3, (c,))
             finish(c, ("vector", "scalar")[c % 2])

@@ -263,8 +263,8 @@ def tile_list_upgrade_offer_scores_kernel(
             if engine == "pool":
                 nc.gpsimd.tensor_scalar(dst.rearrange("p (n t) -> p n t", t=4), src.rearrange("p t n -> p n t"), 1.0, 0.0, MULT, ADD)
             else:
-                copy = nc.scalar.copy if engine == "scalar" else nc.vector.tensor_copy
-                copy(dst.rearrange("p (c i t) -> p c t i", t=4, i=4), src.rearrange("p t (c i) -> p c t i", i=4))
+                copy, run = (nc.scalar.copy, 2) if engine == "scalar" else (nc.vector.tensor_copy, 4)
+                copy(dst.rearrange("p (c i t) -> p c t i", t=4, i=run), src.rearrange("p t (c i) -> p c t i", i=run))
 
         def quantize_w(name, j0=0, j1=None):
             values, codes, scales = groups[name]

@@ -158,7 +158,7 @@ def tile_list_upgrade_offer_scores_kernel(
         w_raw = tile("w_raw", [P, 16 * N], F32, tag="v_words0")
         raw = {}
         at = 0
-        for k, c0, c1 in ((0, 0, N), (1, 0, N), (2, 0, N), (3, 0, PASS), (3, PASS, N)):
+        for k, c0, c1 in ((0, 0, N), (1, 0, N), (2, 0, PASS), (3, 0, PASS), (2, PASS, N), (3, PASS, N)):
             piece = w_raw[:, at : at + 4 * (c1 - c0)].rearrange("p (t n) -> p t n", t=4)
             at = at + 4 * (c1 - c0)
             rows = (w1, w2)[k % 2][k // 2 * PASS : (k // 2 + 1) * PASS, c0:c1].rearrange("(q t e) n -> t q e n", t=4, e=4)

@@ -34,7 +34,6 @@ def tile_list_upgrade_offer_scores_kernel(
         lists = ctx.enter_context(tc.tile_pool(name="lists", bufs=1))
         sb = ctx.enter_context(tc.tile_pool(name="sb", bufs=1))
         shared = ctx.enter_context(tc.tile_pool(name="shared", bufs=1))
-        late = ctx.enter_context(tc.tile_pool(name="late", bufs=1))
         ps = ctx.enter_context(tc.psum_pool(name="ps", bufs=1))
 
         def tile(name, shape, dtype, tag=None):
@@ -240,17 +239,13 @@ def tile_list_upgrade_offer_scores_kernel(
         groups = {}
         place = {}
 
-        def new_group(name, tiles, tag=None, values_at=None, scales_at=None):
+        def new_group(name, tiles, tag=None):
             width = P * len(tiles)
-            if values_at is None:
-                values = tile(name + "_bf", [P, 4 * width], BF16, tag=tag)
-            else:
-                values = late.tile([P, 4 * width], BF16, name=name + "_bf", align_bytes=64, offset=values_at)
-            if scales_at is None:
-                scales = tile(name + "_s", [P, width], U8)
-            else:
-                scales = late.tile([P, width], U8, name=name + "_s", align_bytes=64, offset=scales_at)
-            groups[name] = (values, tile(name + "_q", [P, width], U32), scales)
+            groups[name] = (
+                tile(name + "_bf", [P, 4 * width], BF16, tag=tag),
+                tile(name + "_q", [P, width], U32),
+                tile(name + "_s", [P, width], U8),
+            )
             for j, kc in enumerate(tiles):
                 place[kc] = (name, j * P)
 
@@ -300,7 +295,7 @@ def tile_list_upgrade_offer_scores_kernel(
         new_group("w1a", [(1, c) for c in range(4)], "wr_raw0")
         new_group("w0a", [(0, c) for c in range(4)], "v_sc")
         new_group("w2a", [(2, c) for c in range(4)])
-        new_group("w3a", [(3, 0), (3, 1)], values_at=4096)
+        new_group("w3a", [(3, 0), (3, 1)])
         new_group("w3b", [(3, 2), (3, 3)], "v2_words")
         make_room(0)
         make_arrival(0)
@@ -342,7 +337,7 @@ def tile_list_upgrade_offer_scores_kernel(
             cast_w("pool", 1, c, c + 1)
         cast_w("scalar", 2, 0, 4)
         cast_w("scalar", 3, 0, 2)
-        cast_w("scalar", 3, 2, 4)
+        cast_w("scalar", 3, 2, 3)
         for n in range(4):
             product(0, 1, n, guest[n])
         quantize_w("w1a")
@@ -352,6 +347,7 @@ def tile_list_upgrade_offer_scores_kernel(
         quantize_w("w2a")
         score(2, range(4))
         quantize_h(1, 1)
+        cast_w("vector", 3, 3, 4)
         quantize_w("w1b")
         quantize_w("w3a")
         for c in (0, 1):
@@ -359,7 +355,7 @@ def tile_list_upgrade_offer_scores_kernel(
             finish(c, "scalar")
         score(0, (4, 5))
         score(1, (4, 5))
-        new_group("last", [(2, 4), (2, 5), (3, 4), (3, 5)], values_at=64)
+        new_group("last", [(2, 4), (2, 5), (3, 4), (3, 5)])
         cast_w("vector", 2, 4, 6)
         quantize_w("w3b")
         for c in (2, 3):

@@ -21,8 +21,6 @@ IDENTITY = mybir.ActivationFunctionType.Identity
 P = 128
 PASS = 512
 CHUNK = 128
-ROW0 = 112
-PAIR = 256
 
 
 def tile_list_upgrade_offer_scores_kernel(
@@ -34,6 +32,7 @@ def tile_list_upgrade_offer_scores_kernel(
         lists = ctx.enter_context(tc.tile_pool(name="lists", bufs=1))
         sb = ctx.enter_context(tc.tile_pool(name="sb", bufs=1))
         shared = ctx.enter_context(tc.tile_pool(name="shared", bufs=1))
+        late = ctx.enter_context(tc.tile_pool(name="late", bufs=1))
         ps = ctx.enter_context(tc.psum_pool(name="ps", bufs=1))
 
         def tile(name, shape, dtype, tag=None):
@@ -57,9 +56,12 @@ def tile_list_upgrade_offer_scores_kernel(
         bias_rows = tile("bias_rows", [P, 7 * P], F32)
         ident = tile("ident", [P, P], F32)
         wr_raw = [tile("wr_raw0", [P, 4, PASS], F32)]
-        v_words = [tile("v_words0", [P, T], U32)]
+        v_words = [late.tile([P, T + PASS], U32, name="v_words0", align_bytes=64, offset=64 * N - 4 * T)[:, 0:T]]
         v2_words = tile("v2_words", [P, T2], U32)
-        wg_raw = tile("wg_raw", [P, 4 * H], U8)
+        wg_raw = [tile("wg_raw0", [P, 2, PASS // 2], U32)]
+        wa_raw = [tile("wa_raw0", [P, 4 * PASS], U8)]
+        wg_rows = wg_words.bitcast(I32).rearrange("a p (h c) -> h p a c", h=2)
+        wa_rows = wa_words[0].rearrange("p c i -> p (c i)")
         v3_words = tile("v3_words", [P, T3], U16)
         wr_rows = wr.rearrange("(p j) r -> p j r", j=4)
 
@@ -86,13 +88,12 @@ def tile_list_upgrade_offer_scores_kernel(
         nc.sync.dma_start(planes[0:P:8, 2 * H : 3 * H].bitcast(I32), wa_scales[0].bitcast(I32))
         nc.sync.dma_start(bias_raw[0:2, :], br.rearrange("(a r) -> a r", a=2))
         nc.sync.dma_start(v2_words[:].bitcast(I32), tab2_words[0].rearrange("p t i -> p (t i)").bitcast(I32))
-        nc.sync.dma_start(
-            wg_raw[:].rearrange("p (a c) -> p a c", a=2).bitcast(I32), wg_words.rearrange("a p c -> p a c").bitcast(I32)
-        )
+        nc.sync.dma_start(wg_raw[0][:].bitcast(I32), wg_rows[0])
         nc.sync.dma_start(bias_raw[2:4, :], ba.rearrange("(a r) -> a r", a=2))
         nc.sync.dma_start(bo_raw[:], bo.rearrange("(h n) -> h n", h=2))
-        nc.sync.dma_start(v_words[0][:].bitcast(I32), tab_words[0].rearrange("p t i -> p (t i)").bitcast(I32))
+        nc.sync.dma_start(v_words[0].bitcast(I32), tab_words[0].rearrange("p t i -> p (t i)").bitcast(I32))
         nc.sync.dma_start(v3_words[:].bitcast(I32), tab3_words[0].bitcast(I32))
+        nc.sync.dma_start(wa_raw[0][:].bitcast(I32), wa_rows[:, 0 : 4 * PASS].bitcast(I32))
 
         wr_bf = [tile("wr_bf%d" % a, [P, 4 * PASS], BF16) for a in range(2)]
 
@@ -128,9 +129,6 @@ def tile_list_upgrade_offer_scores_kernel(
         nc.vector.tensor_copy(planes[:, 3 * H :].bitcast(I32), got_sc[:].bitcast(I32))
         for r in range(1, 4):
             nc.sync.dma_start(planes[r:P:32, :].bitcast(I32), planes[8 * r : P : 32, :].bitcast(I32))
-        wa_rows = wa_words[0].rearrange("p c i -> p (c i)")
-        wa_raw = [shared.tile([P, 4 * PASS], U8, name="wa_raw0", align_bytes=64, offset=0)]
-        nc.sync.dma_start(wa_raw[0][:].bitcast(I32), wa_rows[:, 0 : 4 * PASS].bitcast(I32))
         v_words.append(shared.tile([P, T], U32, name="v_words1", align_bytes=64, offset=4 * PASS))
         nc.sync.dma_start(v_words[1][:].bitcast(I32), tab_words[1].rearrange("p t i -> p (t i)").bitcast(I32))
         g_sc = [planes[:, 3 * H + a * S : 3 * H + (a + 1) * S] for a in range(2)]
@@ -140,21 +138,27 @@ def tile_list_upgrade_offer_scores_kernel(
         g = [tile("g%d" % a, [P, S], U32) for a in range(2)]
         g2 = tile("g2", [P, S], U32)
         g3 = tile("g3", [P, S], U16)
-        wg_p = tile("wg_p", [P, 4 * H], U8)
-        wr_q = [tile("wr_q%d" % a, [P, PASS], U32, tag=tag) for a, tag in enumerate(("wr_q0", "wr_q1"))]
+        wg_p = [tile("wg_p0", [P, PASS], U32)]
+        wr_q = [tile("wr_q0", [P, PASS], U32)]
         wr_s = [tile("wr_s%d" % a, [P, PASS], U8) for a in range(2)]
         nc.vector.tensor_copy(g2[:], v2_words[:].indirect(idx2[:]))
         quantize(wr_q[0][:], wr_s[0][:], wr_bf[0][:])
         wa_raw.append(tile("wa_raw1", [P, 4 * PASS], U8, tag="v2_words"))
         nc.sync.dma_start(wa_raw[1][:].bitcast(I32), wa_rows[:, 4 * PASS :].bitcast(I32))
-        nc.vector.tensor_copy(
-            wg_p[:].bitcast(I32).rearrange("p (h t q w) -> p h t q w", t=4, q=32, w=2),
-            wg_raw[:].bitcast(I32).rearrange("p (h q t w) -> p h t q w", t=4, q=32, w=2),
-        )
-        wr_raw.append(tile("wr_raw1", [P, 4, PASS], F32, tag="wg_raw"))
+        wg_raw.append(tile("wg_raw1", [P, 2, PASS // 2], U32, tag="wr_bf0"))
+        nc.sync.dma_start(wg_raw[1][:].bitcast(I32), wg_rows[1])
+
+        def deal_wg(copy, dtype, a):
+            copy(
+                wg_p[a][:].bitcast(dtype).rearrange("p (k t q w) -> p k t q w", t=4, q=32, w=2),
+                wg_raw[a][:].bitcast(dtype).rearrange("p k (q t w) -> p k t q w", t=4, w=2),
+            )
+
+        deal_wg(nc.vector.tensor_copy, I32, 0)
+        wr_raw.append(tile("wr_raw1", [P, 4, PASS], F32, tag="wg_raw0"))
         nc.sync.dma_start(wr_raw[1][:], wr_rows[:, :, PASS:H])
-        nc.vector.tensor_copy(g[0][:], v_words[0][:].indirect(idx[:]))
-        w_raw = tile("w_raw", [P, 16 * N], F32, tag="v_words0")
+        nc.vector.tensor_copy(g[0][:], v_words[0].indirect(idx[:]))
+        w_raw = late.tile([P, 16 * N], F32, name="w_raw", align_bytes=64, offset=0)
         raw = {}
         at = 0
         for k, c0, c1 in ((0, 0, N), (1, 0, N), (2, 0, PASS), (3, 0, PASS), (2, PASS, N), (3, PASS, N)):
@@ -174,7 +178,7 @@ def tile_list_upgrade_offer_scores_kernel(
         )
         wg_sc = [w_sc[:, a * H : (a + 1) * H] for a in range(2)]
         wa_sc = w_sc[:, 2 * H : 3 * H]
-        wa_p = [tile("wa_p0", [P, 4 * PASS], U8)]
+        wa_p = [late.tile([P, 4 * PASS], U8, name="wa_p0", align_bytes=64, offset=64 * N)]
 
         def deal_wa(a):
             nc.vector.tensor_copy(
@@ -187,6 +191,8 @@ def tile_list_upgrade_offer_scores_kernel(
             nc.vector.tensor_copy(g[1][:, u * S // 2 : (u + 1) * S // 2], v_words[1][:].indirect(idx[:, u * 16 : (u + 1) * 16]))
         wa_p.append(shared.tile([P, 4 * PASS], U8, name="wa_p1", align_bytes=64, offset=4 * PASS))
         deal_wa(1)
+        wg_p.append(shared.tile([P, PASS], U32, name="wg_p1", align_bytes=64, offset=8 * PASS))
+        deal_wg(nc.vector.tensor_copy, I32, 1)
 
         room = [tile("room%d" % a, [P, 4, S], F32) for a in range(2)]
         arrival = [tile("arrival%d" % a, [P, 4, S], F32) for a in range(2)]
@@ -217,7 +223,7 @@ def tile_list_upgrade_offer_scores_kernel(
                     for k in range(2):
                         nc.tensor.matmul_mx(
                             acc[:, t * CHUNK : (t + 1) * CHUNK],
-                            wg_p[:, 2 * (k * H + c0) : 2 * (k * H + c0 + P)].bitcast(FP4X4), wg_sc[k][:, c0 : c0 + P],
+                            wg_p[a][:].bitcast(U8)[:, 2 * (k * PASS + t * P) : 2 * (k * PASS + (t + 1) * P)].bitcast(FP4X4), wg_sc[k][:, c0 : c0 + P],
                             g[k][:, tok].bitcast(FP8X4), g_sc[k][:, tok], start=(k == 0), stop=(k == 1),
                         )
                 banks.append(acc)
@@ -284,7 +290,7 @@ def tile_list_upgrade_offer_scores_kernel(
                                     start=(done[c] == 1), stop=(done[c] == 4))
 
         def finish(c, engine):
-            res = tile("res%d" % c, [P, S], F32, tag=("g0", "g1", "g2", "wr_q1", "wr_bf0", "wr_q0")[c])
+            res = tile("res%d" % c, [P, S], F32, tag=("g0", "g1", "g2", "h_bf00", "wr_bf0", "wr_q0")[c])
             bo_c = bias_o[:, c % 3, c // 3 : c // 3 + 1]
             if engine == "vector":
                 nc.vector.tensor_scalar(res[:], acc[c][:], bo_c, None, ADD)
@@ -319,12 +325,13 @@ def tile_list_upgrade_offer_scores_kernel(
             wr_raw[1][:].rearrange("p j (q t e) -> p t q j e", t=4, e=4)[:, 3],
         )
         quantize_h(0, 0)
+        quantize_h(1, 0)
+        wr_q.append(tile("wr_q1", [P, PASS], U32, tag="h_bf00"))
         quantize(wr_q[1][:], wr_s[1][:], wr_bf[1][:])
         cast_w("scalar", 0, 0, 4)
         make_room(1)
         guest = make_guest(1, range(4))
-        quantize_h(1, 0)
-        new_group("w0b", [(0, 4), (0, 5)], "h_bf10")
+        new_group("w0b", [(0, 4), (0, 5)], "wr_bf1")
         for c in range(4, 6):
             cast_w("pool", 0, c, c + 1)
         cast_w("scalar", 1, 0, 4)

@@ -52,8 +52,8 @@ def tile_list_upgrade_offer_scores_kernel(
         v3_sc = tile("v3_sc", [P, T3], U8)
         planes = tile("planes", [P, 3 * H + 4 * S], U8)
         bias_raw = tile("bias_raw", [4, PASS], F32)
-        bo_raw = tile("bo_raw", [2, 3 * P], F32)
-        bias_rows = tile("bias_rows", [P, 7 * P], F32)
+        bo_raw = tile("bo_raw", [34, 3 * P], F32)
+        bias_rows = tile("bias_rows", [P, PASS], F32)
         ident = tile("ident", [P, P], F32)
         wr_raw = [tile("wr_raw0", [P, 4, PASS], F32)]
         v_words = [late.tile([P, T + PASS], U32, name="v_words0", align_bytes=64, offset=64 * N - 4 * T)[:, 0:T]]
@@ -90,7 +90,7 @@ def tile_list_upgrade_offer_scores_kernel(
         nc.sync.dma_start(v2_words[:].bitcast(I32), tab2_words[0].rearrange("p t i -> p (t i)").bitcast(I32))
         nc.sync.dma_start(wg_raw[0][:].bitcast(I32), wg_rows[0])
         nc.sync.dma_start(bias_raw[2:4, :], ba.rearrange("(a r) -> a r", a=2))
-        nc.sync.dma_start(bo_raw[:], bo.rearrange("(h n) -> h n", h=2))
+        nc.sync.dma_start(bo_raw[32:34, :], bo.rearrange("(h n) -> h n", h=2))
         nc.sync.dma_start(v_words[0].bitcast(I32), tab_words[0].rearrange("p t i -> p (t i)").bitcast(I32))
         nc.sync.dma_start(v3_words[:].bitcast(I32), tab3_words[0].bitcast(I32))
         nc.sync.dma_start(wa_raw[0][:].bitcast(I32), wa_rows[:, 0 : 4 * PASS].bitcast(I32))
@@ -106,20 +106,15 @@ def tile_list_upgrade_offer_scores_kernel(
         cast_wr(nc.scalar.copy, 0)
 
         nc.scalar.copy(
-            bias_rows[0:4, 0:PASS].rearrange("a (t q e) -> a t q e", t=4, e=4),
+            bias_rows[0:4, :].rearrange("a (t q e) -> a t q e", t=4, e=4),
             bias_raw[:].rearrange("a (q t e) -> a t q e", t=4, e=4),
         )
+        nc.scalar.copy(bias_rows[32:34, 0 : 3 * P], bo_raw[32:34, :])
         bias_ps = bank("bias_ps", 2)
         for t in range(4):
             nc.tensor.transpose(bias_ps[:, t * P : (t + 1) * P], bias_rows[:, t * P : (t + 1) * P], ident[:])
-        bias = tile("bias", [P, 4, 4], F32)
-        nc.scalar.activation(bias[:], bias_ps[:].rearrange("p (t c) -> p t c", t=4)[:, :, 0:4], IDENTITY)
-        nc.scalar.copy(bias_rows[0:2, PASS:], bo_raw[:])
-        bo_ps = bank("bo_ps", 3)
-        for c in range(3):
-            nc.tensor.transpose(bo_ps[:, c * P : (c + 1) * P], bias_rows[:, PASS + c * P : PASS + (c + 1) * P], ident[:])
-        bias_o = tile("bias_o", [P, 3, 2], F32)
-        nc.scalar.activation(bias_o[:], bo_ps[:, 0 : 3 * P].rearrange("p (c h) -> p c h", c=3)[:, :, 0:2], IDENTITY)
+        bias = tile("bias", [P, 4, 34], F32)
+        nc.scalar.activation(bias[:], bias_ps[:].rearrange("p (t c) -> p t c", t=4)[:, :, 0:34], IDENTITY)
 
         got_sc = shared.tile([P, 4 * S], U8, name="got_sc", align_bytes=64, offset=2 * S)
         nc.vector.tensor_copy(got_sc[:, 2 * S : 3 * S], v2_sc[:].indirect(idx2[:]))
@@ -291,7 +286,7 @@ def tile_list_upgrade_offer_scores_kernel(
 
         def finish(c, engine):
             res = tile("res%d" % c, [P, S], F32, tag=("g0", "g1", "g2", "h_bf00", "wr_bf0", "wr_q0")[c])
-            bo_c = bias_o[:, c % 3, c // 3 : c // 3 + 1]
+            bo_c = bias[:, c % 3, 32 + c // 3 : 33 + c // 3]
             if engine == "vector":
                 nc.vector.tensor_scalar(res[:], acc[c][:], bo_c, None, ADD)
             else:

@@ -138,6 +138,10 @@ def tile_list_upgrade_offer_scores_kernel(
         wr_s = [tile("wr_s%d" % a, [P, PASS], U8) for a in range(2)]
         nc.vector.tensor_copy(g2[:], v2_words[:].indirect(idx2[:]))
         quantize(wr_q[0][:], wr_s[0][:], wr_bf[0][:])
+        warm = bank("warm_ps", 0)
+        for t in range(4):
+            nc.tensor.matmul_mx(warm[:], wr_q[0][:, t * P : (t + 1) * P].bitcast(FP8X4), wr_s[0][:, t * P : (t + 1) * P],
+                                wr_q[0][:].bitcast(FP8X4), wr_s[0][:], start=True, stop=True)
         wa_raw.append(tile("wa_raw1", [P, 4 * PASS], U8, tag="v2_words"))
         nc.sync.dma_start(wa_raw[1][:].bitcast(I32), wa_rows[:, 4 * PASS :].bitcast(I32))
         wg_raw.append(tile("wg_raw1", [P, 2, PASS // 2], U32, tag="wr_bf0"))

@@ -17,6 +17,7 @@ FP4X4 = mybir.dt.float4_e2m1fn_x4
 MULT = mybir.AluOpType.mult
 ADD = mybir.AluOpType.add
 IDENTITY = mybir.ActivationFunctionType.Identity
+COPY = mybir.ActivationFunctionType.Copy
 
 P = 128
 PASS = 512
@@ -31,12 +32,14 @@ def tile_list_upgrade_offer_scores_kernel(
     with ExitStack() as ctx:
         lists = ctx.enter_context(tc.tile_pool(name="lists", bufs=1))
         sb = ctx.enter_context(tc.tile_pool(name="sb", bufs=1))
-        shared = ctx.enter_context(tc.tile_pool(name="shared", bufs=1))
         late = ctx.enter_context(tc.tile_pool(name="late", bufs=1))
         ps = ctx.enter_context(tc.psum_pool(name="ps", bufs=1))
 
         def tile(name, shape, dtype, tag=None):
             return sb.tile(shape, dtype, name=name, tag=tag or name, align_bytes=64)
+
+        def placed(name, shape, dtype, offset):
+            return late.tile(shape, dtype, name=name, align_bytes=64, offset=offset)
 
         def bank(name, b):
             return ps.tile([P, PASS], F32, name=name, tag="bank%d" % b)
@@ -44,66 +47,63 @@ def tile_list_upgrade_offer_scores_kernel(
         def quantize(codes, scales, values):
             nc.vector.quantize_mx(out=codes.bitcast(FP8X4), scales=scales, in_=values)
 
+        def load(dst, src):
+            nc.sync.dma_start(dst.bitcast(I32), src.bitcast(I32))
+
+        at_wa = 0
+        at_tab = (4 * H, 4 * H + 4 * T)
+        at_wg1 = at_tab[1] + 4 * T
+        at_wr1 = at_wg1 + 4 * PASS
+        at_narrow = at_wr1 + 16 * PASS
+        at_w = at_narrow + 16 * PASS
+        at_wr0 = at_w + 32 * N + 32 * PASS
+        at_room0 = at_wr0 + 14 * PASS
+        at_planes = at_room0 + 16 * S
+        at_w1a = at_planes + 8 * PASS
+        at_h11 = at_w1a + 8 * PASS
+
         idx = lists.tile([P, S // 16], U16, name="idx")
         idx2 = lists.tile([P, S // 16], U16, name="idx2")
         idx3 = lists.tile([P, S // 16], U16, name="idx3")
-        v_sc = tile("v_sc", [P, 2 * T], U8)
+        v_sc = placed("v_sc", [P, T + 128], U8, at_wg1 - 64)[:, 0:T]
         v2_sc = tile("v2_sc", [P, T2], U8)
         v3_sc = tile("v3_sc", [P, T3], U8)
-        planes = tile("planes", [P, 3 * H + 4 * S], U8)
+        planes = placed("planes", [P, 3 * H + 2 * S], U8, at_planes)
+        g_planes = tile("g_planes", [P, 2 * S], U8)
         bias_raw = tile("bias_raw", [4, PASS], F32)
-        bo_raw = tile("bo_raw", [34, 3 * P], F32)
+        bo_raw = placed("bo_raw", [34, 3 * P], F32, at_wr0 + 2 * PASS)
         bias_rows = tile("bias_rows", [P, PASS], F32)
         ident = tile("ident", [P, P], F32)
-        wr_raw = [tile("wr_raw0", [P, 4, PASS], F32)]
-        v_words = [late.tile([P, T + PASS], U32, name="v_words0", align_bytes=64, offset=64 * N - 4 * T)[:, 0:T]]
+        wr_raw = [placed("wr_raw0", [P, 4, PASS], F32, at_narrow + 4 * PASS)]
         v2_words = tile("v2_words", [P, T2], U32)
+        v3_words = tile("v3_words", [P, T3], U16)
         wg_raw = [tile("wg_raw0", [P, 2, PASS // 2], U32)]
-        wa_raw = [tile("wa_raw0", [P, 4 * PASS], U8)]
         wg_rows = wg_words.bitcast(I32).rearrange("a p (h c) -> h p a c", h=2)
         wa_rows = wa_words[0].rearrange("p c i -> p (c i)")
-        v3_words = tile("v3_words", [P, T3], U16)
         wr_rows = wr.rearrange("(p j) r -> p j r", j=4)
 
         nc.gpsimd.memset(v3_sc[:].bitcast(I32), 0)
-        nc.vector.memset(v_sc[:].bitcast(I32), 0)
         nc.vector.memset(planes[:, 0 : 3 * H].bitcast(I32), 0)
-        nc.gpsimd.memset(bias_rows[:], 0.0)
+        nc.vector.memset(v_sc.bitcast(I32), 0)
+        nc.vector.memset(g_planes[:].bitcast(I32), 0)
         make_identity(nc, ident[:])
+        nc.scalar.activation(bias_rows[:], ident[:, 0:1].to_broadcast([P, PASS]), COPY, scale=0.0)
 
         nc.sync.dma_start(idx2[:], offs2)
         nc.sync.dma_start(v2_sc[:].bitcast(I32), tab2_scales[0].bitcast(I32).unsqueeze(1).to_broadcast([16, 8, T2 // 4]))
         nc.sync.dma_start(idx3[:], offs3)
-        nc.sync.dma_start(idx[:], offs)
-        nc.sync.dma_start(v3_sc[0:P:8, :].bitcast(I32), tab3_scales[0].bitcast(I32))
-        nc.sync.dma_start(wr_raw[0][:], wr_rows[:, :, 0:PASS])
-        nc.sync.dma_start(
-            v_sc[0:P:8, :].rearrange("q (a t) -> q a t", a=2).bitcast(I32),
-            tab_scales.rearrange("a q t -> q a t").bitcast(I32),
-        )
-        nc.sync.dma_start(
-            planes[0:P:8, 0 : 2 * H].rearrange("q (a c) -> q a c", a=2).bitcast(I32),
-            wg_scales.rearrange("a q c -> q a c").bitcast(I32),
-        )
-        nc.sync.dma_start(planes[0:P:8, 2 * H : 3 * H].bitcast(I32), wa_scales[0].bitcast(I32))
+        load(v3_sc[0:P:8, :], tab3_scales[0])
         nc.sync.dma_start(bias_raw[0:2, :], br.rearrange("(a r) -> a r", a=2))
-        nc.sync.dma_start(v2_words[:].bitcast(I32), tab2_words[0].rearrange("p t i -> p (t i)").bitcast(I32))
-        nc.sync.dma_start(wg_raw[0][:].bitcast(I32), wg_rows[0])
         nc.sync.dma_start(bias_raw[2:4, :], ba.rearrange("(a r) -> a r", a=2))
         nc.sync.dma_start(bo_raw[32:34, :], bo.rearrange("(h n) -> h n", h=2))
-        nc.sync.dma_start(v_words[0].bitcast(I32), tab_words[0].rearrange("p t i -> p (t i)").bitcast(I32))
-        nc.sync.dma_start(v3_words[:].bitcast(I32), tab3_words[0].bitcast(I32))
-        nc.sync.dma_start(wa_raw[0][:].bitcast(I32), wa_rows[:, 0 : 4 * PASS].bitcast(I32))
-
-        wr_bf = [tile("wr_bf%d" % a, [P, 4 * PASS], BF16) for a in range(2)]
-
-        def cast_wr(copy, a):
-            copy(
-                wr_bf[a][:].rearrange("p (t q e j) -> p t q j e", t=4, e=4, j=4),
-                wr_raw[a][:].rearrange("p j (q t e) -> p t q j e", t=4, e=4),
-            )
-
-        cast_wr(nc.scalar.copy, 0)
+        nc.sync.dma_start(wr_raw[0][:], wr_rows[:, :, 0:PASS])
+        load(planes[0:P:8, 2 * H : 3 * H], wa_scales[0])
+        load(planes[0:P:8, 0 : 2 * H].rearrange("q (a c) -> q a c", a=2), wg_scales.rearrange("a q c -> q a c"))
+        nc.sync.dma_start(idx[:], offs)
+        load(v_sc[0:P:4, :], tab_scales.rearrange("a q t -> q a t"))
+        load(v2_words[:], tab2_words[0].rearrange("p t i -> p (t i)"))
+        load(v3_words[:], tab3_words[0])
+        nc.sync.dma_start(wg_raw[0][:].bitcast(I32), wg_rows[0])
 
         nc.scalar.copy(
             bias_rows[0:4, :].rearrange("a (t q e) -> a t q e", t=4, e=4),
@@ -116,126 +116,128 @@ def tile_list_upgrade_offer_scores_kernel(
         bias = tile("bias", [P, 4, 34], F32)
         nc.scalar.activation(bias[:], bias_ps[:].rearrange("p (t c) -> p t c", t=4)[:, :, 0:34], IDENTITY)
 
-        got_sc = shared.tile([P, 4 * S], U8, name="got_sc", align_bytes=64, offset=2 * S)
-        nc.vector.tensor_copy(got_sc[:, 2 * S : 3 * S], v2_sc[:].indirect(idx2[:]))
-        nc.vector.tensor_copy(got_sc[:, 3 * S : 4 * S], v3_sc[:].indirect(idx3[:]))
-        for a in range(2):
-            nc.vector.tensor_copy(got_sc[:, a * S : (a + 1) * S], v_sc[:, a * T : (a + 1) * T].indirect(idx[:]))
-        nc.vector.tensor_copy(planes[:, 3 * H :].bitcast(I32), got_sc[:].bitcast(I32))
-        for r in range(1, 4):
-            nc.sync.dma_start(planes[r:P:32, :].bitcast(I32), planes[8 * r : P : 32, :].bitcast(I32))
-        v_words.append(shared.tile([P, T], U32, name="v_words1", align_bytes=64, offset=4 * PASS))
-        nc.sync.dma_start(v_words[1][:].bitcast(I32), tab_words[1].rearrange("p t i -> p (t i)").bitcast(I32))
-        g_sc = [planes[:, 3 * H + a * S : 3 * H + (a + 1) * S] for a in range(2)]
-        g2_sc = planes[:, 3 * H + 2 * S : 3 * H + 3 * S]
-        g3_sc = planes[:, 3 * H + 3 * S :]
-
-        g = [tile("g%d" % a, [P, S], U32) for a in range(2)]
-        g2 = tile("g2", [P, S], U32)
-        g3 = tile("g3", [P, S], U16)
-        wg_p = [tile("wg_p0", [P, PASS], U32)]
-        wr_q = [tile("wr_q0", [P, PASS], U32)]
-        wr_s = [tile("wr_s%d" % a, [P, PASS], U8) for a in range(2)]
-        nc.vector.tensor_copy(g2[:], v2_words[:].indirect(idx2[:]))
-        quantize(wr_q[0][:], wr_s[0][:], wr_bf[0][:])
-        warm = bank("warm_ps", 0)
-        for t in range(4):
-            nc.tensor.matmul_mx(warm[:], wr_q[0][:, t * P : (t + 1) * P].bitcast(FP8X4), wr_s[0][:, t * P : (t + 1) * P],
-                                wr_q[0][:].bitcast(FP8X4), wr_s[0][:], start=True, stop=True)
-        wa_raw.append(tile("wa_raw1", [P, 4 * PASS], U8, tag="v2_words"))
-        nc.sync.dma_start(wa_raw[1][:].bitcast(I32), wa_rows[:, 4 * PASS :].bitcast(I32))
-        wg_raw.append(tile("wg_raw1", [P, 2, PASS // 2], U32, tag="wr_bf0"))
-        nc.sync.dma_start(wg_raw[1][:].bitcast(I32), wg_rows[1])
-
-        def deal_wg(copy, dtype, a):
-            copy(
-                wg_p[a][:].bitcast(dtype).rearrange("p (k t q w) -> p k t q w", t=4, q=32, w=2),
-                wg_raw[a][:].bitcast(dtype).rearrange("p k (q t w) -> p k t q w", t=4, w=2),
+        def cast_wr(dst, src, t0, t1):
+            nc.scalar.copy(
+                dst.rearrange("p (t q e j) -> p t q j e", q=32, e=4, j=4),
+                src.rearrange("p j (q t e) -> p t q j e", t=4, e=4)[:, t0:t1],
             )
 
-        deal_wg(nc.vector.tensor_copy, I32, 0)
-        wr_raw.append(tile("wr_raw1", [P, 4, PASS], F32, tag="wg_raw0"))
+        wr_bf0 = placed("wr_bf0", [P, 4 * PASS], BF16, at_wr0 + 2 * PASS)
+        cast_wr(wr_bf0[:], wr_raw[0][:], 0, 4)
+
+        got = placed("got", [P, 2 * S], U8, at_tab[0] - S)
+        nc.vector.tensor_copy(got[:, 0:S], v2_sc[:].indirect(idx2[:]))
+        nc.vector.tensor_copy(got[:, S : 2 * S], v3_sc[:].indirect(idx3[:]))
+        nc.vector.tensor_copy(planes[:, 3 * H :].bitcast(I32), got[:].bitcast(I32))
+        for r in range(1, 4):
+            load(planes[r:P:32, :], planes[8 * r : P : 32, :])
+        wa_raw = placed("wa_raw", [P, H], U32, at_wa)
+        load(wa_raw[:], wa_rows)
+        v_words = [placed("v_words0", [P, T], U32, at_tab[0])]
+        load(v_words[0][:], tab_words[0].rearrange("p t i -> p (t i)"))
+        got_v = tile("got_v", [P, S], U8)
+        nc.vector.tensor_copy(got_v[:], v_sc.indirect(idx[:]))
+        v_words.append(placed("v_words1", [P, T], U32, at_tab[1]))
+        load(v_words[1][:], tab_words[1].rearrange("p t i -> p (t i)"))
+        for q in (0, 2, 1, 3):
+            load(g_planes[32 * q : 32 * q + 4, :], got_v[32 * q : 32 * q + 32 : 4, :])
+        g_sc = [g_planes[:, a * S : (a + 1) * S] for a in range(2)]
+        g2_sc = planes[:, 3 * H : 3 * H + S]
+        g3_sc = planes[:, 3 * H + S :]
+
+        wr_raw.append(placed("wr_raw1", [P, 4, PASS], F32, at_wr1))
         nc.sync.dma_start(wr_raw[1][:], wr_rows[:, :, PASS:H])
-        nc.vector.tensor_copy(g[0][:], v_words[0].indirect(idx[:]))
-        w_raw = late.tile([P, 16 * N], F32, name="w_raw", align_bytes=64, offset=0)
+        wg_raw.append(placed("wg_raw1", [P, 2, PASS // 2], U32, at_wg1))
+        nc.sync.dma_start(wg_raw[1][:].bitcast(I32), wg_rows[1])
+        w_raw = placed("w_raw", [P, 8 * N + 8 * PASS], F32, at_w)
         raw = {}
         at = 0
-        for k, c0, c1 in ((0, 0, N), (1, 0, N), (2, 0, PASS), (3, 0, PASS), (2, PASS, N), (3, PASS, N)):
-            piece = w_raw[:, at : at + 4 * (c1 - c0)].rearrange("p (t n) -> p t n", t=4)
-            at = at + 4 * (c1 - c0)
+        for k, c0, c1 in ((0, 0, N), (1, 0, N), (3, 0, PASS), (2, 0, PASS), (3, PASS, N), (2, PASS, N)):
+            if c0 == 0:
+                piece = w_raw[:, at : at + 4 * c1].rearrange("p (t n) -> p t n", t=4)
+                at = at + 4 * c1
+            else:
+                piece = placed("narrow%d" % k, [P, 4, c1 - c0], F32, at_narrow + 8 * PASS * (k - 2))
             rows = (w1, w2)[k % 2][k // 2 * PASS : (k // 2 + 1) * PASS, c0:c1].rearrange("(q t e) n -> t q e n", t=4, e=4)
             for t in range(4):
                 nc.sync.dma_start(piece[:, t, :], rows[t])
             for c in range(c0 // P, c1 // P):
                 raw[k, c] = (piece, c * P - c0)
 
+        g = [tile("g%d" % a, [P, S], U32) for a in range(2)]
+        g2 = tile("g2", [P, S], U32)
+        wr_q0 = tile("wr_q0", [P, PASS], U32)
+        wr_s0 = tile("wr_s0", [P, PASS], U8)
+        nc.vector.tensor_copy(g2[:], v2_words[:].indirect(idx2[:]))
+        quantize(wr_q0[:], wr_s0[:], wr_bf0[:])
+        g3 = placed("g3", [P, S], U16, at_wr0 + 4 * PASS)
         nc.vector.tensor_copy(g3[:], v3_words[:].indirect(idx3[:]))
-        w_sc = tile("w_sc", [P, 3 * H], U8, tag="v3_words")
+        w_sc = tile("w_sc", [P, 3 * H], U8)
         nc.vector.tensor_copy(
             w_sc[:].bitcast(I32).rearrange("p (h t u w) -> p h u t w", t=4, u=8, w=4),
             planes[:, 0 : 3 * H].bitcast(I32).rearrange("p (h u w t) -> p h u t w", t=4, u=8, w=4),
         )
         wg_sc = [w_sc[:, a * H : (a + 1) * H] for a in range(2)]
         wa_sc = w_sc[:, 2 * H : 3 * H]
-        wa_p = [late.tile([P, 4 * PASS], U8, name="wa_p0", align_bytes=64, offset=64 * N)]
+        wa_p = placed("wa_p", [P, H], U32, at_wr0 + 6 * PASS)
+        wg_p = [placed("wg_p0", [P, PASS], U32, at_wr0), placed("wg_p1", [P, PASS], U32, at_room0 + 12 * PASS)]
+        nc.vector.tensor_copy(
+            wa_p[:].bitcast(I32).rearrange("p (a t q w) -> p a t q w", a=2, t=4, w=4),
+            wa_raw[:].bitcast(I32).rearrange("p (a q t w) -> p a t q w", a=2, t=4, w=4),
+        )
 
-        def deal_wa(a):
+        def deal_wg(a):
             nc.vector.tensor_copy(
-                wa_p[a][:].bitcast(I32).rearrange("p (t q w) -> p t q w", t=4, w=4),
-                wa_raw[a][:].bitcast(I32).rearrange("p (q t w) -> p t q w", t=4, w=4),
+                wg_p[a][:].bitcast(I32).rearrange("p (k t q w) -> p k t q w", t=4, q=32, w=2),
+                wg_raw[a][:].bitcast(I32).rearrange("p k (q t w) -> p k t q w", t=4, w=2),
             )
 
-        deal_wa(0)
-        for u in range(2):
-            nc.vector.tensor_copy(g[1][:, u * S // 2 : (u + 1) * S // 2], v_words[1][:].indirect(idx[:, u * 16 : (u + 1) * 16]))
-        wa_p.append(shared.tile([P, 4 * PASS], U8, name="wa_p1", align_bytes=64, offset=4 * PASS))
-        deal_wa(1)
-        wg_p.append(shared.tile([P, PASS], U32, name="wg_p1", align_bytes=64, offset=8 * PASS))
-        deal_wg(nc.vector.tensor_copy, I32, 1)
+        deal_wg(0)
+        nc.vector.tensor_copy(g[0][:], v_words[0][:].indirect(idx[:]))
+        for j0, j1 in ((0, CHUNK), (CHUNK, 2 * CHUNK), (2 * CHUNK, S)):
+            nc.vector.tensor_copy(g[1][:, j0:j1], v_words[1][:].indirect(idx[:, j0 // 16 : j1 // 16]))
 
-        room = [tile("room%d" % a, [P, 4, S], F32) for a in range(2)]
+        room = [placed("room0", [P, 4, S], F32, at_room0), tile("room1", [P, 4, S], F32)]
         arrival = [tile("arrival%d" % a, [P, 4, S], F32) for a in range(2)]
 
-        def make_room(a):
-            for t in range(4):
-                acc = bank("room_ps%d%d" % (a, t), 4 + t)
-                cols = slice(t * P, (t + 1) * P)
-                nc.tensor.matmul_mx(acc[:], wr_q[a][:, cols].bitcast(FP8X4), wr_s[a][:, cols], g2[:].bitcast(FP8X4), g2_sc,
-                                    start=True, stop=True)
-                nc.scalar.activation(room[a][:, t, :], acc[:], IDENTITY, bias=bias[:, t, a : a + 1])
+        def make_room(a, t, codes, scales):
+            acc = bank("room_ps%d%d" % (a, t), 4 + t)
+            nc.tensor.matmul_mx(acc[:], codes.bitcast(FP8X4), scales, g2[:].bitcast(FP8X4), g2_sc, start=True, stop=True)
+            nc.scalar.activation(room[a][:, t, :], acc[:], IDENTITY, bias=bias[:, t, a : a + 1])
 
         def make_arrival(a):
             for t in range(4):
                 acc = bank("arrival_ps%d%d" % (a, t), 4 + t)
                 c0 = a * PASS + t * P
-                nc.tensor.matmul_mx(acc[:], wa_p[a][:, 4 * t * P : 4 * (t + 1) * P].bitcast(FP8X4), wa_sc[:, c0 : c0 + P],
+                nc.tensor.matmul_mx(acc[:], wa_p[:, c0 : c0 + P].bitcast(FP8X4), wa_sc[:, c0 : c0 + P],
                                     g3[:].bitcast(FP4X4), g3_sc, start=True, stop=True)
                 nc.scalar.activation(arrival[a][:, t, :], acc[:], IDENTITY, bias=bias[:, t, 2 + a : 3 + a])
 
-        def make_guest(a, chunks):
-            banks = []
-            for n in chunks:
-                acc = bank("guest_ps%d%d" % (a, n), n)
-                tok = slice(n * CHUNK, (n + 1) * CHUNK)
-                for t in range(4):
-                    c0 = a * PASS + t * P
-                    for k in range(2):
-                        nc.tensor.matmul_mx(
-                            acc[:, t * CHUNK : (t + 1) * CHUNK],
-                            wg_p[a][:].bitcast(U8)[:, 2 * (k * PASS + t * P) : 2 * (k * PASS + (t + 1) * P)].bitcast(FP4X4), wg_sc[k][:, c0 : c0 + P],
-                            g[k][:, tok].bitcast(FP8X4), g_sc[k][:, tok], start=(k == 0), stop=(k == 1),
-                        )
-                banks.append(acc)
+        def guest_pass(a, k, n, acc):
+            tok = slice(n * CHUNK, (n + 1) * CHUNK)
+            for t in range(4):
+                c0 = a * PASS + t * P
+                nc.tensor.matmul_mx(
+                    acc[:, t * CHUNK : (t + 1) * CHUNK],
+                    wg_p[a][:].bitcast(U8)[:, 2 * (k * PASS + t * P) : 2 * (k * PASS + (t + 1) * P)].bitcast(FP4X4), wg_sc[k][:, c0 : c0 + P],
+                    g[k][:, tok].bitcast(FP8X4), g_sc[k][:, tok], start=(k == 0 and t == 0), stop=(k == 1 and t == 3),
+                )
+
+        def make_guest(a):
+            banks = [bank("guest_ps%d%d" % (a, n), n) for n in range(4)]
+            order = [(k, n) for k in range(2) for n in range(4)] if a == 0 else [(k, n) for n in range(4) for k in range(2)]
+            for k, n in order:
+                guest_pass(a, k, n, banks[n])
             return banks
 
-        h_bf = [[tile("h_bf%d%d" % (i, a), [P, 4 * S], BF16) for a in range(2)] for i in range(2)]
-        h_q = [[tile("h_q%d%d" % (i, a), [P, S], U32) for a in range(2)] for i in range(2)]
+        h_bf = {}
+        h_q = {}
         h_s = [[tile("h_s%d%d" % (i, a), [P, S], U8) for a in range(2)] for i in range(2)]
 
         def product(i, a, n, guest):
             other = (room, arrival)[i][a]
             nc.vector.tensor_tensor(
-                h_bf[i][a][:, 4 * n * CHUNK : 4 * (n + 1) * CHUNK].rearrange("p (c i t) -> p c t i", t=4, i=2),
+                h_bf[i, a][:, 4 * n * CHUNK : 4 * (n + 1) * CHUNK].rearrange("p (c i t) -> p c t i", t=4, i=2),
                 guest[:].rearrange("p (t c i) -> p c t i", t=4, i=2),
                 other[:, :, n * CHUNK : (n + 1) * CHUNK].rearrange("p t (c i) -> p c t i", i=2),
                 MULT,
@@ -244,35 +246,27 @@ def tile_list_upgrade_offer_scores_kernel(
         groups = {}
         place = {}
 
-        def new_group(name, tiles, tag=None):
-            width = P * len(tiles)
-            groups[name] = (
-                tile(name + "_bf", [P, 4 * width], BF16, tag=tag),
-                tile(name + "_q", [P, width], U32),
-                tile(name + "_s", [P, width], U8),
-            )
-            for j, kc in enumerate(tiles):
-                place[kc] = (name, j * P)
-
-        def cast_w(engine, k, c0, c1):
-            piece, r0 = raw[k, c0]
-            name, b0 = place[k, c0]
+        def cast_w(engine, k, c0, c1, values):
             width = P * (c1 - c0)
+            name = "w%d%d" % (k, c0)
+            groups[k, c0] = (values, tile(name + "_q", [P, width], U32), tile(name + "_s", [P, width], U8))
+            for c in range(c0, c1):
+                place[k, c] = (c0, (c - c0) * P)
+            piece, r0 = raw[k, c0]
             src = piece[:, :, r0 : r0 + width]
-            dst = groups[name][0][:, 4 * b0 : 4 * (b0 + width)]
             if engine == "pool":
-                nc.gpsimd.tensor_scalar(dst.rearrange("p (n t) -> p n t", t=4), src.rearrange("p t n -> p n t"), 1.0, 0.0, MULT, ADD)
+                nc.gpsimd.tensor_scalar(values.rearrange("p (n t) -> p n t", t=4), src.rearrange("p t n -> p n t"), 1.0, 0.0, MULT, ADD)
             else:
                 copy, run = (nc.scalar.copy, 2) if engine == "scalar" else (nc.vector.tensor_copy, 4)
-                copy(dst.rearrange("p (c i t) -> p c t i", t=4, i=run), src.rearrange("p t (c i) -> p c t i", i=run))
+                copy(values.rearrange("p (c i t) -> p c t i", t=4, i=run), src.rearrange("p t (c i) -> p c t i", i=run))
 
-        def quantize_w(name, j0=0, j1=None):
-            values, codes, scales = groups[name]
-            c0, c1 = j0 * P, codes.shape[1] if j1 is None else j1 * P
-            quantize(codes[:, c0:c1], scales[:, c0:c1], values[:, 4 * c0 : 4 * c1])
+        def quantize_w(k, c0):
+            values, codes, scales = groups[k, c0]
+            quantize(codes[:], scales[:], values)
 
-        def quantize_h(i, a):
-            quantize(h_q[i][a][:], h_s[i][a][:], h_bf[i][a][:])
+        def quantize_h(i, a, tag=None):
+            h_q[i, a] = tile("h_q%d%d" % (i, a), [P, S], U32, tag=tag)
+            quantize(h_q[i, a][:], h_s[i][a][:], h_bf[i, a][:])
 
         acc = {}
         done = {}
@@ -282,14 +276,17 @@ def tile_list_upgrade_offer_scores_kernel(
                 if c not in acc:
                     acc[c] = bank("out_ps%d" % c, (4 + c) % 8)
                 done[c] = done.get(c, 0) + 1
-                name, b0 = place[k, c]
+                c0, b0 = place[k, c]
                 cols = slice(b0, b0 + P)
-                nc.tensor.matmul_mx(acc[c][:], groups[name][1][:, cols].bitcast(FP8X4), groups[name][2][:, cols],
-                                    h_q[k % 2][k // 2][:].bitcast(FP8X4), h_s[k % 2][k // 2][:],
+                nc.tensor.matmul_mx(acc[c][:], groups[k, c0][1][:, cols].bitcast(FP8X4), groups[k, c0][2][:, cols],
+                                    h_q[k % 2, k // 2][:].bitcast(FP8X4), h_s[k % 2][k // 2][:],
                                     start=(done[c] == 1), stop=(done[c] == 4))
 
         def finish(c, engine):
-            res = tile("res%d" % c, [P, S], F32, tag=("g0", "g1", "g2", "h_bf00", "wr_bf0", "wr_q0")[c])
+            if c == 0:
+                res = placed("res0", [P, S], F32, at_narrow + 8 * PASS)
+            else:
+                res = tile("res%d" % c, [P, S], F32, tag=("g0", "g1", "wg_raw0", "bias_raw", "v2_words", "v3_words")[c])
             bo_c = bias[:, c % 3, 32 + c // 3 : 33 + c // 3]
             if engine == "vector":
                 nc.vector.tensor_scalar(res[:], acc[c][:], bo_c, None, ADD)
@@ -297,80 +294,72 @@ def tile_list_upgrade_offer_scores_kernel(
                 nc.scalar.activation(res[:], acc[c][:], IDENTITY, bias=bo_c)
             nc.sync.dma_start(out[c * P : (c + 1) * P, :], res[:])
 
-        new_group("w1a", [(1, c) for c in range(4)], "wr_raw0")
-        new_group("w0a", [(0, c) for c in range(4)], "v_sc")
-        new_group("w2a", [(2, c) for c in range(4)])
-        new_group("w3a", [(3, 0), (3, 1)])
-        new_group("w3b", [(3, 2), (3, 3)], "v2_words")
-        make_room(0)
+        for t in range(4):
+            make_room(0, t, wr_q0[:, t * P : (t + 1) * P], wr_s0[:, t * P : (t + 1) * P])
         make_arrival(0)
-        guest = make_guest(0, (0, 1))
         make_arrival(1)
-        guest = guest + make_guest(0, (2, 3))
-        for t in range(3):
-            nc.gpsimd.tensor_scalar(
-                wr_bf[1][:].rearrange("p (t q e j) -> p t q e j", t=4, e=4, j=4)[:, t],
-                wr_raw[1][:].rearrange("p j (q t e) -> p t q e j", t=4, e=4)[:, t],
-                1.0, 0.0, MULT, ADD,
-            )
-        for i in range(2):
-            for n in range(2):
-                product(i, 0, n, guest[n])
-        for n in range(2, 4):
-            for i in range(2):
-                product(i, 0, n, guest[n])
-        nc.scalar.copy(
-            wr_bf[1][:].rearrange("p (t q e j) -> p t q j e", t=4, e=4, j=4)[:, 3],
-            wr_raw[1][:].rearrange("p j (q t e) -> p t q j e", t=4, e=4)[:, 3],
-        )
+        guest = make_guest(0)
+        wr_bf1 = [placed("wr_bf1%d" % u, [P, 2 * PASS], BF16, at_wg1 - 4 * PASS * (2 - u)) for u in range(2)]
+        for u in range(2):
+            cast_wr(wr_bf1[u][:], wr_raw[1][:], 2 * u, 2 * u + 2)
+        h_bf[0, 0] = tile("h_bf00", [P, 4 * S], BF16)
+        for n in range(4):
+            product(0, 0, n, guest[n])
+        for u in range(2):
+            codes = tile("wr_q1%d" % u, [P, 2 * P], U32)
+            scales = tile("wr_s1%d" % u, [P, 2 * P], U8)
+            quantize(codes[:], scales[:], wr_bf1[u][:])
+            for t in range(2):
+                make_room(1, 2 * u + t, codes[:, t * P : (t + 1) * P], scales[:, t * P : (t + 1) * P])
         quantize_h(0, 0)
-        quantize_h(1, 0)
-        wr_q.append(tile("wr_q1", [P, PASS], U32, tag="h_bf00"))
-        quantize(wr_q[1][:], wr_s[1][:], wr_bf[1][:])
-        cast_w("scalar", 0, 0, 4)
-        make_room(1)
-        guest = make_guest(1, range(4))
-        new_group("w0b", [(0, 4), (0, 5)], "wr_bf1")
-        for c in range(4, 6):
-            cast_w("pool", 0, c, c + 1)
-        cast_w("scalar", 1, 0, 4)
+        deal_wg(1)
+        h_bf[1, 0] = placed("h_bf10", [P, 4 * S], BF16, at_wg1 - 6 * PASS)
+        for n in range(4):
+            product(1, 0, n, guest[n])
+        guest = make_guest(1)
+        cast_w("scalar", 0, 0, 2, tile("w0a_bf", [P, 8 * P], BF16, tag="g2")[:])
+        cast_w("pool", 0, 2, 6, placed("w0b_bf", [P, 16 * P], BF16, at_planes)[:])
+        cast_w("scalar", 1, 0, 4, placed("w1a_bf", [P, 16 * P], BF16, at_w1a)[:])
+        h_bf[1, 1] = placed("h_bf11", [P, 4 * S], BF16, at_h11)
         for n in range(4):
             product(1, 1, n, guest[n])
-        quantize_w("w0a")
-        score(0, range(4))
-        new_group("w1b", [(1, 4), (1, 5)], "v_sc")
-        for c in range(4, 6):
-            cast_w("pool", 1, c, c + 1)
-        cast_w("scalar", 2, 0, 4)
-        cast_w("scalar", 3, 0, 2)
-        cast_w("scalar", 3, 2, 3)
+        quantize_w(0, 0)
+        score(0, (0, 1))
+        quantize_w(0, 2)
+        score(0, (2, 3))
+        quantize_h(1, 0, "arrival1")
+        quantize_w(1, 0)
+        score(1, range(4))
+        quantize_h(1, 1)
+        cast_w("pool", 1, 4, 6, placed("w1b_bf", [P, 8 * P], BF16, at_h11 - 2 * PASS)[:])
+        cast_w("scalar", 3, 0, 2, tile("w3a_bf", [P, 8 * P], BF16, tag="wr_q11")[:])
+        cast_w("scalar", 3, 2, 4, tile("w3b_bf", [P, 8 * P], BF16, tag="wr_q10")[:])
+        cast_w("scalar", 2, 0, 2, tile("w2a_bf", [P, 8 * P], BF16, tag="g2")[:])
+        cast_w("scalar", 2, 2, 4, tile("w2b_bf", [P, 8 * P], BF16, tag="wr_s11")[:])
+        cast_w("scalar", 3, 4, 6, tile("w3c_bf", [P, 8 * P], BF16, tag="h_bf00")[:])
+        h_bf[0, 1] = placed("h_bf01", [P, 4 * S], BF16, at_w1a - 4 * PASS)
         for n in range(4):
             product(0, 1, n, guest[n])
-        quantize_w("w1a")
-        score(1, range(4))
-        quantize_h(0, 1)
-        quantize_w("w0b")
-        quantize_w("w2a")
-        score(2, range(4))
-        quantize_h(1, 1)
-        cast_w("vector", 3, 3, 4)
-        quantize_w("w1b")
-        quantize_w("w3a")
-        for c in (0, 1):
-            score(3, (c,))
-            finish(c, "scalar")
         score(0, (4, 5))
-        score(1, (4, 5))
-        new_group("last", [(2, 4), (2, 5), (3, 4), (3, 5)])
-        cast_w("vector", 2, 4, 6)
-        quantize_w("w3b")
-        for c in (2, 3):
-            score(3, (c,))
+        quantize_w(3, 0)
+        score(3, (0, 1))
+        quantize_w(3, 2)
+        score(3, (2, 3))
+        quantize_h(0, 1, "wr_q11")
+        quantize_w(2, 0)
+        for c in (0, 1):
+            score(2, (c,))
             finish(c, "scalar")
-        cast_w("vector", 3, 4, 6)
-        quantize_w("last", 0, 2)
-        score(2, (4, 5))
-        quantize_w("last", 2, 4)
+        quantize_w(1, 4)
+        score(1, (4, 5))
+        quantize_w(2, 2)
+        for c in (2, 3):
+            score(2, (c,))
+            finish(c, "scalar")
+        cast_w("vector", 2, 4, 6, tile("w2c_bf", [P, 8 * P], BF16, tag="g2")[:])
+        quantize_w(3, 4)
+        score(3, (4, 5))
+        quantize_w(2, 4)
         for c in (4, 5):
-            score(3, (c,))
+            score(2, (c,))
             finish(c, ("vector", "scalar")[c % 2])

@@ -50,8 +50,7 @@ def tile_list_upgrade_offer_scores_kernel(
         def load(dst, src):
             nc.sync.dma_start(dst.bitcast(I32), src.bitcast(I32))
 
-        at_wa = 0
-        at_tab = (4 * H, 4 * H + 4 * T)
+        at_tab = (4 * PASS, 4 * PASS + 4 * T)
         at_wg1 = at_tab[1] + 4 * T
         at_wr1 = at_wg1 + 4 * PASS
         at_narrow = at_wr1 + 16 * PASS
@@ -77,7 +76,7 @@ def tile_list_upgrade_offer_scores_kernel(
         wr_raw = [placed("wr_raw0", [P, 4, PASS], F32, at_narrow + 4 * PASS)]
         v2_words = tile("v2_words", [P, T2], U32)
         v3_words = tile("v3_words", [P, T3], U16)
-        wg_raw = [tile("wg_raw0", [P, 2, PASS // 2], U32)]
+        wa_raw = tile("wa_raw", [P, H], U32)
         wg_rows = wg_words.bitcast(I32).rearrange("a p (h c) -> h p a c", h=2)
         wa_rows = wa_words[0].rearrange("p c i -> p (c i)")
         wr_rows = wr.rearrange("(p j) r -> p j r", j=4)
@@ -102,12 +101,12 @@ def tile_list_upgrade_offer_scores_kernel(
         nc.sync.dma_start(idx[:], offs)
         load(v_sc[0:P:4, :], tab_scales.rearrange("a q t -> q a t"))
         load(v2_words[:], tab2_words[0].rearrange("p t i -> p (t i)"))
+        load(wa_raw[:], wa_rows)
         load(v3_words[:], tab3_words[0])
-        nc.sync.dma_start(wg_raw[0][:].bitcast(I32), wg_rows[0])
 
         nc.scalar.copy(
-            bias_rows[0:4, :].rearrange("a (t q e) -> a t q e", t=4, e=4),
-            bias_raw[:].rearrange("a (q t e) -> a t q e", t=4, e=4),
+            bias_rows[0:4, :].rearrange("a (t m) -> a t m", t=4),
+            bias_raw[:].rearrange("a (m t) -> a t m", t=4),
         )
         nc.scalar.copy(bias_rows[32:34, 0 : 3 * P], bo_raw[32:34, :])
         bias_ps = bank("bias_ps", 2)
@@ -118,8 +117,8 @@ def tile_list_upgrade_offer_scores_kernel(
 
         def cast_wr(dst, src, t0, t1):
             nc.scalar.copy(
-                dst.rearrange("p (t q e j) -> p t q j e", q=32, e=4, j=4),
-                src.rearrange("p j (q t e) -> p t q j e", t=4, e=4)[:, t0:t1],
+                dst.rearrange("p (t m j) -> p m j t", m=P, j=4),
+                src.rearrange("p j (m t) -> p m j t", t=4)[:, :, :, t0:t1],
             )
 
         wr_bf0 = placed("wr_bf0", [P, 4 * PASS], BF16, at_wr0 + 2 * PASS)
@@ -131,8 +130,8 @@ def tile_list_upgrade_offer_scores_kernel(
         nc.vector.tensor_copy(planes[:, 3 * H :].bitcast(I32), got[:].bitcast(I32))
         for r in range(1, 4):
             load(planes[r:P:32, :], planes[8 * r : P : 32, :])
-        wa_raw = placed("wa_raw", [P, H], U32, at_wa)
-        load(wa_raw[:], wa_rows)
+        wg_raw = [placed("wg_raw0", [P, 2, PASS // 2], U32, at_tab[0] - 4 * PASS)]
+        nc.sync.dma_start(wg_raw[0][:].bitcast(I32), wg_rows[0])
         v_words = [placed("v_words0", [P, T], U32, at_tab[0])]
         load(v_words[0][:], tab_words[0].rearrange("p t i -> p (t i)"))
         got_v = tile("got_v", [P, S], U8)
@@ -158,9 +157,8 @@ def tile_list_upgrade_offer_scores_kernel(
                 at = at + 4 * c1
             else:
                 piece = placed("narrow%d" % k, [P, 4, c1 - c0], F32, at_narrow + 8 * PASS * (k - 2))
-            rows = (w1, w2)[k % 2][k // 2 * PASS : (k // 2 + 1) * PASS, c0:c1].rearrange("(q t e) n -> t q e n", t=4, e=4)
-            for t in range(4):
-                nc.sync.dma_start(piece[:, t, :], rows[t])
+            rows = (w1, w2)[k % 2][k // 2 * PASS : (k // 2 + 1) * PASS, c0:c1].rearrange("(p t) n -> p t n", t=4)
+            nc.sync.dma_start(piece[:, :, :], rows)
             for c in range(c0 // P, c1 // P):
                 raw[k, c] = (piece, c * P - c0)
 
@@ -173,23 +171,28 @@ def tile_list_upgrade_offer_scores_kernel(
         g3 = placed("g3", [P, S], U16, at_wr0 + 4 * PASS)
         nc.vector.tensor_copy(g3[:], v3_words[:].indirect(idx3[:]))
         w_sc = tile("w_sc", [P, 3 * H], U8)
-        nc.vector.tensor_copy(
-            w_sc[:].bitcast(I32).rearrange("p (h t u w) -> p h u t w", t=4, u=8, w=4),
-            planes[:, 0 : 3 * H].bitcast(I32).rearrange("p (h u w t) -> p h u t w", t=4, u=8, w=4),
-        )
+
+        def deal_scales(c0, c1):
+            nc.vector.tensor_copy(
+                w_sc[:, c0:c1].rearrange("p (h t u i) -> p h u t i", t=4, u=8, i=16),
+                planes[:, c0:c1].rearrange("p (h u i t) -> p h u t i", t=4, u=8, i=16),
+            )
+
+        deal_scales(2 * H, 3 * H)
+        deal_scales(0, 2 * H)
         wg_sc = [w_sc[:, a * H : (a + 1) * H] for a in range(2)]
         wa_sc = w_sc[:, 2 * H : 3 * H]
-        wa_p = placed("wa_p", [P, H], U32, at_wr0 + 6 * PASS)
+        wa_p = tile("wa_p", [P, H], U32)
         wg_p = [placed("wg_p0", [P, PASS], U32, at_wr0), placed("wg_p1", [P, PASS], U32, at_room0 + 12 * PASS)]
-        nc.vector.tensor_copy(
-            wa_p[:].bitcast(I32).rearrange("p (a t q w) -> p a t q w", a=2, t=4, w=4),
-            wa_raw[:].bitcast(I32).rearrange("p (a q t w) -> p a t q w", a=2, t=4, w=4),
+        nc.scalar.copy(
+            wa_p[:].rearrange("p (a t u i) -> p a u t i", a=2, t=4, i=4),
+            wa_raw[:].rearrange("p (a u i t) -> p a u t i", a=2, t=4, i=4),
         )
 
         def deal_wg(a):
             nc.vector.tensor_copy(
-                wg_p[a][:].bitcast(I32).rearrange("p (k t q w) -> p k t q w", t=4, q=32, w=2),
-                wg_raw[a][:].bitcast(I32).rearrange("p k (q t w) -> p k t q w", t=4, w=2),
+                wg_p[a][:].bitcast(U16).rearrange("p (k t u i) -> p k u t i", k=2, t=4, i=8),
+                wg_raw[a][:].bitcast(U16).rearrange("p k (u i t) -> p k u t i", t=4, i=8),
             )
 
         deal_wg(0)
@@ -286,7 +289,7 @@ def tile_list_upgrade_offer_scores_kernel(
             if c == 0:
                 res = placed("res0", [P, S], F32, at_narrow + 8 * PASS)
             else:
-                res = tile("res%d" % c, [P, S], F32, tag=("g0", "g1", "wg_raw0", "bias_raw", "v2_words", "v3_words")[c])
+                res = tile("res%d" % c, [P, S], F32, tag=("g0", "g1", "wa_raw", "bias_raw", "v2_words", "v3_words")[c])
             bo_c = bias[:, c % 3, 32 + c // 3 : 33 + c // 3]
             if engine == "vector":
                 nc.vector.tensor_scalar(res[:], acc[c][:], bo_c, None, ADD)

@@ -50,7 +50,7 @@ def tile_list_upgrade_offer_scores_kernel(
         def load(dst, src):
             nc.sync.dma_start(dst.bitcast(I32), src.bitcast(I32))
 
-        at_tab = (4 * PASS, 4 * PASS + 4 * T)
+        at_tab = (2 * T3, 2 * T3 + 4 * T)
         at_wg1 = at_tab[1] + 4 * T
         at_wr1 = at_wg1 + 4 * PASS
         at_narrow = at_wr1 + 16 * PASS
@@ -69,13 +69,12 @@ def tile_list_upgrade_offer_scores_kernel(
         v3_sc = tile("v3_sc", [P, T3], U8)
         planes = placed("planes", [P, 3 * H + 2 * S], U8, at_planes)
         g_planes = tile("g_planes", [P, 2 * S], U8)
-        bias_raw = tile("bias_raw", [4, PASS], F32)
-        bo_raw = placed("bo_raw", [34, 3 * P], F32, at_wr0 + 2 * PASS)
+        bias_raw = placed("bias_raw", [4, PASS], F32, at_wr0 + 2 * PASS)
         bias_rows = tile("bias_rows", [P, PASS], F32)
         ident = tile("ident", [P, P], F32)
         wr_raw = [placed("wr_raw0", [P, 4, PASS], F32, at_narrow + 4 * PASS)]
         v2_words = tile("v2_words", [P, T2], U32)
-        v3_words = tile("v3_words", [P, T3], U16)
+        wg_raw = [tile("wg_raw0", [P, 2, PASS // 2], U32)]
         wa_raw = tile("wa_raw", [P, H], U32)
         wg_rows = wg_words.bitcast(I32).rearrange("a p (h c) -> h p a c", h=2)
         wa_rows = wa_words[0].rearrange("p c i -> p (c i)")
@@ -85,40 +84,50 @@ def tile_list_upgrade_offer_scores_kernel(
         nc.vector.memset(planes[:, 0 : 3 * H].bitcast(I32), 0)
         nc.vector.memset(v_sc.bitcast(I32), 0)
         nc.vector.memset(g_planes[:].bitcast(I32), 0)
+        nc.gpsimd.memset(bias_rows[64:P, :], 0.0)
         make_identity(nc, ident[:])
-        nc.scalar.activation(bias_rows[:], ident[:, 0:1].to_broadcast([P, PASS]), COPY, scale=0.0)
+        nc.scalar.activation(bias_rows[0:64, :], ident[0:64, 0:1].to_broadcast([64, PASS]), COPY, scale=0.0)
 
+        nc.sync.dma_start(wg_raw[0][:].bitcast(I32), wg_rows[0])
         nc.sync.dma_start(idx2[:], offs2)
         nc.sync.dma_start(v2_sc[:].bitcast(I32), tab2_scales[0].bitcast(I32).unsqueeze(1).to_broadcast([16, 8, T2 // 4]))
         nc.sync.dma_start(idx3[:], offs3)
         load(v3_sc[0:P:8, :], tab3_scales[0])
         nc.sync.dma_start(bias_raw[0:2, :], br.rearrange("(a r) -> a r", a=2))
         nc.sync.dma_start(bias_raw[2:4, :], ba.rearrange("(a r) -> a r", a=2))
-        nc.sync.dma_start(bo_raw[32:34, :], bo.rearrange("(h n) -> h n", h=2))
         nc.sync.dma_start(wr_raw[0][:], wr_rows[:, :, 0:PASS])
+        nc.sync.dma_start(bias_rows[64:66, 0 : 3 * P], bo.rearrange("(h n) -> h n", h=2))
         load(planes[0:P:8, 2 * H : 3 * H], wa_scales[0])
         load(planes[0:P:8, 0 : 2 * H].rearrange("q (a c) -> q a c", a=2), wg_scales.rearrange("a q c -> q a c"))
         nc.sync.dma_start(idx[:], offs)
         load(v_sc[0:P:4, :], tab_scales.rearrange("a q t -> q a t"))
         load(v2_words[:], tab2_words[0].rearrange("p t i -> p (t i)"))
         load(wa_raw[:], wa_rows)
-        load(v3_words[:], tab3_words[0])
 
         nc.scalar.copy(
-            bias_rows[0:4, :].rearrange("a (t m) -> a t m", t=4),
-            bias_raw[:].rearrange("a (m t) -> a t m", t=4),
+            bias_rows[0:4, :].rearrange("a (t q e) -> a t q e", t=4, e=4),
+            bias_raw[:].rearrange("a (q t e) -> a t q e", t=4, e=4),
         )
-        nc.scalar.copy(bias_rows[32:34, 0 : 3 * P], bo_raw[32:34, :])
         bias_ps = bank("bias_ps", 2)
         for t in range(4):
             nc.tensor.transpose(bias_ps[:, t * P : (t + 1) * P], bias_rows[:, t * P : (t + 1) * P], ident[:])
-        bias = tile("bias", [P, 4, 34], F32)
-        nc.scalar.activation(bias[:], bias_ps[:].rearrange("p (t c) -> p t c", t=4)[:, :, 0:34], IDENTITY)
+        bias = tile("bias", [P, 4, 66], F32)
+        nc.scalar.activation(bias[:], bias_ps[:].rearrange("p (t c) -> p t c", t=4)[:, :, 0:66], IDENTITY)
+
+        wg_p = [tile("wg_p0", [P, PASS], U32), tile("wg_p1", [P, PASS], U32)]
+
+        def deal_wg(copy, dtype, a):
+            copy(
+                wg_p[a][:].bitcast(dtype).rearrange("p (k t q w) -> p k t q w", t=4, q=32, w=2),
+                wg_raw[a][:].bitcast(dtype).rearrange("p k (q t w) -> p k t q w", t=4, w=2),
+            )
+
+        deal_wg(nc.scalar.copy, U32, 0)
 
         def cast_wr(dst, src, t0, t1):
             nc.scalar.copy(
-                dst.rearrange("p (t m j) -> p m j t", m=P, j=4),
-                src.rearrange("p j (m t) -> p m j t", t=4)[:, :, :, t0:t1],
+                dst.rearrange("p (t q e j) -> p t q j e", q=32, e=4, j=4),
+                src.rearrange("p j (q t e) -> p t q j e", t=4, e=4)[:, t0:t1],
             )
 
         wr_bf0 = placed("wr_bf0", [P, 4 * PASS], BF16, at_wr0 + 2 * PASS)
@@ -130,16 +139,16 @@ def tile_list_upgrade_offer_scores_kernel(
         nc.vector.tensor_copy(planes[:, 3 * H :].bitcast(I32), got[:].bitcast(I32))
         for r in range(1, 4):
             load(planes[r:P:32, :], planes[8 * r : P : 32, :])
-        wg_raw = [placed("wg_raw0", [P, 2, PASS // 2], U32, at_tab[0] - 4 * PASS)]
-        nc.sync.dma_start(wg_raw[0][:].bitcast(I32), wg_rows[0])
+        v3_words = placed("v3_words", [P, T3], U16, 0)
+        load(v3_words[:], tab3_words[0])
         v_words = [placed("v_words0", [P, T], U32, at_tab[0])]
         load(v_words[0][:], tab_words[0].rearrange("p t i -> p (t i)"))
         got_v = tile("got_v", [P, S], U8)
         nc.vector.tensor_copy(got_v[:], v_sc.indirect(idx[:]))
-        v_words.append(placed("v_words1", [P, T], U32, at_tab[1]))
-        load(v_words[1][:], tab_words[1].rearrange("p t i -> p (t i)"))
         for q in (0, 2, 1, 3):
             load(g_planes[32 * q : 32 * q + 4, :], got_v[32 * q : 32 * q + 32 : 4, :])
+        v_words.append(placed("v_words1", [P, T], U32, at_tab[1]))
+        load(v_words[1][:], tab_words[1].rearrange("p t i -> p (t i)"))
         g_sc = [g_planes[:, a * S : (a + 1) * S] for a in range(2)]
         g2_sc = planes[:, 3 * H : 3 * H + S]
         g3_sc = planes[:, 3 * H + S :]
@@ -157,8 +166,9 @@ def tile_list_upgrade_offer_scores_kernel(
                 at = at + 4 * c1
             else:
                 piece = placed("narrow%d" % k, [P, 4, c1 - c0], F32, at_narrow + 8 * PASS * (k - 2))
-            rows = (w1, w2)[k % 2][k // 2 * PASS : (k // 2 + 1) * PASS, c0:c1].rearrange("(p t) n -> p t n", t=4)
-            nc.sync.dma_start(piece[:, :, :], rows)
+            rows = (w1, w2)[k % 2][k // 2 * PASS : (k // 2 + 1) * PASS, c0:c1].rearrange("(q t e) n -> t q e n", t=4, e=4)
+            for t in range(4):
+                nc.sync.dma_start(piece[:, t, :], rows[t])
             for c in range(c0 // P, c1 // P):
                 raw[k, c] = (piece, c * P - c0)
 
@@ -168,37 +178,33 @@ def tile_list_upgrade_offer_scores_kernel(
         wr_s0 = tile("wr_s0", [P, PASS], U8)
         nc.vector.tensor_copy(g2[:], v2_words[:].indirect(idx2[:]))
         quantize(wr_q0[:], wr_s0[:], wr_bf0[:])
+
+        def deal_scales(dst, src):
+            nc.vector.tensor_copy(
+                dst.bitcast(I32).rearrange("p h (t u w) -> p h u t w", t=4, w=4),
+                src.bitcast(I32).rearrange("p h (u w t) -> p h u t w", t=4, w=4),
+            )
+
+        def deal_wa(dst, a, t0, t1):
+            nc.vector.tensor_copy(
+                dst.bitcast(I32).rearrange("p (t q e) -> p t q e", q=32, e=4),
+                wa_raw[:, a * PASS : (a + 1) * PASS].bitcast(I32).rearrange("p (q t e) -> p t q e", t=4, e=4)[:, t0:t1],
+            )
+
+        wa_sc = placed("wa_sc", [P, 2, PASS], U8, at_wr0 + 2 * PASS)
+        deal_scales(wa_sc[:], planes[:, 2 * H : 3 * H].rearrange("p (a c) -> p a c", a=2))
+        wa_p0 = placed("wa_p0", [P, PASS], U32, at_wr0 + 6 * PASS)
+        deal_wa(wa_p0[:], 0, 0, 4)
         g3 = placed("g3", [P, S], U16, at_wr0 + 4 * PASS)
         nc.vector.tensor_copy(g3[:], v3_words[:].indirect(idx3[:]))
-        w_sc = tile("w_sc", [P, 3 * H], U8)
-
-        def deal_scales(c0, c1):
-            nc.vector.tensor_copy(
-                w_sc[:, c0:c1].rearrange("p (h t u i) -> p h u t i", t=4, u=8, i=16),
-                planes[:, c0:c1].rearrange("p (h u i t) -> p h u t i", t=4, u=8, i=16),
-            )
-
-        deal_scales(2 * H, 3 * H)
-        deal_scales(0, 2 * H)
-        wg_sc = [w_sc[:, a * H : (a + 1) * H] for a in range(2)]
-        wa_sc = w_sc[:, 2 * H : 3 * H]
-        wa_p = tile("wa_p", [P, H], U32)
-        wg_p = [placed("wg_p0", [P, PASS], U32, at_wr0), placed("wg_p1", [P, PASS], U32, at_room0 + 12 * PASS)]
-        nc.scalar.copy(
-            wa_p[:].rearrange("p (a t u i) -> p a u t i", a=2, t=4, i=4),
-            wa_raw[:].rearrange("p (a u i t) -> p a u t i", a=2, t=4, i=4),
-        )
-
-        def deal_wg(a):
-            nc.vector.tensor_copy(
-                wg_p[a][:].bitcast(U16).rearrange("p (k t u i) -> p k u t i", k=2, t=4, i=8),
-                wg_raw[a][:].bitcast(U16).rearrange("p k (u i t) -> p k u t i", t=4, i=8),
-            )
-
-        deal_wg(0)
+        wg_sc = placed("wg_sc", [P, 4, PASS], U8, 0)
+        deal_scales(wg_sc[:], planes[:, 0 : 2 * H].rearrange("p (h c) -> p h c", h=4))
         nc.vector.tensor_copy(g[0][:], v_words[0][:].indirect(idx[:]))
+        wa_p1 = [placed("wa_p1%d" % u, [P, 2 * P], U32, at_tab[u]) for u in range(2)]
+        deal_wa(wa_p1[0][:], 1, 0, 2)
         for j0, j1 in ((0, CHUNK), (CHUNK, 2 * CHUNK), (2 * CHUNK, S)):
             nc.vector.tensor_copy(g[1][:, j0:j1], v_words[1][:].indirect(idx[:, j0 // 16 : j1 // 16]))
+        deal_wa(wa_p1[1][:], 1, 2, 4)
 
         room = [placed("room0", [P, 4, S], F32, at_room0), tile("room1", [P, 4, S], F32)]
         arrival = [tile("arrival%d" % a, [P, 4, S], F32) for a in range(2)]
@@ -208,39 +214,31 @@ def tile_list_upgrade_offer_scores_kernel(
             nc.tensor.matmul_mx(acc[:], codes.bitcast(FP8X4), scales, g2[:].bitcast(FP8X4), g2_sc, start=True, stop=True)
             nc.scalar.activation(room[a][:, t, :], acc[:], IDENTITY, bias=bias[:, t, a : a + 1])
 
-        def make_arrival(a):
-            for t in range(4):
-                acc = bank("arrival_ps%d%d" % (a, t), 4 + t)
-                c0 = a * PASS + t * P
-                nc.tensor.matmul_mx(acc[:], wa_p[:, c0 : c0 + P].bitcast(FP8X4), wa_sc[:, c0 : c0 + P],
-                                    g3[:].bitcast(FP4X4), g3_sc, start=True, stop=True)
-                nc.scalar.activation(arrival[a][:, t, :], acc[:], IDENTITY, bias=bias[:, t, 2 + a : 3 + a])
+        def make_arrival(a, t, codes):
+            acc = bank("arrival_ps%d%d" % (a, t), 4 + t)
+            nc.tensor.matmul_mx(acc[:], codes.bitcast(FP8X4), wa_sc[:, a, t * P : (t + 1) * P],
+                                g3[:].bitcast(FP4X4), g3_sc, start=True, stop=True)
+            nc.scalar.activation(arrival[a][:, t, :], acc[:], IDENTITY, bias=bias[:, t, 2 + a : 3 + a])
 
         def guest_pass(a, k, n, acc):
             tok = slice(n * CHUNK, (n + 1) * CHUNK)
             for t in range(4):
-                c0 = a * PASS + t * P
                 nc.tensor.matmul_mx(
                     acc[:, t * CHUNK : (t + 1) * CHUNK],
-                    wg_p[a][:].bitcast(U8)[:, 2 * (k * PASS + t * P) : 2 * (k * PASS + (t + 1) * P)].bitcast(FP4X4), wg_sc[k][:, c0 : c0 + P],
+                    wg_p[a][:].bitcast(U8)[:, 2 * (k * PASS + t * P) : 2 * (k * PASS + (t + 1) * P)].bitcast(FP4X4), wg_sc[:, 2 * k + a, t * P : (t + 1) * P],
                     g[k][:, tok].bitcast(FP8X4), g_sc[k][:, tok], start=(k == 0 and t == 0), stop=(k == 1 and t == 3),
                 )
-
-        def make_guest(a):
-            banks = [bank("guest_ps%d%d" % (a, n), n) for n in range(4)]
-            order = [(k, n) for k in range(2) for n in range(4)] if a == 0 else [(k, n) for n in range(4) for k in range(2)]
-            for k, n in order:
-                guest_pass(a, k, n, banks[n])
-            return banks
 
         h_bf = {}
         h_q = {}
         h_s = [[tile("h_s%d%d" % (i, a), [P, S], U8) for a in range(2)] for i in range(2)]
 
-        def product(i, a, n, guest):
+        def product(i, a, n, guest, values=None):
             other = (room, arrival)[i][a]
+            if values is None:
+                values = h_bf[i, a][:, 4 * n * CHUNK : 4 * (n + 1) * CHUNK]
             nc.vector.tensor_tensor(
-                h_bf[i, a][:, 4 * n * CHUNK : 4 * (n + 1) * CHUNK].rearrange("p (c i t) -> p c t i", t=4, i=2),
+                values.rearrange("p (c i t) -> p c t i", t=4, i=2),
                 guest[:].rearrange("p (t c i) -> p c t i", t=4, i=2),
                 other[:, :, n * CHUNK : (n + 1) * CHUNK].rearrange("p t (c i) -> p c t i", i=2),
                 MULT,
@@ -289,8 +287,8 @@ def tile_list_upgrade_offer_scores_kernel(
             if c == 0:
                 res = placed("res0", [P, S], F32, at_narrow + 8 * PASS)
             else:
-                res = tile("res%d" % c, [P, S], F32, tag=("g0", "g1", "wa_raw", "bias_raw", "v2_words", "v3_words")[c])
-            bo_c = bias[:, c % 3, 32 + c // 3 : 33 + c // 3]
+                res = tile("res%d" % c, [P, S], F32, tag=("g0", "g1", "wa_raw", "bias_rows", "v2_words", "wg_raw0")[c])
+            bo_c = bias[:, c % 3, 64 + c // 3 : 65 + c // 3]
             if engine == "vector":
                 nc.vector.tensor_scalar(res[:], acc[c][:], bo_c, None, ADD)
             else:
@@ -299,27 +297,44 @@ def tile_list_upgrade_offer_scores_kernel(
 
         for t in range(4):
             make_room(0, t, wr_q0[:, t * P : (t + 1) * P], wr_s0[:, t * P : (t + 1) * P])
-        make_arrival(0)
-        make_arrival(1)
-        guest = make_guest(0)
-        wr_bf1 = [placed("wr_bf1%d" % u, [P, 2 * PASS], BF16, at_wg1 - 4 * PASS * (2 - u)) for u in range(2)]
+        for t in range(4):
+            make_arrival(0, t, wa_p0[:, t * P : (t + 1) * P])
+        guest = [bank("guest_ps0%d" % n, n) for n in range(4)]
+        for n in range(4):
+            guest_pass(0, 0, n, guest[n])
         for u in range(2):
-            cast_wr(wr_bf1[u][:], wr_raw[1][:], 2 * u, 2 * u + 2)
+            for t in range(2):
+                make_arrival(1, 2 * u + t, wa_p1[u][:, t * P : (t + 1) * P])
+            for n in range(2) if u == 0 else range(2, 4):
+                guest_pass(0, 1, n, guest[n])
+        wr_bf1 = [placed("wr_bf1%d" % u, [P, 2 * PASS], BF16, at_wg1 - 4 * PASS * (2 - u)) for u in range(2)]
+        nc.gpsimd.tensor_scalar(
+            wr_bf1[0][:].rearrange("p (t q e j) -> p q t e j", q=32, e=4, j=4),
+            wr_raw[1][:].rearrange("p j (q t e) -> p q t e j", t=4, e=4)[:, :, 0:2],
+            1.0, 0.0, MULT, ADD,
+        )
+        cast_wr(wr_bf1[1][:], wr_raw[1][:], 2, 4)
         h_bf[0, 0] = tile("h_bf00", [P, 4 * S], BF16)
         for n in range(4):
             product(0, 0, n, guest[n])
+        h_first = tile("h_bf10a", [P, PASS], BF16)
+        product(1, 0, 0, guest[0], h_first[:])
+        deal_wg(nc.scalar.copy, U32, 1)
         for u in range(2):
             codes = tile("wr_q1%d" % u, [P, 2 * P], U32)
             scales = tile("wr_s1%d" % u, [P, 2 * P], U8)
             quantize(codes[:], scales[:], wr_bf1[u][:])
             for t in range(2):
                 make_room(1, 2 * u + t, codes[:, t * P : (t + 1) * P], scales[:, t * P : (t + 1) * P])
-        quantize_h(0, 0)
-        deal_wg(1)
-        h_bf[1, 0] = placed("h_bf10", [P, 4 * S], BF16, at_wg1 - 6 * PASS)
+        h_q[0, 0] = placed("h_q00", [P, S], U32, at_wg1 - 8 * PASS)
+        quantize(h_q[0, 0][:], h_s[0][0][:], h_bf[0, 0][:])
+        h_rest = placed("h_bf10b", [P, 3 * PASS], BF16, at_wg1 - 2 * PASS)
+        for n in range(1, 4):
+            product(1, 0, n, guest[n], h_rest[:, 4 * (n - 1) * CHUNK : 4 * n * CHUNK])
+        guest = [bank("guest_ps1%d" % n, n) for n in range(4)]
         for n in range(4):
-            product(1, 0, n, guest[n])
-        guest = make_guest(1)
+            for k in range(2):
+                guest_pass(1, k, n, guest[n])
         cast_w("scalar", 0, 0, 2, tile("w0a_bf", [P, 8 * P], BF16, tag="g2")[:])
         cast_w("pool", 0, 2, 6, placed("w0b_bf", [P, 16 * P], BF16, at_planes)[:])
         cast_w("scalar", 1, 0, 4, placed("w1a_bf", [P, 16 * P], BF16, at_w1a)[:])
@@ -330,7 +345,9 @@ def tile_list_upgrade_offer_scores_kernel(
         score(0, (0, 1))
         quantize_w(0, 2)
         score(0, (2, 3))
-        quantize_h(1, 0, "arrival1")
+        h_q[1, 0] = tile("h_q10", [P, S], U32, tag="arrival1")
+        quantize(h_q[1, 0][:, 0:CHUNK], h_s[1][0][:, 0:CHUNK], h_first[:])
+        quantize(h_q[1, 0][:, CHUNK:S], h_s[1][0][:, CHUNK:S], h_rest[:])
         quantize_w(1, 0)
         score(1, range(4))
         quantize_h(1, 1)

@@ -284,10 +284,7 @@ def tile_list_upgrade_offer_scores_kernel(
                                     start=(done[c] == 1), stop=(done[c] == 4))
 
         def finish(c, engine):
-            if c == 0:
-                res = placed("res0", [P, S], F32, at_narrow + 8 * PASS)
-            else:
-                res = tile("res%d" % c, [P, S], F32, tag=("g0", "g1", "wa_raw", "bias_rows", "v2_words", "wg_raw0")[c])
+            res = tile("res%d" % c, [P, S], F32, tag=("g0", "g1", "wa_raw", "bias_rows", "v2_words", "wg_raw0")[c])
             bo_c = bias[:, c % 3, 64 + c // 3 : 65 + c // 3]
             if engine == "vector":
                 nc.vector.tensor_scalar(res[:], acc[c][:], bo_c, None, ADD)
@@ -356,7 +353,6 @@ def tile_list_upgrade_offer_scores_kernel(
         cast_w("scalar", 3, 2, 4, tile("w3b_bf", [P, 8 * P], BF16, tag="wr_q10")[:])
         cast_w("scalar", 2, 0, 2, tile("w2a_bf", [P, 8 * P], BF16, tag="g2")[:])
         cast_w("scalar", 2, 2, 4, tile("w2b_bf", [P, 8 * P], BF16, tag="wr_s11")[:])
-        cast_w("scalar", 3, 4, 6, tile("w3c_bf", [P, 8 * P], BF16, tag="h_bf00")[:])
         h_bf[0, 1] = placed("h_bf01", [P, 4 * S], BF16, at_w1a - 4 * PASS)
         for n in range(4):
             product(0, 1, n, guest[n])
@@ -376,6 +372,7 @@ def tile_list_upgrade_offer_scores_kernel(
         for c in (2, 3):
             score(2, (c,))
             finish(c, "scalar")
+        cast_w("vector", 3, 4, 6, tile("w3c_bf", [P, 8 * P], BF16, tag="wr_q10")[:])
         cast_w("vector", 2, 4, 6, tile("w2c_bf", [P, 8 * P], BF16, tag="g2")[:])
         quantize_w(3, 4)
         score(3, (4, 5))

from contextlib import ExitStack

import concourse.mybir as mybir
from concourse.masks import make_identity

K, M, H, N, T, T2, T3, S = 1024, 512, 1024, 768, 2048, 1024, 2048, 512
FLOPS = 2 * S * (K * H + 2 * M * H + 2 * H * N)

F32 = mybir.dt.float32
BF16 = mybir.dt.bfloat16
I32 = mybir.dt.int32
U32 = mybir.dt.uint32
U16 = mybir.dt.uint16
U8 = mybir.dt.uint8
FP8X4 = mybir.dt.float8_e4m3fn_x4
FP4X4 = mybir.dt.float4_e2m1fn_x4
MULT = mybir.AluOpType.mult
ADD = mybir.AluOpType.add
IDENTITY = mybir.ActivationFunctionType.Identity
COPY = mybir.ActivationFunctionType.Copy

P = 128
PASS = 512
CHUNK = 128


def tile_list_upgrade_offer_scores_kernel(
    tc, tab_words, tab_scales, tab2_words, tab2_scales, tab3_words, tab3_scales, offs, offs2, offs3,
    wg_words, wg_scales, wr, br, wa_words, wa_scales, ba, w1, w2, bo, out,
):
    nc = tc.nc
    with ExitStack() as ctx:
        lists = ctx.enter_context(tc.tile_pool(name="lists", bufs=1))
        sb = ctx.enter_context(tc.tile_pool(name="sb", bufs=1))
        late = ctx.enter_context(tc.tile_pool(name="late", bufs=1))
        ps = ctx.enter_context(tc.psum_pool(name="ps", bufs=1))

        def tile(name, shape, dtype, tag=None):
            return sb.tile(shape, dtype, name=name, tag=tag or name, align_bytes=64)

        def placed(name, shape, dtype, offset):
            return late.tile(shape, dtype, name=name, align_bytes=64, offset=offset)

        def bank(name, b):
            return ps.tile([P, PASS], F32, name=name, tag="bank%d" % b)

        def quantize(codes, scales, values):
            nc.vector.quantize_mx(out=codes.bitcast(FP8X4), scales=scales, in_=values)

        def load(dst, src):
            nc.sync.dma_start(dst.bitcast(I32), src.bitcast(I32))

        at_tab = (2 * T3, 2 * T3 + 4 * T)
        at_wg1 = at_tab[1] + 4 * T
        at_wr1 = at_wg1 + 4 * PASS
        at_narrow = at_wr1 + 16 * PASS
        at_w = at_narrow + 16 * PASS
        at_wr0 = at_w + 32 * N + 32 * PASS
        at_room0 = at_wr0 + 14 * PASS
        at_planes = at_room0 + 16 * S
        at_w1a = at_planes + 8 * PASS
        at_h11 = at_w1a + 8 * PASS

        idx = lists.tile([P, S // 16], U16, name="idx")
        idx2 = lists.tile([P, S // 16], U16, name="idx2")
        idx3 = lists.tile([P, S // 16], U16, name="idx3")
        v_sc = placed("v_sc", [P, T + 128], U8, at_wg1 - 64)[:, 0:T]
        v2_sc = tile("v2_sc", [P, T2], U8)
        v3_sc = tile("v3_sc", [P, T3], U8)
        planes = placed("planes", [P, 3 * H + 2 * S], U8, at_planes)
        g_planes = tile("g_planes", [P, 2 * S], U8)
        bias_raw = placed("bias_raw", [4, PASS], F32, at_wr0 + 2 * PASS)
        bias_rows = tile("bias_rows", [P, PASS], F32)
        ident = tile("ident", [P, P], F32)
        wr_raw = [placed("wr_raw0", [P, 4, PASS], F32, at_narrow + 4 * PASS)]
        v2_words = tile("v2_words", [P, T2], U32)
        wg_raw = [tile("wg_raw0", [P, 2, PASS // 2], U32)]
        wa_raw = tile("wa_raw", [P, H], U32)
        wg_rows = wg_words.bitcast(I32).rearrange("a p (h c) -> h p a c", h=2)
        wa_rows = wa_words[0].rearrange("p c i -> p (c i)")
        wr_rows = wr.rearrange("(p j) r -> p j r", j=4)

        nc.gpsimd.memset(v3_sc[:].bitcast(I32), 0)
        nc.vector.memset(planes[:, 0 : 3 * H].bitcast(I32), 0)
        nc.vector.memset(v_sc.bitcast(I32), 0)
        nc.vector.memset(g_planes[:].bitcast(I32), 0)
        nc.gpsimd.memset(bias_rows[64:P, :], 0.0)
        make_identity(nc, ident[:])
        nc.scalar.activation(bias_rows[0:64, :], ident[0:64, 0:1].to_broadcast([64, PASS]), COPY, scale=0.0)

        nc.sync.dma_start(wg_raw[0][:].bitcast(I32), wg_rows[0])
        nc.sync.dma_start(idx2[:], offs2)
        nc.sync.dma_start(v2_sc[:].bitcast(I32), tab2_scales[0].bitcast(I32).unsqueeze(1).to_broadcast([16, 8, T2 // 4]))
        nc.sync.dma_start(idx3[:], offs3)
        load(v3_sc[0:P:8, :], tab3_scales[0])
        nc.sync.dma_start(bias_raw[0:2, :], br.rearrange("(a r) -> a r", a=2))
        nc.sync.dma_start(bias_raw[2:4, :], ba.rearrange("(a r) -> a r", a=2))
        nc.sync.dma_start(wr_raw[0][:], wr_rows[:, :, 0:PASS])
        nc.sync.dma_start(bias_rows[64:66, 0 : 3 * P], bo.rearrange("(h n) -> h n", h=2))
        load(planes[0:P:8, 2 * H : 3 * H], wa_scales[0])
        load(planes[0:P:8, 0 : 2 * H].rearrange("q (a c) -> q a c", a=2), wg_scales.rearrange("a q c -> q a c"))
        nc.sync.dma_start(idx[:], offs)
        load(v_sc[0:P:4, :], tab_scales.rearrange("a q t -> q a t"))
        load(v2_words[:], tab2_words[0].rearrange("p t i -> p (t i)"))
        load(wa_raw[:], wa_rows)

        nc.scalar.copy(
            bias_rows[0:4, :].rearrange("a (t q e) -> a t q e", t=4, e=4),
            bias_raw[:].rearrange("a (q t e) -> a t q e", t=4, e=4),
        )
        bias_ps = bank("bias_ps", 2)
        for t in range(4):
            nc.tensor.transpose(bias_ps[:, t * P : (t + 1) * P], bias_rows[:, t * P : (t + 1) * P], ident[:])
        bias = tile("bias", [P, 4, 66], F32)
        nc.scalar.activation(bias[:], bias_ps[:].rearrange("p (t c) -> p t c", t=4)[:, :, 0:66], IDENTITY)

        wg_p = [tile("wg_p0", [P, PASS], U32), tile("wg_p1", [P, PASS], U32)]

        def deal_wg(copy, dtype, a):
            copy(
                wg_p[a][:].bitcast(dtype).rearrange("p (k t q w) -> p k t q w", t=4, q=32, w=2),
                wg_raw[a][:].bitcast(dtype).rearrange("p k (q t w) -> p k t q w", t=4, w=2),
            )

        deal_wg(nc.scalar.copy, U32, 0)

        def cast_wr(dst, src, t0, t1):
            nc.scalar.copy(
                dst.rearrange("p (t q e j) -> p t q j e", q=32, e=4, j=4),
                src.rearrange("p j (q t e) -> p t q j e", t=4, e=4)[:, t0:t1],
            )

        wr_bf0 = placed("wr_bf0", [P, 4 * PASS], BF16, at_wr0 + 2 * PASS)
        cast_wr(wr_bf0[:], wr_raw[0][:], 0, 4)

        got = placed("got", [P, 2 * S], U8, at_tab[0] - S)
        nc.vector.tensor_copy(got[:, 0:S], v2_sc[:].indirect(idx2[:]))
        nc.vector.tensor_copy(got[:, S : 2 * S], v3_sc[:].indirect(idx3[:]))
        nc.vector.tensor_copy(planes[:, 3 * H :].bitcast(I32), got[:].bitcast(I32))
        for r in range(1, 4):
            load(planes[r:P:32, :], planes[8 * r : P : 32, :])
        v3_words = placed("v3_words", [P, T3], U16, 0)
        load(v3_words[:], tab3_words[0])
        v_words = [placed("v_words0", [P, T], U32, at_tab[0])]
        load(v_words[0][:], tab_words[0].rearrange("p t i -> p (t i)"))
        got_v = tile("got_v", [P, S], U8)
        nc.vector.tensor_copy(got_v[:], v_sc.indirect(idx[:]))
        for q in (0, 2, 1, 3):
            load(g_planes[32 * q : 32 * q + 4, :], got_v[32 * q : 32 * q + 32 : 4, :])
        v_words.append(placed("v_words1", [P, T], U32, at_tab[1]))
        load(v_words[1][:], tab_words[1].rearrange("p t i -> p (t i)"))
        g_sc = [g_planes[:, a * S : (a + 1) * S] for a in range(2)]
        g2_sc = planes[:, 3 * H : 3 * H + S]
        g3_sc = planes[:, 3 * H + S :]

        wr_raw.append(placed("wr_raw1", [P, 4, PASS], F32, at_wr1))
        nc.sync.dma_start(wr_raw[1][:], wr_rows[:, :, PASS:H])
        wg_raw.append(placed("wg_raw1", [P, 2, PASS // 2], U32, at_wg1))
        nc.sync.dma_start(wg_raw[1][:].bitcast(I32), wg_rows[1])
        w_raw = placed("w_raw", [P, 8 * N + 8 * PASS], F32, at_w)
        raw = {}
        at = 0
        for k, c0, c1 in ((0, 0, N), (1, 0, N), (3, 0, PASS), (2, 0, PASS), (3, PASS, N), (2, PASS, N)):
            if c0 == 0:
                piece = w_raw[:, at : at + 4 * c1].rearrange("p (t n) -> p t n", t=4)
                at = at + 4 * c1
            else:
                piece = placed("narrow%d" % k, [P, 4, c1 - c0], F32, at_narrow + 8 * PASS * (k - 2))
            rows = (w1, w2)[k % 2][k // 2 * PASS : (k // 2 + 1) * PASS, c0:c1].rearrange("(q t e) n -> t q e n", t=4, e=4)
            for t in range(4):
                nc.sync.dma_start(piece[:, t, :], rows[t])
            for c in range(c0 // P, c1 // P):
                raw[k, c] = (piece, c * P - c0)

        g = [tile("g%d" % a, [P, S], U32) for a in range(2)]
        g2 = tile("g2", [P, S], U32)
        wr_q0 = tile("wr_q0", [P, PASS], U32)
        wr_s0 = tile("wr_s0", [P, PASS], U8)
        nc.vector.tensor_copy(g2[:], v2_words[:].indirect(idx2[:]))
        quantize(wr_q0[:], wr_s0[:], wr_bf0[:])

        def deal_scales(dst, src):
            nc.vector.tensor_copy(
                dst.bitcast(I32).rearrange("p h (t u w) -> p h u t w", t=4, w=4),
                src.bitcast(I32).rearrange("p h (u w t) -> p h u t w", t=4, w=4),
            )

        def deal_wa(dst, a, t0, t1):
            nc.vector.tensor_copy(
                dst.bitcast(I32).rearrange("p (t q e) -> p t q e", q=32, e=4),
                wa_raw[:, a * PASS : (a + 1) * PASS].bitcast(I32).rearrange("p (q t e) -> p t q e", t=4, e=4)[:, t0:t1],
            )

        wa_sc = placed("wa_sc", [P, 2, PASS], U8, at_wr0 + 2 * PASS)
        deal_scales(wa_sc[:], planes[:, 2 * H : 3 * H].rearrange("p (a c) -> p a c", a=2))
        wa_p0 = placed("wa_p0", [P, PASS], U32, at_wr0 + 6 * PASS)
        deal_wa(wa_p0[:], 0, 0, 4)
        g3 = placed("g3", [P, S], U16, at_wr0 + 4 * PASS)
        nc.vector.tensor_copy(g3[:], v3_words[:].indirect(idx3[:]))
        wg_sc = placed("wg_sc", [P, 4, PASS], U8, 0)
        deal_scales(wg_sc[:], planes[:, 0 : 2 * H].rearrange("p (h c) -> p h c", h=4))
        nc.vector.tensor_copy(g[0][:], v_words[0][:].indirect(idx[:]))
        wa_p1 = [placed("wa_p1%d" % u, [P, 2 * P], U32, at_tab[u]) for u in range(2)]
        deal_wa(wa_p1[0][:], 1, 0, 2)
        for j0, j1 in ((0, CHUNK), (CHUNK, 2 * CHUNK), (2 * CHUNK, S)):
            nc.vector.tensor_copy(g[1][:, j0:j1], v_words[1][:].indirect(idx[:, j0 // 16 : j1 // 16]))
        deal_wa(wa_p1[1][:], 1, 2, 4)

        room = [placed("room0", [P, 4, S], F32, at_room0), tile("room1", [P, 4, S], F32)]
        arrival = [tile("arrival%d" % a, [P, 4, S], F32) for a in range(2)]

        def make_room(a, t, codes, scales):
            acc = bank("room_ps%d%d" % (a, t), 4 + t)
            nc.tensor.matmul_mx(acc[:], codes.bitcast(FP8X4), scales, g2[:].bitcast(FP8X4), g2_sc, start=True, stop=True)
            nc.scalar.activation(room[a][:, t, :], acc[:], IDENTITY, bias=bias[:, t, a : a + 1])

        def make_arrival(a, t, codes):
            acc = bank("arrival_ps%d%d" % (a, t), 4 + t)
            nc.tensor.matmul_mx(acc[:], codes.bitcast(FP8X4), wa_sc[:, a, t * P : (t + 1) * P],
                                g3[:].bitcast(FP4X4), g3_sc, start=True, stop=True)
            nc.scalar.activation(arrival[a][:, t, :], acc[:], IDENTITY, bias=bias[:, t, 2 + a : 3 + a])

        def guest_pass(a, k, n, acc):
            tok = slice(n * CHUNK, (n + 1) * CHUNK)
            for t in range(4):
                nc.tensor.matmul_mx(
                    acc[:, t * CHUNK : (t + 1) * CHUNK],
                    wg_p[a][:].bitcast(U8)[:, 2 * (k * PASS + t * P) : 2 * (k * PASS + (t + 1) * P)].bitcast(FP4X4), wg_sc[:, 2 * k + a, t * P : (t + 1) * P],
                    g[k][:, tok].bitcast(FP8X4), g_sc[k][:, tok], start=(k == 0 and t == 0), stop=(k == 1 and t == 3),
                )

        h_bf = {}
        h_q = {}
        h_s = [[tile("h_s%d%d" % (i, a), [P, S], U8) for a in range(2)] for i in range(2)]

        def product(i, a, n, guest, values=None):
            other = (room, arrival)[i][a]
            if values is None:
                values = h_bf[i, a][:, 4 * n * CHUNK : 4 * (n + 1) * CHUNK]
            nc.vector.tensor_tensor(
                values.rearrange("p (c i t) -> p c t i", t=4, i=2),
                guest[:].rearrange("p (t c i) -> p c t i", t=4, i=2),
                other[:, :, n * CHUNK : (n + 1) * CHUNK].rearrange("p t (c i) -> p c t i", i=2),
                MULT,
            )

        groups = {}
        place = {}

        def cast_w(engine, k, c0, c1, values):
            width = P * (c1 - c0)
            name = "w%d%d" % (k, c0)
            groups[k, c0] = (values, tile(name + "_q", [P, width], U32), tile(name + "_s", [P, width], U8))
            for c in range(c0, c1):
                place[k, c] = (c0, (c - c0) * P)
            piece, r0 = raw[k, c0]
            src = piece[:, :, r0 : r0 + width]
            if engine == "pool":
                nc.gpsimd.tensor_scalar(values.rearrange("p (n t) -> p n t", t=4), src.rearrange("p t n -> p n t"), 1.0, 0.0, MULT, ADD)
            else:
                copy, run = (nc.scalar.copy, 2) if engine == "scalar" else (nc.vector.tensor_copy, 4)
                copy(values.rearrange("p (c i t) -> p c t i", t=4, i=run), src.rearrange("p t (c i) -> p c t i", i=run))

        def quantize_w(k, c0):
            values, codes, scales = groups[k, c0]
            quantize(codes[:], scales[:], values)

        def quantize_h(i, a, tag=None):
            h_q[i, a] = tile("h_q%d%d" % (i, a), [P, S], U32, tag=tag)
            quantize(h_q[i, a][:], h_s[i][a][:], h_bf[i, a][:])

        acc = {}
        done = {}

        def score(k, tiles):
            for c in tiles:
                if c not in acc:
                    acc[c] = bank("out_ps%d" % c, (4 + c) % 8)
                done[c] = done.get(c, 0) + 1
                c0, b0 = place[k, c]
                cols = slice(b0, b0 + P)
                nc.tensor.matmul_mx(acc[c][:], groups[k, c0][1][:, cols].bitcast(FP8X4), groups[k, c0][2][:, cols],
                                    h_q[k % 2, k // 2][:].bitcast(FP8X4), h_s[k % 2][k // 2][:],
                                    start=(done[c] == 1), stop=(done[c] == 4))

        def finish(c, engine):
            res = tile("res%d" % c, [P, S], F32, tag=("g0", "g1", "wa_raw", "bias_rows", "v2_words", "wg_raw0")[c])
            bo_c = bias[:, c % 3, 64 + c // 3 : 65 + c // 3]
            if engine == "vector":
                nc.vector.tensor_scalar(res[:], acc[c][:], bo_c, None, ADD)
            else:
                nc.scalar.activation(res[:], acc[c][:], IDENTITY, bias=bo_c)
            nc.sync.dma_start(out[c * P : (c + 1) * P, :], res[:])

        for t in range(4):
            make_room(0, t, wr_q0[:, t * P : (t + 1) * P], wr_s0[:, t * P : (t + 1) * P])
        for t in range(4):
            make_arrival(0, t, wa_p0[:, t * P : (t + 1) * P])
        guest = [bank("guest_ps0%d" % n, n) for n in range(4)]
        for n in range(4):
            guest_pass(0, 0, n, guest[n])
        for u in range(2):
            for t in range(2):
                make_arrival(1, 2 * u + t, wa_p1[u][:, t * P : (t + 1) * P])
            for n in range(2) if u == 0 else range(2, 4):
                guest_pass(0, 1, n, guest[n])
        wr_bf1 = [placed("wr_bf1%d" % u, [P, 2 * PASS], BF16, at_wg1 - 4 * PASS * (2 - u)) for u in range(2)]
        nc.gpsimd.tensor_scalar(
            wr_bf1[0][:].rearrange("p (t q e j) -> p q t e j", q=32, e=4, j=4),
            wr_raw[1][:].rearrange("p j (q t e) -> p q t e j", t=4, e=4)[:, :, 0:2],
            1.0, 0.0, MULT, ADD,
        )
        cast_wr(wr_bf1[1][:], wr_raw[1][:], 2, 4)
        h_bf[0, 0] = tile("h_bf00", [P, 4 * S], BF16)
        for n in range(4):
            product(0, 0, n, guest[n])
        h_first = tile("h_bf10a", [P, PASS], BF16)
        product(1, 0, 0, guest[0], h_first[:])
        deal_wg(nc.scalar.copy, U32, 1)
        for u in range(2):
            codes = tile("wr_q1%d" % u, [P, 2 * P], U32)
            scales = tile("wr_s1%d" % u, [P, 2 * P], U8)
            quantize(codes[:], scales[:], wr_bf1[u][:])
            for t in range(2):
                make_room(1, 2 * u + t, codes[:, t * P : (t + 1) * P], scales[:, t * P : (t + 1) * P])
        h_q[0, 0] = placed("h_q00", [P, S], U32, at_wg1 - 8 * PASS)
        quantize(h_q[0, 0][:], h_s[0][0][:], h_bf[0, 0][:])
        h_rest = placed("h_bf10b", [P, 3 * PASS], BF16, at_wg1 - 2 * PASS)
        for n in range(1, 4):
            product(1, 0, n, guest[n], h_rest[:, 4 * (n - 1) * CHUNK : 4 * n * CHUNK])
        guest = [bank("guest_ps1%d" % n, n) for n in range(4)]
        for n in range(4):
            for k in range(2):
                guest_pass(1, k, n, guest[n])
        cast_w("scalar", 0, 0, 2, tile("w0a_bf", [P, 8 * P], BF16, tag="g2")[:])
        cast_w("pool", 0, 2, 6, placed("w0b_bf", [P, 16 * P], BF16, at_planes)[:])
        cast_w("scalar", 1, 0, 4, placed("w1a_bf", [P, 16 * P], BF16, at_w1a)[:])
        h_bf[1, 1] = placed("h_bf11", [P, 4 * S], BF16, at_h11)
        for n in range(4):
            product(1, 1, n, guest[n])
        quantize_w(0, 0)
        score(0, (0, 1))
        quantize_w(0, 2)
        score(0, (2, 3))
        h_q[1, 0] = tile("h_q10", [P, S], U32, tag="arrival1")
        quantize(h_q[1, 0][:, 0:CHUNK], h_s[1][0][:, 0:CHUNK], h_first[:])
        quantize(h_q[1, 0][:, CHUNK:S], h_s[1][0][:, CHUNK:S], h_rest[:])
        quantize_w(1, 0)
        score(1, range(4))
        quantize_h(1, 1)
        cast_w("pool", 1, 4, 6, placed("w1b_bf", [P, 8 * P], BF16, at_h11 - 2 * PASS)[:])
        cast_w("scalar", 3, 0, 2, tile("w3a_bf", [P, 8 * P], BF16, tag="wr_q11")[:])
        cast_w("scalar", 3, 2, 4, tile("w3b_bf", [P, 8 * P], BF16, tag="wr_q10")[:])
        cast_w("scalar", 2, 0, 2, tile("w2a_bf", [P, 8 * P], BF16, tag="g2")[:])
        cast_w("scalar", 2, 2, 4, tile("w2b_bf", [P, 8 * P], BF16, tag="wr_s11")[:])
        h_bf[0, 1] = placed("h_bf01", [P, 4 * S], BF16, at_w1a - 4 * PASS)
        for n in range(4):
            product(0, 1, n, guest[n])
        score(0, (4, 5))
        quantize_w(3, 0)
        score(3, (0, 1))
        quantize_w(3, 2)
        score(3, (2, 3))
        quantize_h(0, 1, "wr_q11")
        quantize_w(2, 0)
        for c in (0, 1):
            score(2, (c,))
            finish(c, "scalar")
        quantize_w(1, 4)
        score(1, (4, 5))
        quantize_w(2, 2)
        for c in (2, 3):
            score(2, (c,))
            finish(c, "scalar")
        cast_w("vector", 3, 4, 6, tile("w3c_bf", [P, 8 * P], BF16, tag="wr_q10")[:])
        cast_w("vector", 2, 4, 6, tile("w2c_bf", [P, 8 * P], BF16, tag="g2")[:])
        quantize_w(3, 4)
        score(3, (4, 5))
        quantize_w(2, 4)
        for c in (4, 5):
            score(2, (c,))
            finish(c, ("vector", "scalar")[c % 2])
